import numpy as np, ml_dtypes
CORES = [13,21,141,149]
N = 4
BF = ml_dtypes.bfloat16
def gentries(a):
    return np.ascontiguousarray(a.reshape(8, 16, -1).transpose(0, 2, 1)).reshape(8, -1)
def gtable(e):
    e = np.asarray(e); return np.ascontiguousarray(e.reshape(8, -1, 16).transpose(0, 2, 1)).reshape(128, -1).astype(np.int32)
S, K, W, C, RO = 256, 16, 2048, 8, 5
def H(e, v):
    return ((e * v >> 5) + e + 37 * v) & (W - 1)
def U(x, w):
    return np.add.reduce(x * w, axis=-1, dtype=np.int32) & (W - 1)
def applies(d, x, least):
    return np.add.reduce(d > x, axis=-1, dtype=np.int32) >= least
def parts(rng):
    lev = rng.choice(np.array([96, 160, 256]), (N, 8, 1, W))
    d = (rng.random((N, 8, 16, W)) * lev).astype(np.int64)
    return d, rng.integers(0, W, (N, 8, S, K)), rng.integers(0, 256, (N, 8, 16, S)), rng.integers(1, 256, (N, 8, 16))
def pack(d, e, z, w):
    return {"dv": d.reshape(N, 128, W).astype(np.float32).astype(BF), "ef": np.stack([gtable(a.reshape(8, -1)) for a in e]),
            "zv": z.reshape(N, 128, S).astype(np.float32).astype(BF), "wt": w.reshape(N, 128, 1).astype(np.int32)}
def stage(rng, d, w, r, g):
    o = rng.permutation(16); w[r, g] = 1; w[r, g, o[:8]] = 255
    m = np.zeros(16, np.int64); m[o[:4]] = 255; m[o[8:12]] = 255
    q = np.zeros(16, np.int64); q[rng.permutation(o[:15])[:9]] = 255
    row = int(o[15]); one = np.zeros(16, np.int64); one[row] = 255
    d[r, g, :, 0] = m; d[r, g, :, W - 1] = q; d[r, g, :, H(W - 1, 255 * 1024 & (W - 1))] = 255
    d[r, g, :, H(0, 255)] = m + one; d[r, g, :, H(W - 1, 255)] = q + one
    return row
def setup_inputs(rng):
    return pack(*parts(rng))
def setup_inputs_corners(rng):
    d, e, z, w = parts(rng); i = np.arange(S); kk = np.arange(K)
    for r in range(N):
        for g in range(8):
            if (r + g) % 2 == 1:
                stage(rng, d, w, r, g)
                few = np.argsort(np.argsort(rng.random((16, 64)), axis=0), axis=0) < np.where(np.arange(64) % 4 == 1, 0, 7)
                d[r, g, :, 16:80] = few * rng.integers(1, 256, (16, 64))
                goal = rng.choice(np.array([0, 1, 2, K - 2, K - 1]), S)[:, None]
                cold = rng.integers(16, 80, (S, K))
                v = np.where((kk < goal) | (goal == 0), cold, np.where(kk == goal, W - 1, e[r, g])); v[:, 0] = 0
                m = i % 4 != 3
                e[r, g] = np.where(m[:, None], v, e[r, g]); z[r, g] = np.where(m, 0, z[r, g])
            else:
                e[r, g, ::4] = e[r, g, ::4, :1]; e[r, g, 1::4] = (W - 1) * rng.integers(0, 2, e[r, g, 1::4].shape)
                z[r, g, :, 5::8] = 255; z[r, g, :, 6::8] = 0
    return pack(d, e, z, w)
def setup_inputs_ends(rng):
    p = rng.choice(np.array([0.0, 0.25, 0.5, 0.75, 0.9, 1.0]), (N, 8, 1, W)); d = 255 * (rng.random((N, 8, 16, W)) < p).astype(np.int64)
    d[..., 2::4] = rng.integers(0, 256, d[..., 2::4].shape)
    p = rng.choice(np.array([0.0, 0.1, 0.3, 0.5, 1.0]), (N, 8, 1, S)); z = 255 * (rng.random((N, 8, 16, S)) < p).astype(np.int64)
    z[..., 2::5] = rng.integers(0, 256, z[..., 2::5].shape)
    e = (W - 1) * rng.integers(0, 2, (N, 8, S, K)); w = np.where(rng.random((N, 8, 16)) < 0.5, 1, 255)
    for r in range(N):
        for g in range(8):
            if r < 2:
                row = stage(rng, d, w, r, g); z[r, g] = 0; z[r, g, row] = 255 * rng.integers(0, 2, S); z[r, g, row, 0] = 255; z[r, g, row, S - 1] = 0
                e[r, g, :, 0] = 0; e[r, g, :, 1:3] = 2 + 4 * rng.integers(0, W // 4, (S, 2)); e[r, g, :, K - 1] = W - 1
            elif (r == N - 1 and g == 7) or (r == N - 2 and g == 6):
                w[r, g] = 255; z[r, g, :, 1] = 255; z[r, g, :, S - 1] = 255; z[r, g, :, 3] = 0
            else:
                w[r, g, 13:15] = 1; w[r, g, 15] = 255
                for j in (1, S - 1):
                    z[r, g, :, j] = 0; z[r, g, 13:, j] = 255; e[r, g, j, 0] = W - 1; e[r, g, j, K - 1] = W - 1
    z[0, 7, :, S - 1] = 255
    return pack(d, e, z, w)
def setup_inputs_full(rng):
    d, e, z, w = parts(rng); i = np.arange(S); kk = np.arange(K); quiet = int(rng.integers(0, N)); turn = int(rng.integers(0, 8))
    for r in range(N):
        for g in range(8):
            kind = (5, 1, 5, 3)[g % 4] if r == quiet else (g + 3 * r + turn) % 8
            if kind == 1:
                o = np.argsort(np.argsort(rng.random((16, S)), axis=0), axis=0)
                z[r, g] = np.where(o < rng.integers(9, 17, S), 255, z[r, g])
            elif kind == 2:
                stage(rng, d, w, r, g)
                few = np.argsort(np.argsort(rng.random((16, 64)), axis=0), axis=0) < np.where(np.arange(64) % 4 == 1, 0, 7)
                d[r, g, :, 16:80] = few * rng.integers(1, 256, (16, 64))
                goal = rng.integers(4, K, S)[:, None]
                v = np.where(kk < goal, rng.integers(16, 80, (S, K)), np.where(kk == goal, W - 1, e[r, g])); v[:, 0] = 0
                m = i % 8 != 5
                e[r, g] = np.where(m[:, None], v, e[r, g]); z[r, g] = np.where(m, 0, z[r, g])
            elif kind == 3 or kind == 6:
                d[r, g] = rng.integers(160, 256, (16, W)); z[r, g] = rng.integers(100, 160, (16, S))
                if kind == 6: d[r, g] = np.where(rng.random(W) < 0.04, rng.integers(0, 100, (16, W)), d[r, g])
            elif kind == 4:
                w[r, g] = 255; half = (rng.permutation(16) < 8)[:, None]
                low = half ^ (rng.random(S) < 0.5)
                z[r, g] = np.where(low, rng.integers(0, 5, (16, S)), rng.integers(251, 256, (16, S)))
                t = rng.random(W); top = np.where(t < 0.3, half, np.where(t < 0.6, ~half, t < 0.85))
                v = np.where(top, rng.integers(251, 256, (16, W)), rng.integers(0, 5, (16, W)))
                d[r, g] = np.where((t >= 0.6) & (t < 0.85), 255, v)
            elif kind == 5:
                e[r, g] = e[r, g, :, :1]
            elif kind == 7:
                w[r, g] = 255; z[r, g] = rng.integers(244, 255, (16, S))
                o = np.argsort(np.argsort(rng.random((16, W)), axis=0), axis=0)
                d[r, g] = np.where((o < rng.integers(8, 17, W)) & (rng.random(W) < 0.6), 255, d[r, g])
    return pack(d, e, z, w)
def setup_inputs_spread(rng):
    d = (np.exp2(8 * rng.random((N, 8, 1, W))) * rng.random((N, 8, 16, W))).astype(np.int64)
    z = (np.exp2(8 * rng.random((N, 8, 1, S))) * rng.random((N, 8, 16, S))).astype(np.int64)
    e = np.minimum((np.exp2((W.bit_length() - 1) * rng.random((N, 8, S, K))) * rng.random((N, 8, S, K))).astype(np.int64), W - 1)
    e = np.where(rng.random((N, 8, S, 1)) < 0.5, W - 1 - e, e)
    w = np.minimum(1 + (np.exp2(8 * rng.random((N, 8, 16))) * rng.random((N, 8, 16))).astype(np.int64), 255)
    return pack(np.minimum(d, 255), e, np.minimum(z, 255), w)
def setup_inputs_ties(rng):
    d, e, z, w = parts(rng)
    d = rng.choice(np.array([0, 0, 100, 252]), (N, 8, 1, W)) + rng.integers(0, 4, d.shape)
    z = rng.choice(np.array([0, 100, 100, 252]), (N, 8, 1, S)) + rng.integers(0, 4, z.shape)
    e[:, :, ::4] = e[:, :, ::4, :1]; e[:, :, 1::4] = rng.choice(np.array([0, 1, W - 2, W - 1]), e[:, :, 1::4].shape)
    e[:, :, 2::4, K // 2:] = e[:, :, 2::4, :K // 2]
    return pack(d, e, z, w)
def check_inputs(d):
    bad = []
    for k, lo, hi in (("dv", 0, 255), ("ef", 0, W - 1), ("zv", 0, 255), ("wt", 1, 255)):
        x = np.asarray(d[k]).astype(np.float32)
        if not np.all((x >= lo) & (x <= hi) & (x == np.floor(x))): bad.append("range of " + k)
    return bad
def reference(dv, ef, zv, wt):
    g2 = np.arange(8)[:, None]; g3 = g2[:, :, None]; kk = np.arange(K - 1)
    D = [np.ascontiguousarray(a.astype(np.float32).astype(np.int32).reshape(8, 16, W).transpose(0, 2, 1)) for a in dv]
    E = [gentries(a).astype(np.int32).reshape(8, S, K) for a in ef]
    z = [np.ascontiguousarray(a.astype(np.float32).astype(np.int32).reshape(8, 16, S).transpose(0, 2, 1)) for a in zv]
    w = wt.astype(np.int32).reshape(N, 8, 1, 1, 16)
    A = [0] * N
    for t in range(RO):
        name = []
        for r in range(N):
            least = 8 + (A[r] & 1); e = E[r]; x = z[r][:, :, None, :]
            n = H(e, U(x, w[r]))
            d = D[r][g3, n]
            a = applies(d, x, least)
            zk = np.where(a[..., None], np.abs(x - d), x); z0 = zk[:, :, :1]
            b = applies(D[r][g3, H(e[:, :, :1], U(zk, w[r]))], zk, least)
            c = applies(D[r][g3, H(e, U(z0, w[r]))], z0, least)
            ok = (b != a[:, :, :1]) & (c == a); ok[:, :, 0] = False
            s = np.argmax(ok, axis=2)
            name.append(np.take_along_axis(n, s[:, :, None], 2)[:, :, 0])
            z[r] = np.take_along_axis(zk, s[:, :, None, None], 2)[:, :, 0]
            E[r] = np.concatenate([np.take_along_axis(e, kk + (kk >= s[:, :, None]), 2), np.zeros((8, S, 1), np.int32)], axis=2)
            A[r] = int(np.count_nonzero(s))
        for r in range(N):
            q = (r - 1 - t % (N - 1)) % N
            E[r][:, :, K - 1] = name[q]
            col = C * np.arange(S) + (name[q] & (C - 1))
            D[r][g2, col] = (D[r][g2, col] + z[q]) >> 1
    return {"yd": np.stack([a.transpose(0, 2, 1).reshape(128, W) for a in D]).astype(np.float32).astype(BF),
            "ye": np.stack([gtable(a.reshape(8, -1)) for a in E]).astype(np.float32),
            "yz": np.stack([a.transpose(0, 2, 1).reshape(128, S) for a in z]).astype(np.float32).astype(BF)}

@@ -1,0 +1,551 @@
+import numpy as np
+from concourse.mybir import AluOpType as A
+from concourse.mybir import ActivationFunctionType as AF
+
+RO = 5
+NS = 8
+NENG = 8
+PAY = 288
+BIG = 2.0 ** 25
+FLOOR = -1055.5 / 2048
+
+
+def _s(n, dt):
+    return ("sbuf", [128, n], dt)
+
+
+SCRATCH = {
+    "Ea": _s(256, "float32"), "Eb": _s(256, "float32"),
+    "Za": _s(544, "bfloat16"), "Zb": _s(544, "bfloat16"),
+}
+for _n, _w in (("D", 2048), ("Z4", 1024),
+               ("ZK", 4096),
+               ("DF", 4096), ("SG", 4096),
+               ("CC", 3840), ("BB", 3840),
+               ("DG", 256 * NS),
+               ("Tt", 240), ("Th", 240),
+               ("fl", 16), ("O8", 8), ("B8a", 8), ("B8", 8), ("F", 144), ("Fh", 144), ("Fw", 144), ("FB", 144), ("FhB", 144),
+               ("ON", 256), ("ID", 128), ("NI", 128), ("C1", 128), ("CB", 128), ("C32", 128)):
+    SCRATCH[_n] = _s(_w, "bfloat16")
+for _n, _w in (("v", 16), ("w", 16), ("Ub", 240), ("a0c", 16), ("SB", 240), ("Rk", 256), ("Rg", 256), ("pcS", 240), ("mm", 256),
+               ("y", 256), ("x", 256), ("Sc", 256), ("NB", 16), ("S3", 16), ("keep", 240), ("kd", 240), ("As", 1), ("jk", 16),
+               ("PT", 3),
+               ("e15", 16), ("e16", 16), ("X", 512), ("XT", 512), ("YL", 256), ("wf", 1), ("IF", 128), ("JF", 128), ("pmf", 1),
+               ("jb", 16), ("cb", 16), ("KC", 256), ("TH", 256), ("RS", 256)):
+    SCRATCH[_n] = _s(_w, "float32")
+for _n, _w in (("N", 256), ("P", 256), ("Nc", 240), ("Pc", 240), ("Nb", 240), ("Pb", 240), ("Ui", 240), ("vi", 16), ("wi", 16),
+               ("o0i", 16), ("Oj", 16), ("Ni", 16), ("LH", 32), ("Ai", 1), ("Aj", 1), ("ci", 16), ("su", 256), ("sh", 256),
+               ("EL", 256), ("wti", 1), ("ip", 32), ("pm", 32), ("p16", 16), ("p31", 16), ("i1", 32), ("i2", 16), ("i3", 32),
+               ("i4", 16), ("i5", 16), ("i6", 16), ("i8", 16), ("i9", 256), ("i10", 256), ("t1", 32), ("t2", 32)):
+    SCRATCH[_n] = _s(_w, "int32")
+for _n, _w in (("off", 256), ("offc", 240), ("offb", 240), ("o0u", 16), ("ou", 16), ("cu", 16), ("cl", 16), ("l1", 32),
+               ("l2", 16), ("l3", 32), ("l4", 16), ("pn", 16), ("p2", 16)):
+    SCRATCH[_n] = _s(_w, "uint16")
+PSUM = ["pu", "pa", "pU", "pc", "pb", "d0", "d1", "d2"]
+for _n in PSUM:
+    SCRATCH[_n] = ("psum", [128, 512], "float32")
+for _t in range(RO):
+    SCRATCH["L%d" % _t] = _s(PAY, "bfloat16")
+    SCRATCH["R%d" % _t] = _s(PAY, "bfloat16")
+DMAS = ["wt", "zv", "ef", "da", "db", "yda", "ydb", "ye", "yz"]
+SEMAPHORES = (["qv", "qs", "qp", "qg"] + ["dma_" + k for k in DMAS] +
+              ["arr%d" % t for t in range(RO)] + ["rl%d" % t for t in range(RO)] + ["loc%d" % t for t in range(RO)])
+
+
+def target(cores, rank, t):
+    return cores[(rank + 1 + t % 3) % len(cores)]
+
+
+def route(topo, src, dst):
+    if topo.may_write(src, dst):
+        return src
+    cand = [c for c in topo.cores_of(src) if c != src and topo.may_write(c, dst)]
+    same = [c for c in cand if topo.die(c) == topo.die(src)]
+    return (same or cand)[0]
+
+
+def engines(topo, src, dst):
+    e = topo.engines(src, dst)[:NENG]
+    return sum(1 << k for k in e), len(e)
+
+
+def relay_program(g, core, T, topo):
+    used = []
+    for t in range(RO):
+        for r in range(len(T.cores)):
+            src, dst = T.cores[r], target(T.cores, r, t)
+            if src != core and route(topo, src, dst) == core:
+                m, n = engines(topo, core, dst)
+                _, nin = engines(topo, src, core)
+                rid, pid = topo.addr(dst, core)
+                g.wait_ge(T.sem["rl%d" % t], nin)
+                g.remote_dma(T["L%d" % t][:, :], T["R%d" % t][:, :], T.sem["arr%d" % t], T.sem["loc%d" % t], pid, rid, m)
+                used.append((t, n))
+    for t, n in used:
+        g.wait_ge(T.sem["loc%d" % t], n)
+
+
+def rank_program(g, core, T, topo):
+    rank = T.rank_of(core)
+    if rank is None:
+        relay_program(g, core, T, topo)
+        return
+    cores = T.cores
+    eng = {"v": g.vector, "s": g.scalar, "p": g.tensor, "g": g, "y": g.sync}
+    known = {k: {} for k in eng}
+    snap, acc, total = {}, {}, {}
+
+    def wait(q, tok):
+        s, n = tok
+        if known[q].get(s, 0) >= n:
+            return
+        eng[q].wait_ge(T.sem[s], n)
+        for a, b in snap.get(tok, {}).items():
+            if known[q].get(a, 0) < b:
+                known[q][a] = b
+        known[q][s] = n
+
+    def before(q, reads, writes):
+        need = {}
+        for regs, wr in ((reads, False), (writes, True)):
+            for b, lo, hi in regs:
+                ps = b in PSUM
+                for l2, h2, w2, tok, q2 in acc.get(b, []):
+                    if ps:
+                        hit = (q2 != q) or (q != "p" and (wr or w2) and lo < h2 and l2 < hi)
+                    else:
+                        hit = (wr or w2) and lo < h2 and l2 < hi
+                    if hit and need.get(tok[0], 0) < tok[1]:
+                        need[tok[0]] = tok[1]
+        for s in sorted(need):
+            wait(q, (s, need[s]))
+
+    def after(q, reads, writes, tok):
+        snap[tok] = dict(known[q])
+        for b, lo, hi in writes:
+            l = acc.get(b, [])
+            acc[b] = [r for r in l if not (lo <= r[0] and r[1] <= hi and b not in PSUM)] + [(lo, hi, True, tok, q)]
+        for b, lo, hi in reads:
+            l = acc.setdefault(b, [])
+            acc[b] = [r for r in l if not (r[4] == q and not r[2] and lo <= r[0] and r[1] <= hi and r[3][0] == tok[0])] + [(lo, hi, False, tok, q)]
+        for b, lo, hi in list(reads) + list(writes):
+            if b in PSUM:
+                last = {}
+                for r in acc[b]:
+                    last[(r[4], r[2], r[0], r[1])] = r
+                acc[b] = list(last.values())
+
+    def op(q, fn, reads, writes):
+        before(q, reads, writes)
+        s = "q" + q
+        total[s] = total.get(s, 0) + 1
+        fn(eng[q]).then_inc(T.sem[s], 1)
+        after(q, reads, writes, (s, total[s]))
+
+    def dma(q, name, out, in_, reads, writes):
+        before(q, reads, writes)
+        s = "dma_" + name
+        eng[q].dma_start(out, in_).then_inc(T.sem[s], 16)
+        total[s] = 16
+        after(q, reads, writes, (s, 16))
+
+    def ap(v):
+        return T[v[0]][:, v[1]:v[2]] if len(v) == 3 else T[v[0]][:, v[1]:v[2]:v[3]]
+
+    def rg(v):
+        return (v[0], v[1], v[2])
+
+    def opnd(v):
+        if isinstance(v[0], tuple):
+            return ap(v[0]).indirect(ap(v[1])), [rg(v[0]), rg(v[1])]
+        return ap(v), [rg(v)]
+
+    def tt(out, a, b, o):
+        oa, orr = opnd(out)
+        aa, ar = opnd(a)
+        ba, br = opnd(b)
+        op("v", lambda e: e.tensor_tensor(oa, aa, ba, o), ar + br + orr[1:], orr[:1])
+
+    def ts(out, a, s1, o1, s2=None, o2=None):
+        oa, orr = opnd(out)
+        aa, ar = opnd(a)
+        rd = list(ar)
+        sc = []
+        for s in (s1, s2):
+            if isinstance(s, tuple):
+                rd.append(rg(s))
+                sc.append(ap(s))
+            else:
+                sc.append(s)
+        if o2 is None:
+            op("v", lambda e: e.tensor_scalar(oa, aa, sc[0], None, o1), rd, orr[:1])
+        else:
+            op("v", lambda e: e.tensor_scalar(oa, aa, sc[0], sc[1], o1, o2), rd, orr[:1])
+
+    def cp(out, a):
+        oa, orr = opnd(out)
+        aa, ar = opnd(a)
+        op("v", lambda e: e.tensor_copy(oa, aa), ar + orr[1:], orr[:1])
+
+    def fill(out, c):
+        op("v", lambda e: e.memset(ap(out), c), [], [rg(out)])
+
+    def act(out, a, f, bias=None, scale=None):
+        aa, ar = opnd(a)
+        kw = {}
+        rd = list(ar)
+        for k, c in (("bias", bias), ("scale", scale)):
+            if isinstance(c, tuple):
+                kw[k] = ap(c)
+                rd.append(rg(c))
+            elif c is not None:
+                kw[k] = c
+        op("s", lambda e: e.activation(ap(out), aa, f, **kw), rd, [rg(out)])
+
+    def fold(out, fm, src, lo, hi, *extra):
+        reads = [(fm, 0, 144), (src, lo, hi)]
+        for x in extra:
+            reads += [rg(x[0]), rg(x[1])]
+
+        def fn(e):
+            for x in extra:
+                e.matmul(ap(out), ap(x[0]), ap(x[1]), x is extra[0], False)
+            for jl in range(16):
+                r = e.matmul(ap(out), T[fm][:, 15 - jl:143 - jl], T[src][:, lo + jl:hi:16], jl == 0 and not extra, jl == 15)
+            return r
+        op("p", fn, reads, [rg(out)])
+
+    def usum(bank, lo, hi, src, slo, shi):
+        fold((bank, lo, hi), "Fw", src, slo, shi, (("C32", 0, 128), ("ON", 0, hi - lo)))
+
+    def hlist(P, N, off, lo, hi):
+        return [lambda: ts((N, lo, hi), (P, lo, hi), 5, A.logical_shift_right, 2047, A.bitwise_and),
+                lambda: cp((off, lo, hi), (N, lo, hi))]
+
+    E = ["Ea", "Eb"]
+    Z = ["Za", "Zb"]
+    DALL = ("D", 0, 2048)
+
+    dma("s", "ef", T.EL[:, :], T.ef[:, :], [], [("EL", 0, 256)])
+    dma("y", "wt", T.wti[:, :], T.wt[:, :], [], [("wti", 0, 1)])
+    dma("y", "zv", T[Z[0]][:, 256:512], T.zv[:, :], [], [(Z[0], 256, 512)])
+    dma("s", "da", T.D[:, 1184:2048], T.dv[:, 0:864], [], [("D", 1184, 2048)])
+    dma("y", "db", T.D[:, 0:1184], T.dv[:, 864:2048], [], [("D", 0, 1184)])
+
+    def iota(name, pattern, base, cm):
+        n = SCRATCH[name][1][1]
+        op("g", lambda e: e.iota(T[name][:, :], pattern, base, cm), [], [(name, 0, n)])
+
+    fill(("O8", 0, 8), 1.0)
+    fill(("F", 0, 144), 0.0)
+    fill(("ON", 0, 256), 1.0)
+    iota("ip", [[0, 32]], 0, 1)
+    iota("i1", [[16, 16], [0, 2]], 0, 0)
+    op("g", lambda e: e.affine_select(T.B8a[:, :], T.O8[:, :], [[-16, 8]], A.is_ge, 0.0, 0, 1), [("O8", 0, 8)], [("B8a", 0, 8)])
+    op("g", lambda e: e.affine_select(T.B8[:, :], T.B8a[:, :], [[16, 8]], A.is_ge, 0.0, 15, -1), [("B8a", 0, 8)], [("B8", 0, 8)])
+    iota("i2", [[-1, 16]], 15, 32)
+    iota("i5", [[1, 16]], 240, 16)
+    iota("i6", [[1, 16]], 0, 16)
+    iota("i8", [[16, 16]], 0, 0)
+    op("g", lambda e: e.affine_select(T.ID[:, :], T.ON[:, 0:128], [[-1, 128]], A.is_equal, 0.0, 0, 1), [("ON", 0, 128)], [("ID", 0, 128)])
+    iota("i9", [[16, 16], [256, 16]], 0, 0)
+    iota("i4", [[32, 16]], 0, 0)
+    iota("i3", [[1, 16], [0, 2]], 2288, -16)
+    iota("i10", [[1, 16], [0, 16]], 1, 0)
+
+    ts(("pm", 0, 32), ("ip", 0, 32), 15, A.bitwise_and)
+    ts(("p16", 0, 16), ("ip", 0, 16), 16, A.bitwise_and)
+    tt(("t1", 0, 32), ("pm", 0, 32), ("i1", 0, 32), A.add)
+    cp(("cl", 0, 16), ("pm", 0, 16))
+    cp(("l1", 0, 32), ("t1", 0, 32))
+    cp(("F", 15, 128, 16), ("B8", 0, 8))
+    ts(("t2", 0, 16), ("i2", 0, 16), 511, A.bitwise_and)
+    fill(("C32", 0, 128), 1.0 / 8192)
+    fill(("PT", 0, 1), 0.0)
+    fill(("PT", 1, 2), 7.5)
+    fill(("PT", 2, 3), -0.5)
+    fill(("C1", 0, 128), -1.0 / 128)
+    fill(("CB", 0, 128), -BIG / 128)
+    fill(("y", 0, 16), BIG)
+    fill(("mm", 0, 16), BIG)
+    fill(("RS", 0, 256), 1.0)
+    fill(("RS", 0, 256, 16), 0.0)
+    ts(("FB", 0, 144), ("F", 0, 144), BIG, A.mult)
+    ts(("FhB", 0, 144), ("F", 0, 144), 0.5 * BIG, A.mult)
+    cp(("wf", 0, 1), ("wti", 0, 1))
+    tt(("t2", 16, 32), ("t2", 0, 16), ("p16", 0, 16), A.add)
+    ts(("Fw", 0, 144), ("F", 0, 144), ("wf", 0, 1), A.mult, 1.0 / 2048, A.mult)
+    cp(("l2", 0, 16), ("t2", 16, 32))
+
+    ts(("X", 0, 512), (("EL", 0, 256), ("l1", 0, 32)), 1184.0, A.add, 2048.0, A.mult)
+    usum("pu", 0, 16, Z[0], 256, 512)
+    ts(("vi", 0, 16), ("pu", 0, 16), FLOOR, A.add)
+    op("v", lambda e: e.transpose(T.XT[:, :], T.X[:, :]), [("X", 0, 512)], [("XT", 0, 512)])
+    tt(("v", 0, 16), ("pu", 0, 16), ("vi", 0, 16), A.subtract)
+    cp((E[0], 0, 256), (("XT", 0, 512), ("l2", 0, 16)))
+    tt(("P", 0, 256), (("v", 0, 16), ("cl", 0, 16)), (E[0], 0, 256), A.mult)
+    h = hlist("P", "N", "off", 0, 256)
+    h[0]()
+    ts(("Fh", 0, 144), ("F", 0, 144), 0.5, A.mult)
+    h[1]()
+
+    tt(("jb", 0, 16), ("pm", 0, 16), ("i8", 0, 16), A.add)
+    ts(("NI", 0, 128), ("ID", 0, 128), -1.0, A.mult)
+    cp(("pmf", 0, 1), ("pm", 0, 1))
+    ts(("t1", 0, 16), ("i5", 0, 16), 255, A.bitwise_and)
+    ts(("t1", 16, 32), ("i6", 0, 16), 255, A.bitwise_and)
+    ts(("KC", 0, 256), ("i9", 0, 256), ("pmf", 0, 1), A.add, 2048.0, A.mult)
+    cp(("pn", 0, 16), ("t1", 0, 16))
+    cp(("p2", 0, 16), ("t1", 16, 32))
+    ts(("KC", 0, 256), ("KC", 0, 256), 0.5, A.add)
+    cp(("IF", 0, 128), ("ID", 0, 128))
+    cp(("JF", 0, 128), ("NI", 0, 128))
+
+    def codes():
+        tt(("Rk", 0, 256), (("N", 0, 256), ("pn", 0, 16)), ("KC", 0, 256), A.add)
+
+    def consts2():
+        ts(("TH", 0, 256), ("i10", 0, 256), 524288.0, A.mult)
+        ts(("ci", 0, 16), ("jb", 0, 16), 148.0, A.add)
+        ts(("p31", 0, 16), ("ip", 0, 16), 31, A.bitwise_and)
+        ts(("t1", 0, 16), ("ci", 0, 16), 255, A.bitwise_and)
+        ts(("t2", 0, 32), ("i3", 0, 32), 255, A.bitwise_and)
+        ts(("cb", 0, 16), ("t1", 0, 16), 8.0, A.mult)
+        tt(("t1", 16, 32), ("p31", 0, 16), ("i4", 0, 16), A.add)
+        cp(("l3", 0, 32), ("t2", 0, 32))
+        cp(("l4", 0, 16), ("t1", 16, 32))
+
+    def z4(src):
+        act(("Z4", 0, 256), src, AF.Copy)
+        act(("Z4", 256, 512), src, AF.Copy)
+        act(("Z4", 512, 1024), ("Z4", 0, 512), AF.Copy)
+
+    def tcol():
+        act(("Tt", 0, 240), ("ON", 0, 240), AF.Copy, None, ("PT", 1, 2))
+        act(("Th", 0, 240), ("ON", 0, 240), AF.Copy, None, ("PT", 2, 3))
+
+    def shift(e, lo, hi):
+        a, b = 16 * lo, 16 * hi
+
+        def fn(x):
+            x.matmul(T.d2[:, a - 16:b - 16], T.IF[:, :], T[e][:, a:b], True, False)
+            x.matmul(T.d2[:, a - 16:b - 16], T.JF[:, :], T[e][:, a - 16:b - 16], False, True)
+            return x.matmul(T.d2[:, 240 + a:240 + b], T.IF[:, :], T[e][:, a - 16:b - 16], True, True)
+        op("p", fn, [("IF", 0, 128), ("JF", 0, 128), (e, a - 16, b)], [("d2", a - 16, b - 16), ("d2", 240 + a, 240 + b)])
+
+    codes()
+    shift(E[0], 1, 16)
+    z4((Z[0], 256, 512))
+    tcol()
+    late = []
+
+    for t in range(RO):
+        ec, en, zc, zn = E[t % 2], E[(t + 1) % 2], Z[t % 2], Z[(t + 1) % 2]
+
+        def g1(lo, hi=None):
+            hi = hi or lo + 1
+            tt(("DF", 256 * lo, 256 * hi), (DALL, ("off", 16 * lo, 16 * hi)), ("Z4", 0, 256 * (hi - lo)), A.subtract)
+
+        def absq(lo, hi):
+            act(("ZK", 256 * lo + 256, 256 * hi + 256), ("DF", 256 * lo, 256 * hi), AF.Abs)
+            usum("pU", 16 * lo, 16 * hi, "ZK", 256 * lo + 256, 256 * hi + 256)
+
+        def sgn(lo, hi):
+            act(("SG", 256 * lo, 256 * hi), ("DF", 256 * lo, 256 * hi), AF.Sign, -0.5)
+
+        def cnta(lo, hi):
+            fold(("pa", 16 * lo, 16 * hi), "FhB", "SG", 256 * lo, 256 * hi, (("CB", 0, 128), ("Th", 0, 16 * (hi - lo))))
+
+        def cv(q):
+            tt(("CC", 256 * q, 256 * q + 256), (DALL, ("offc", 16 * q, 16 * q + 16)), ("ZK", 0, 256), A.is_gt)
+
+        pairs = [(q, min(q + 2, NS)) for q in range(0, NS, 2)]
+
+        def sgath(n):
+            lo, hi = pairs[n]
+            act(("DG", 256 * lo, 256 * hi), (DALL, ("offc", 16 * lo, 16 * hi)), AF.Copy)
+            bank = "d%d" % (n % 2)
+
+            def fn(e):
+                for k in range(hi - lo):
+                    o = ap((bank, 256 * k, 256 * k + 256))
+                    e.matmul(o, T.NI[:, :], T.ZK[:, 0:256], True, False)
+                    r = e.matmul(o, T.ID[:, :], T.DG[:, 256 * (lo + k):256 * (lo + k) + 256], False, True)
+                return r
+            op("p", fn, [("NI", 0, 128), ("ID", 0, 128), ("ZK", 0, 256), ("DG", 256 * lo, 256 * hi)], [(bank, 0, 256 * (hi - lo))])
+
+        def ssign(n):
+            lo, hi = pairs[n]
+            act(("CC", 256 * lo, 256 * hi), ("d%d" % (n % 2), 0, 256 * (hi - lo)), AF.Sign, -0.5)
+
+        def bv(lo, hi):
+            tt(("BB", 256 * lo, 256 * hi), (DALL, ("offb", 16 * lo, 16 * hi)), ("ZK", 256 * lo + 256, 256 * hi + 256), A.is_gt)
+            fold(("pb", 16 * lo, 16 * hi), "F", "BB", 256 * lo, 256 * hi, (("C1", 0, 128), ("Tt", 0, 16 * (hi - lo))))
+
+        g1(15)
+        for f in late:
+            f()
+        sgn(15, 16)
+        act((zc, 0, 256), ("DF", 3840, 4096), AF.Abs)
+        fold(("pu", 32, 48), "Fh", "SG", 3840, 4096)
+        g1(12, 15)
+        absq(12, 15)
+        ts(("a0c", 0, 16), ("pu", 32, 48), ("PT", 0, 1), A.is_lt, 256.0, A.mult)
+        sgn(12, 15)
+        g1(11)
+        tt(("o0i", 0, 16), ("a0c", 0, 16), ("jb", 0, 16), A.add)
+        act(("SB", 0, 240), (("a0c", 0, 16), ("cl", 0, 15)), AF.Identity, -BIG, BIG / 128)
+        g1(10)
+        cp(("o0u", 0, 16), ("o0i", 0, 16))
+        g1(9)
+        cp(("ZK", 0, 256), ((zc, 0, 512), ("o0u", 0, 16)))
+        usum("pu", 64, 80, "ZK", 0, 256)
+        g1(7, 9)
+        absq(8, 12)
+        cnta(12, 15)
+        sgn(8, 12)
+        ts(("wi", 0, 16), ("pu", 64, 80), FLOOR, A.add)
+        g1(6)
+        tt(("w", 0, 16), ("pu", 64, 80), ("wi", 0, 16), A.subtract)
+        g1(4, 6)
+        absq(4, 8)
+        tt(("Pc", 0, 240), (("w", 0, 16), ("cl", 0, 15)), (ec, 0, 240), A.mult)
+        h = hlist("Pc", "Nc", "offc", 0, 240)
+        g1(3)
+        h[0]()
+        g1(2)
+        h[1]()
+        absq(2, 4)
+        g1(0, 2)
+        absq(0, 2)
+        sgath(0)
+        sgath(1)
+        ssign(0)
+        cnta(8, 12)
+        for n in range(2, len(pairs) - 1):
+            sgath(n)
+            ssign(n - 1)
+
+        chain = [lambda: ts(("Ui", 0, 240), ("pU", 0, 240), FLOOR, A.add),
+                 lambda: tt(("Ub", 0, 240), ("pU", 0, 240), ("Ui", 0, 240), A.subtract),
+                 lambda: tt(("Pb", 0, 240), ((ec, 240, 256), ("cl", 0, 15)), ("Ub", 0, 240), A.mult)]
+        vq = list(range(14, NS - 1, -1))
+        for n, q in enumerate(vq):
+            cv(q)
+            if len(vq) - n <= len(chain):
+                chain[len(chain) - (len(vq) - n)]()
+        fold(("pc", 16 * NS, 240), "FB", "CC", 256 * NS, 3840, (("CB", 0, 128), ("Tt", 0, 240 - 16 * NS)))
+        sgath(len(pairs) - 1)
+        ssign(len(pairs) - 2)
+        ssign(len(pairs) - 1)
+        h = hlist("Pb", "Nb", "offb", 0, 240)
+        h[0]()
+        h[1]()
+
+        bv(0, 4)
+        fold(("pc", 0, 16 * NS), "FhB", "CC", 0, 256 * NS, (("CB", 0, 128), ("Th", 0, 16 * NS)))
+        bv(4, 8)
+        sgn(4, 8)
+        cnta(4, 8)
+        sgn(0, 4)
+        cnta(0, 4)
+        act(("pcS", 0, 240), ("pc", 0, 240), AF.Copy)
+        bv(8, 12)
+        bv(12, 15)
+        tt(("mm", 16, 256), ("pa", 0, 240), ("pcS", 0, 240), A.min)
+        tt(("Rg", 0, 256), (("mm", 0, 256), ("p2", 0, 16)), ("Rk", 0, 256), A.min)
+
+        tt(("y", 16, 256), ("pb", 0, 240), ("SB", 0, 240), A.mult)
+        tt(("x", 0, 256), (("y", 0, 256), ("p2", 0, 16)), ("Rg", 0, 256), A.min)
+        op("v", lambda e: e.tensor_tensor_scan(T.Sc[:, :], T.RS[:, :], T.x[:, :], 0.0, A.mult, A.max),
+           [("RS", 0, 256), ("x", 0, 256)], [("Sc", 0, 256)])
+        sv = ("Sc", 15, 256, 16)
+        ts(("Oj", 0, 16), sv, -1024.0, A.add, 1.0 / 2048, A.mult)
+        ts(("Ni", 0, 16), sv, 863.5, A.add)
+        cp(("ou", 0, 16), ("Oj", 0, 16))
+        ts(("LH", 0, 16), ("Ni", 0, 16), 7, A.bitwise_and)
+        ts(("LH", 16, 32), ("Ni", 0, 16), 3, A.logical_shift_right, 255, A.bitwise_and)
+        cp((zn, 256, 512), (("ZK", 0, 4096), ("ou", 0, 16)))
+        cp((zn, 512, 544), ("LH", 0, 32))
+
+        dst = target(cores, rank, t)
+        via = route(topo, core, dst)
+        to = dst if via == core else via
+        m, n = engines(topo, core, to)
+        rid, pid = topo.addr(to, core)
+        land, sem = (("L%d" % t), "arr%d" % t) if to == dst else (("R%d" % t), "rl%d" % t)
+        before("g", [(zn, 256, 544)], [])
+        g.remote_dma(T[land][:, :], T[zn][:, 256:544], T.sem[sem], T.sem["loc%d" % t], pid, rid, m)
+        after("g", [(zn, 256, 544)], [], ("loc%d" % t, n))
+        total["loc%d" % t] = n
+        frm = cores[(rank - 1 - t % 3) % len(cores)]
+        lc = "L%d" % t
+        narr = engines(topo, route(topo, frm, core), core)[1]
+        acc[lc] = [(0, PAY, True, ("arr%d" % t, narr), "net")]
+
+        last = t == RO - 1
+        if last:
+            dma("y", "yz", T.yz[:, :], T[zn][:, 256:512], [(zn, 256, 512)], [])
+        else:
+            usum("pu", 0, 16, zn, 256, 512)
+            z4((zn, 256, 512))
+        if t == 0:
+            consts2()
+        ts(("NB", 0, 16), sv, 524288.0, A.is_lt, 67108864.0, A.mult)
+        if not last:
+            ts(("fl", 0, 16), sv, 524288.0, A.is_ge)
+            op("p", lambda e: e.matmul(T.pu[:, 96:112], T.ON[:, 0:128], T.fl[:, :], True, True),
+               [("ON", 0, 128), ("fl", 0, 16)], [("pu", 96, 112)])
+        tt(("S3", 0, 16), sv, ("NB", 0, 16), A.add)
+        tt(("keep", 0, 240), (("S3", 0, 16), ("cl", 0, 15)), ("TH", 16, 256), A.is_lt)
+        if not last:
+            ts(("vi", 0, 16), ("pu", 0, 16), FLOOR, A.add)
+        tt(("kd", 0, 240), ("keep", 0, 240), ("d2", 0, 240), A.mult)
+        if not last:
+            tt(("v", 0, 16), ("pu", 0, 16), ("vi", 0, 16), A.subtract)
+        tt((en, 16, 256), ("kd", 0, 240), ("d2", 256, 496), A.add)
+        if not last:
+            op("s", lambda e: e.activation(T.jk[:, :], T.pu[:, 96:112], AF.Identity, accum_out=T.As[:, :]), [("pu", 96, 112)],
+               [("jk", 0, 16), ("As", 0, 1)])
+            tt(("P", 16, 256), (("v", 0, 16), ("cl", 0, 15)), (en, 16, 256), A.mult)
+            cp(("Ai", 0, 1), ("As", 0, 1))
+            h = hlist("P", "N", "off", 16, 256)
+            h[0]()
+            ts(("Aj", 0, 1), ("Ai", 0, 1), 1, A.bitwise_and)
+            h[1]()
+            cp(("PT", 0, 1), ("Aj", 0, 1))
+            act(("PT", 1, 2), ("PT", 0, 1), AF.Identity, 7.5)
+            act(("PT", 2, 3), ("PT", 0, 1), AF.Identity, -0.5)
+            tcol()
+            shift(en, 2, 16)
+            codes()
+        else:
+            cp(("X", 0, 512), ((en, 0, 256), ("l3", 0, 32)))
+
+        tt(("ci", 0, 16), (lc, 256, 272), ("cb", 0, 16), A.add)
+        ts(("e15", 0, 16), (lc, 272, 288), 8.0, A.mult, 1184.0, A.add)
+        cp(("cu", 0, 16), ("ci", 0, 16))
+        tt(("e16", 0, 16), ("e15", 0, 16), (lc, 256, 272), A.add)
+        tt(("su", 0, 256), (DALL, ("cu", 0, 16)), (lc, 0, 256), A.add)
+        ts((en, 0, 16), ("e16", 0, 16), 2048.0, A.mult)
+        ts(("sh", 0, 256), ("su", 0, 256), 1, A.logical_shift_right)
+        if not last:
+            tt(("P", 0, 16), ("v", 0, 16), (en, 0, 16), A.mult)
+        cp((DALL, ("cu", 0, 16)), ("sh", 0, 256))
+        if not last:
+            h = hlist("P", "N", "off", 0, 16)
+            h[0]()
+            shift(en, 1, 2)
+            late = [h[1], lambda: tt(("Rk", 1, 256, 16), ("N", 0, 16), ("KC", 1, 256, 16), A.add)]
+            continue
+
+        dma("y", "yda", T.yd[:, 864:2048], T.D[:, 0:1184], [("D", 0, 1184)], [])
+        dma("s", "ydb", T.yd[:, 0:864], T.D[:, 1184:2048], [("D", 1184, 2048)], [])
+        cp(("X", 15, 512, 32), (en, 0, 16))
+        cp(("X", 31, 512, 32), (en, 0, 16))
+        op("v", lambda e: e.transpose(T.XT[:, :], T.X[:, :]), [("X", 0, 512)], [("XT", 0, 512)])
+        ts(("YL", 0, 256), (("XT", 0, 512), ("l4", 0, 16)), 1.0 / 2048, A.mult, -1184.0, A.add)
+        dma("y", "ye", T.ye[:, :], T.YL[:, :], [("YL", 0, 256)], [])
+
+    for s in sorted(total):
+        wait("g", (s, total[s]))

@@ -3,53 +3,55 @@ from concourse.mybir import AluOpType as A
 from concourse.mybir import ActivationFunctionType as AF
 
 RO = 5
-NS = 8
 NENG = 8
-PAY = 288
-BIG = 2.0 ** 25
+PAY = 144
+BIG = 2.0 ** 28
 FLOOR = -1055.5 / 2048
+ROT = 1184
+JR = 256 - ROT // 8
+Z4, ZH, NM = 2048, 2432, 2560
+CYC, PEC, GATHER, SCATTER, MINC = 0.83, 0.42, 1.3, 3.8, 85
+WAKE, SAME, DMA, HOP, XC = 300.0, 200.0, 1200.0, 1500.0, 1900.0
+PASSES = 4
+BOTH = ()
+LATE = (0, 0, 0, 0.5, 0.5)
+GA = [(12, 16), (8, 12), (4, 8), (0, 4)]
+GB = [(8, 12), (12, 15), (0, 4), (4, 8)]
 
 
 def _s(n, dt):
     return ("sbuf", [128, n], dt)
 
 
-SCRATCH = {
-    "Ea": _s(256, "float32"), "Eb": _s(256, "float32"),
-    "Za": _s(544, "bfloat16"), "Zb": _s(544, "bfloat16"),
-}
-for _n, _w in (("D", 2048), ("Z4", 1024),
-               ("ZK", 4096),
-               ("DF", 4096), ("SG", 4096),
-               ("CC", 3840), ("BB", 3840),
-               ("DG", 256 * NS),
-               ("Tt", 240), ("Th", 240),
-               ("fl", 16), ("O8", 8), ("B8a", 8), ("B8", 8), ("F", 144), ("Fh", 144), ("Fw", 144), ("FB", 144), ("FhB", 144),
-               ("ON", 256), ("ID", 128), ("NI", 128), ("C1", 128), ("CB", 128), ("C32", 128)):
+SCRATCH = {}
+for _w in "01":
+    for _n, _c, _d in (("D", 2048, "bfloat16"), ("ZK", 2576, "bfloat16"), ("Fw", 144, "bfloat16"), ("E", 128, "float32"),
+                       ("v", 8, "float32"), ("kd", 128, "float32"), ("N", 128, "int32"), ("EL", 256, "int32"), ("wti", 1, "int32"),
+                       ("off", 128, "uint16"), ("YL", 128, "float32")):
+        SCRATCH[_n + _w] = _s(_c, _d)
+for _n, _w in (("DF", 2048), ("SG", 2048), ("CC", 1920), ("BB", 1920), ("DG", 1920), ("fac", 248), ("hb", 120), ("fb", 120),
+               ("naf", 16), ("nab", 64), ("fl", 8), ("cb", 8), ("K1", 128), ("K2", 128),
+               ("O8", 8), ("B8a", 8), ("B8", 8), ("F", 144), ("Fh", 144), ("Fq", 144),
+               ("ON", 128), ("ID", 128), ("NI", 128), ("N2", 128), ("IB", 128), ("I11", 128), ("I14", 128), ("I16", 128),
+               ("C32", 128), ("C4", 128), ("CK", 128), ("CE", 128), ("SW", 128)):
     SCRATCH[_n] = _s(_w, "bfloat16")
-for _n, _w in (("v", 16), ("w", 16), ("Ub", 240), ("a0c", 16), ("SB", 240), ("Rk", 256), ("Rg", 256), ("pcS", 240), ("mm", 256),
-               ("y", 256), ("x", 256), ("Sc", 256), ("NB", 16), ("S3", 16), ("keep", 240), ("kd", 240), ("As", 1), ("jk", 16),
-               ("PT", 3),
-               ("e15", 16), ("e16", 16), ("X", 512), ("XT", 512), ("YL", 256), ("wf", 1), ("IF", 128), ("JF", 128), ("pmf", 1),
-               ("jb", 16), ("cb", 16), ("KC", 256), ("TH", 256), ("RS", 256)):
+for _n, _w in (("Ub", 128), ("x", 128), ("m", 112), ("keep", 128), ("acc", 3), ("tau", 1),
+               ("X", 256), ("XT", 256), ("wf", 2), ("IF", 128), ("JF", 128), ("QF", 128), ("pmf", 1), ("TH", 128), ("su", 128), ("SF", 128)):
     SCRATCH[_n] = _s(_w, "float32")
-for _n, _w in (("N", 256), ("P", 256), ("Nc", 240), ("Pc", 240), ("Nb", 240), ("Pb", 240), ("Ui", 240), ("vi", 16), ("wi", 16),
-               ("o0i", 16), ("Oj", 16), ("Ni", 16), ("LH", 32), ("Ai", 1), ("Aj", 1), ("ci", 16), ("su", 256), ("sh", 256),
-               ("EL", 256), ("wti", 1), ("ip", 32), ("pm", 32), ("p16", 16), ("p31", 16), ("i1", 32), ("i2", 16), ("i3", 32),
-               ("i4", 16), ("i5", 16), ("i6", 16), ("i8", 16), ("i9", 256), ("i10", 256), ("t1", 32), ("t2", 32)):
+for _n, _w in (("P", 128), ("PB", 256), ("NB", 256), ("Ui", 128), ("vi", 8), ("Ci", 8), ("Oj", 8), ("LH", 16), ("ri", 1), ("ci", 8),
+               ("sh", 256), ("ip", 16), ("pm", 16), ("t", 160),
+               ("i1", 16), ("i2", 8), ("i3", 16), ("i4", 8), ("i5", 8), ("i6", 128), ("i7", 128)):
     SCRATCH[_n] = _s(_w, "int32")
-for _n, _w in (("off", 256), ("offc", 240), ("offb", 240), ("o0u", 16), ("ou", 16), ("cu", 16), ("cl", 16), ("l1", 32),
-               ("l2", 16), ("l3", 32), ("l4", 16), ("pn", 16), ("p2", 16)):
+for _n, _w in (("offb", 256), ("ou", 8), ("cu", 16), ("cl", 8), ("l1", 16), ("l2", 8), ("l3", 16), ("l4", 8)):
     SCRATCH[_n] = _s(_w, "uint16")
-PSUM = ["pu", "pa", "pU", "pc", "pb", "d0", "d1", "d2"]
+PSUM = ["pu", "pU", "pac", "pb", "px", "pE", "d0", "d1"]
 for _n in PSUM:
     SCRATCH[_n] = ("psum", [128, 512], "float32")
-for _t in range(RO):
+STEPS = 2 * RO
+for _t in range(STEPS):
     SCRATCH["L%d" % _t] = _s(PAY, "bfloat16")
-    SCRATCH["R%d" % _t] = _s(PAY, "bfloat16")
-DMAS = ["wt", "zv", "ef", "da", "db", "yda", "ydb", "ye", "yz"]
-SEMAPHORES = (["qv", "qs", "qp", "qg"] + ["dma_" + k for k in DMAS] +
-              ["arr%d" % t for t in range(RO)] + ["rl%d" % t for t in range(RO)] + ["loc%d" % t for t in range(RO)])
+SEMAPHORES = (["qv", "qs", "qp", "qg"] + [k + w for k in ("wt", "zv", "ef", "dv", "yd", "ye", "yz") for w in ("_0", "_1")] +
+              [k + str(t) for k in ("arr", "rl", "loc", "rep", "xc") for t in range(STEPS)])
 
 
 def target(cores, rank, t):
@@ -71,18 +73,79 @@ def engines(topo, src, dst):
 
 def relay_program(g, core, T, topo):
     used = []
-    for t in range(RO):
+    for n in range(STEPS):
         for r in range(len(T.cores)):
-            src, dst = T.cores[r], target(T.cores, r, t)
+            src, dst = T.cores[r], target(T.cores, r, n // 2)
             if src != core and route(topo, src, dst) == core:
-                m, n = engines(topo, core, dst)
+                m, k = engines(topo, core, dst)
                 _, nin = engines(topo, src, core)
                 rid, pid = topo.addr(dst, core)
-                g.wait_ge(T.sem["rl%d" % t], nin)
-                g.remote_dma(T["L%d" % t][:, :], T["R%d" % t][:, :], T.sem["arr%d" % t], T.sem["loc%d" % t], pid, rid, m)
-                used.append((t, n))
-    for t, n in used:
-        g.wait_ge(T.sem["loc%d" % t], n)
+                g.wait_ge(T.sem["rl%d" % n], nin)
+                g.remote_dma(T["L%d" % n][:, :], T["L%d" % n][:, :], T.sem["arr%d" % n], T.sem["loc%d" % n], pid, rid, m)
+                used.append((n, k))
+    for n, k in used:
+        g.wait_ge(T.sem["loc%d" % n], k)
+
+
+def in_order(calls, stage):
+    n = len(calls)
+    pre = [dict() for _ in range(n)]
+    seen = {}
+    for i, (q, reads, writes, busy, done, issue) in enumerate(calls):
+        for regs, wr in ((reads, False), (writes, True)):
+            for b, lo, hi in regs:
+                for l2, h2, w2, j in seen.get(b, []):
+                    data = (wr or w2) and lo < h2 and l2 < hi
+                    if j != i and (data or b in PSUM):
+                        pre[i][j] = pre[i].get(j, False) or calls[j][0] != q or (data and q != "p")
+        for b, lo, hi in writes:
+            seen[b] = [r for r in seen.get(b, []) if not (lo <= r[0] and r[1] <= hi)] + [(lo, hi, True, i)]
+        for b, lo, hi in reads:
+            seen.setdefault(b, []).append((lo, hi, False, i))
+        for b, lo, hi in list(reads) + list(writes):
+            if b in PSUM:
+                seen[b] = seen[b][-12:]
+    busy = [c[3] for c in calls]
+    fwd = [{j: calls[j][4] + (SAME if calls[j][0] == calls[i][0] else WAKE) if w else busy[j] for j, w in pre[i].items()} for i in range(n)]
+    bwd = [dict() for _ in range(n)]
+    for i in range(n):
+        for j, lag in fwd[i].items():
+            bwd[j][i] = lag + busy[i] - busy[j]
+
+    def place(before, after, first, key):
+        left, at, taken = [len(p) for p in before], [0.0] * n, {}
+        ready = [i for i in range(n) if not left[i]]
+        while ready:
+            i = min(ready, key=lambda i: key[i])
+            ready.remove(i)
+            t = max([first[i]] + [at[j] + lag for j, lag in before[i].items()])
+            l = taken.setdefault(calls[i][0], [])
+            k = len(l)
+            while k and l[k - 1][1] > t:
+                k -= 1
+            while k < len(l) and l[k][0] < t + busy[i]:
+                t = max(t, l[k][1])
+                k += 1
+            l.insert(k, (t, t + busy[i]))
+            at[i] = t
+            for j in after[i]:
+                left[j] -= 1
+                if not left[j]:
+                    ready.append(j)
+        return at
+
+    way = [0.0] * n
+    for i in range(n - 1, -1, -1):
+        way[i] = max([calls[i][4]] + [way[k] + fwd[k][i] for k in bwd[i]])
+    at = place(fwd, bwd, [0.0] * n, [(stage[i], -way[i], i) for i in range(n)])
+    best = None
+    for _ in range(PASSES):
+        end = max(at[i] + calls[i][4] for i in range(n))
+        if best is None or end < best[0]:
+            best = (end, at)
+        back = place(bwd, fwd, [c[4] - c[3] for c in calls], [(-at[i] - busy[i], -i) for i in range(n)])
+        at = place(fwd, bwd, [0.0] * n, [(-back[i] - busy[i], i) for i in range(n)])
+    return [calls[i] for i in sorted(range(n), key=lambda i: (best[1][i], i))]
 
 
 def rank_program(g, core, T, topo):
@@ -92,62 +155,23 @@ def rank_program(g, core, T, topo):
         return
     cores = T.cores
     eng = {"v": g.vector, "s": g.scalar, "p": g.tensor, "g": g, "y": g.sync}
-    known = {k: {} for k in eng}
-    snap, acc, total = {}, {}, {}
+    calls = []
 
-    def wait(q, tok):
-        s, n = tok
-        if known[q].get(s, 0) >= n:
-            return
-        eng[q].wait_ge(T.sem[s], n)
-        for a, b in snap.get(tok, {}).items():
-            if known[q].get(a, 0) < b:
-                known[q][a] = b
-        known[q][s] = n
+    def op(q, fn, reads, writes, ns):
+        def issue(total):
+            s = "q" + q
+            total[s] = total.get(s, 0) + 1
+            fn(eng[q]).then_inc(T.sem[s], 1)
+            return (s, total[s])
+        calls.append((q, reads, writes, ns, ns, issue))
 
-    def before(q, reads, writes):
-        need = {}
-        for regs, wr in ((reads, False), (writes, True)):
-            for b, lo, hi in regs:
-                ps = b in PSUM
-                for l2, h2, w2, tok, q2 in acc.get(b, []):
-                    if ps:
-                        hit = (q2 != q) or (q != "p" and (wr or w2) and lo < h2 and l2 < hi)
-                    else:
-                        hit = (wr or w2) and lo < h2 and l2 < hi
-                    if hit and need.get(tok[0], 0) < tok[1]:
-                        need[tok[0]] = tok[1]
-        for s in sorted(need):
-            wait(q, (s, need[s]))
-
-    def after(q, reads, writes, tok):
-        snap[tok] = dict(known[q])
-        for b, lo, hi in writes:
-            l = acc.get(b, [])
-            acc[b] = [r for r in l if not (lo <= r[0] and r[1] <= hi and b not in PSUM)] + [(lo, hi, True, tok, q)]
-        for b, lo, hi in reads:
-            l = acc.setdefault(b, [])
-            acc[b] = [r for r in l if not (r[4] == q and not r[2] and lo <= r[0] and r[1] <= hi and r[3][0] == tok[0])] + [(lo, hi, False, tok, q)]
-        for b, lo, hi in list(reads) + list(writes):
-            if b in PSUM:
-                last = {}
-                for r in acc[b]:
-                    last[(r[4], r[2], r[0], r[1])] = r
-                acc[b] = list(last.values())
-
-    def op(q, fn, reads, writes):
-        before(q, reads, writes)
-        s = "q" + q
-        total[s] = total.get(s, 0) + 1
-        fn(eng[q]).then_inc(T.sem[s], 1)
-        after(q, reads, writes, (s, total[s]))
-
-    def dma(q, name, out, in_, reads, writes):
-        before(q, reads, writes)
-        s = "dma_" + name
-        eng[q].dma_start(out, in_).then_inc(T.sem[s], 16)
-        total[s] = 16
-        after(q, reads, writes, (s, 16))
+    def dmas(q, s, pairs, reads, writes, ns=None):
+        def issue(total):
+            for out, in_ in pairs:
+                eng[q].dma_start(out, in_).then_inc(T.sem[s], 16)
+            total[s] = 16 * len(pairs)
+            return (s, total[s])
+        calls.append((q, reads, writes, 60.0 * len(pairs), ns or DMA, issue))
 
     def ap(v):
         return T[v[0]][:, v[1]:v[2]] if len(v) == 3 else T[v[0]][:, v[1]:v[2]:v[3]]
@@ -160,11 +184,20 @@ def rank_program(g, core, T, topo):
             return ap(v[0]).indirect(ap(v[1])), [rg(v[0]), rg(v[1])]
         return ap(v), [rg(v)]
 
+    def ns(out, a, per):
+        if isinstance(out[0], tuple):
+            return 50 + (a[2] - a[1]) * SCATTER * CYC
+        n = len(range(*out[1:]))
+        return 50 + n * GATHER * CYC if isinstance(a[0], tuple) else max(MINC, n * per) * CYC
+
+    def narrow(*vs):
+        return 0.5 if all(SCRATCH[v[0]][2] in ("bfloat16", "uint16") for v in vs if not isinstance(v[0], tuple)) else 1
+
     def tt(out, a, b, o):
         oa, orr = opnd(out)
         aa, ar = opnd(a)
         ba, br = opnd(b)
-        op("v", lambda e: e.tensor_tensor(oa, aa, ba, o), ar + br + orr[1:], orr[:1])
+        op("v", lambda e: e.tensor_tensor(oa, aa, ba, o), ar + br + orr[1:], orr[:1], ns(out, a, 1 if a[0] in PSUM else 2))
 
     def ts(out, a, s1, o1, s2=None, o2=None):
         oa, orr = opnd(out)
@@ -178,374 +211,332 @@ def rank_program(g, core, T, topo):
             else:
                 sc.append(s)
         if o2 is None:
-            op("v", lambda e: e.tensor_scalar(oa, aa, sc[0], None, o1), rd, orr[:1])
+            op("v", lambda e: e.tensor_scalar(oa, aa, sc[0], None, o1), rd, orr[:1], ns(out, a, narrow(out, a)))
         else:
-            op("v", lambda e: e.tensor_scalar(oa, aa, sc[0], sc[1], o1, o2), rd, orr[:1])
+            op("v", lambda e: e.tensor_scalar(oa, aa, sc[0], sc[1], o1, o2), rd, orr[:1], ns(out, a, narrow(out, a)))
 
     def cp(out, a):
         oa, orr = opnd(out)
         aa, ar = opnd(a)
-        op("v", lambda e: e.tensor_copy(oa, aa), ar + orr[1:], orr[:1])
+        op("v", lambda e: e.tensor_copy(oa, aa), ar + orr[1:], orr[:1], ns(out, a, narrow(out, a)))
 
     def fill(out, c):
-        op("v", lambda e: e.memset(ap(out), c), [], [rg(out)])
+        op("v", lambda e: e.memset(ap(out), c), [], [rg(out)], ns(out, out, narrow(out)))
 
-    def act(out, a, f, bias=None, scale=None):
+    def act(out, a, f, bias=None, scale=None, accum=None):
         aa, ar = opnd(a)
         kw = {}
         rd = list(ar)
+        wr = [rg(out)]
         for k, c in (("bias", bias), ("scale", scale)):
             if isinstance(c, tuple):
                 kw[k] = ap(c)
                 rd.append(rg(c))
             elif c is not None:
                 kw[k] = c
-        op("s", lambda e: e.activation(ap(out), aa, f, **kw), rd, [rg(out)])
+        if accum is not None:
+            kw["accum_out"] = ap(accum)
+            wr.append(rg(accum))
+        op("s", lambda e: e.activation(ap(out), aa, f, **kw), rd, wr, ns(out, a, 1))
+
+    def pns(out, terms):
+        return sum(max(64, out[2] - out[1]) * (4 if SCRATCH[l][2] == "float32" else 1) * PEC for l, r in terms)
+
+    def mm(out, *terms, first=True, last=True):
+        def fn(e):
+            for n, (l, r) in enumerate(terms):
+                x = e.matmul(ap(out), T[l][:, :], ap(r), first and n == 0, last and n == len(terms) - 1)
+            return x
+        op("p", fn, [(l, 0, 128) for l, r in terms] + [rg(r) for l, r in terms], [rg(out)], pns(out, terms))
 
     def fold(out, fm, src, lo, hi, *extra):
-        reads = [(fm, 0, 144), (src, lo, hi)]
-        for x in extra:
-            reads += [rg(x[0]), rg(x[1])]
-
         def fn(e):
-            for x in extra:
-                e.matmul(ap(out), ap(x[0]), ap(x[1]), x is extra[0], False)
+            for n, (l, r) in enumerate(extra):
+                e.matmul(ap(out), T[l][:, :], ap(r), n == 0, False)
             for jl in range(16):
                 r = e.matmul(ap(out), T[fm][:, 15 - jl:143 - jl], T[src][:, lo + jl:hi:16], jl == 0 and not extra, jl == 15)
             return r
-        op("p", fn, reads, [rg(out)])
+        op("p", fn, [(fm, 0, 144), (src, lo, hi)] + [(l, 0, 128) for l, r in extra] + [rg(r) for l, r in extra], [rg(out)],
+           pns(out, [(fm, 0)] * 16 + list(extra)))
 
-    def usum(bank, lo, hi, src, slo, shi):
-        fold((bank, lo, hi), "Fw", src, slo, shi, (("C32", 0, 128), ("ON", 0, hi - lo)))
+    def usum(bank, lo, hi, w, slo, shi):
+        fold((bank, lo, hi), "Fw" + w, "ZK" + w, slo, shi, ("C32", ("ON", 0, hi - lo)))
 
-    def hlist(P, N, off, lo, hi):
-        return [lambda: ts((N, lo, hi), (P, lo, hi), 5, A.logical_shift_right, 2047, A.bitwise_and),
-                lambda: cp((off, lo, hi), (N, lo, hi))]
-
-    E = ["Ea", "Eb"]
-    Z = ["Za", "Zb"]
-    DALL = ("D", 0, 2048)
-
-    dma("s", "ef", T.EL[:, :], T.ef[:, :], [], [("EL", 0, 256)])
-    dma("y", "wt", T.wti[:, :], T.wt[:, :], [], [("wti", 0, 1)])
-    dma("y", "zv", T[Z[0]][:, 256:512], T.zv[:, :], [], [(Z[0], 256, 512)])
-    dma("s", "da", T.D[:, 1184:2048], T.dv[:, 0:864], [], [("D", 1184, 2048)])
-    dma("y", "db", T.D[:, 0:1184], T.dv[:, 864:2048], [], [("D", 0, 1184)])
+    def turn(out, a):
+        op("v", lambda e: e.transpose(ap(out), ap(a)), [rg(a)], [rg(out)], ns(out, a, 1))
 
     def iota(name, pattern, base, cm):
         n = SCRATCH[name][1][1]
-        op("g", lambda e: e.iota(T[name][:, :], pattern, base, cm), [], [(name, 0, n)])
+        op("g", lambda e: e.iota(T[name][:, :], pattern, base, cm), [], [(name, 0, n)], 130 + 2 * n * CYC)
+
+    def select(out, a, *args):
+        n = SCRATCH[out][1][1]
+        op("g", lambda e: e.affine_select(T[out][:, :], T[a][:, :], *args), [(a, 0, n)], [(out, 0, n)], 170 + 2 * n * CYC)
+
+    def placed(sb, c0, hbm, w):
+        r = slice(64 * int(w), 64 * int(w) + 64)
+        b = 128 - JR
+        return [(sb[0:64, c0:c0 + 128], hbm[r, JR:JR + 128]), (sb[64:128, c0:c0 + b], hbm[r, JR + 128:256]),
+                (sb[64:128, c0 + b:c0 + 128], hbm[r, 0:JR])]
+
+    for w in "01":
+        r = slice(64 * int(w), 64 * int(w) + 64)
+        hs = (slice(0, 64), slice(64, 128))
+        dmas("s", "ef_" + w, [(T["EL" + w][h, :], T.ef[r, :]) for h in hs], [], [("EL" + w, 0, 256)])
+        dmas("y", "wt_" + w, [(T["wti" + w][h, :], T.wt[r, :]) for h in hs], [], [("wti" + w, 0, 1)])
+        dmas("y", "zv_" + w, placed(T["ZK" + w], ZH, T.zv, w), [], [("ZK" + w, ZH, NM)])
+        dmas("s" if w == "0" else "y", "dv_" + w,
+             [(T["D" + w][h, ROT:2048], T.dv[r, 0:2048 - ROT]) for h in hs] + [(T["D" + w][h, 0:ROT], T.dv[r, 2048 - ROT:2048]) for h in hs],
+             [], [("D" + w, 0, 2048)])
 
     fill(("O8", 0, 8), 1.0)
     fill(("F", 0, 144), 0.0)
-    fill(("ON", 0, 256), 1.0)
-    iota("ip", [[0, 32]], 0, 1)
-    iota("i1", [[16, 16], [0, 2]], 0, 0)
-    op("g", lambda e: e.affine_select(T.B8a[:, :], T.O8[:, :], [[-16, 8]], A.is_ge, 0.0, 0, 1), [("O8", 0, 8)], [("B8a", 0, 8)])
-    op("g", lambda e: e.affine_select(T.B8[:, :], T.B8a[:, :], [[16, 8]], A.is_ge, 0.0, 15, -1), [("B8a", 0, 8)], [("B8", 0, 8)])
-    iota("i2", [[-1, 16]], 15, 32)
-    iota("i5", [[1, 16]], 240, 16)
-    iota("i6", [[1, 16]], 0, 16)
-    iota("i8", [[16, 16]], 0, 0)
-    op("g", lambda e: e.affine_select(T.ID[:, :], T.ON[:, 0:128], [[-1, 128]], A.is_equal, 0.0, 0, 1), [("ON", 0, 128)], [("ID", 0, 128)])
-    iota("i9", [[16, 16], [256, 16]], 0, 0)
-    iota("i4", [[32, 16]], 0, 0)
-    iota("i3", [[1, 16], [0, 2]], 2288, -16)
-    iota("i10", [[1, 16], [0, 16]], 1, 0)
-
-    ts(("pm", 0, 32), ("ip", 0, 32), 15, A.bitwise_and)
-    ts(("p16", 0, 16), ("ip", 0, 16), 16, A.bitwise_and)
-    tt(("t1", 0, 32), ("pm", 0, 32), ("i1", 0, 32), A.add)
-    cp(("cl", 0, 16), ("pm", 0, 16))
-    cp(("l1", 0, 32), ("t1", 0, 32))
+    fill(("ON", 0, 128), 1.0)
+    iota("ip", [[0, 16]], 0, 1)
+    iota("i1", [[16, 8], [0, 2]], JR, 0)
+    iota("i2", [[-2, 8]], 15, 32)
+    iota("i3", [[1, 8], [0, 2]], 1144, -8)
+    iota("i4", [[32, 8]], 0, 0)
+    iota("i5", [[16, 8]], 0, 0)
+    iota("i6", [[1, 16], [0, 8]], 0, 0)
+    iota("i7", [[0, 16], [16, 8]], 0, 0)
+    select("B8a", "O8", [[-16, 8]], A.is_ge, 0.0, 0, 1)
+    select("B8", "B8a", [[16, 8]], A.is_ge, 0.0, 15, -1)
+    select("ID", "ON", [[-1, 128]], A.is_equal, 0.0, 0, 1)
     cp(("F", 15, 128, 16), ("B8", 0, 8))
-    ts(("t2", 0, 16), ("i2", 0, 16), 511, A.bitwise_and)
-    fill(("C32", 0, 128), 1.0 / 8192)
-    fill(("PT", 0, 1), 0.0)
-    fill(("PT", 1, 2), 7.5)
-    fill(("PT", 2, 3), -0.5)
-    fill(("C1", 0, 128), -1.0 / 128)
-    fill(("CB", 0, 128), -BIG / 128)
-    fill(("y", 0, 16), BIG)
-    fill(("mm", 0, 16), BIG)
-    fill(("RS", 0, 256), 1.0)
-    fill(("RS", 0, 256, 16), 0.0)
-    ts(("FB", 0, 144), ("F", 0, 144), BIG, A.mult)
-    ts(("FhB", 0, 144), ("F", 0, 144), 0.5 * BIG, A.mult)
-    cp(("wf", 0, 1), ("wti", 0, 1))
-    tt(("t2", 16, 32), ("t2", 0, 16), ("p16", 0, 16), A.add)
-    ts(("Fw", 0, 144), ("F", 0, 144), ("wf", 0, 1), A.mult, 1.0 / 2048, A.mult)
-    cp(("l2", 0, 16), ("t2", 16, 32))
-
-    ts(("X", 0, 512), (("EL", 0, 256), ("l1", 0, 32)), 1184.0, A.add, 2048.0, A.mult)
-    usum("pu", 0, 16, Z[0], 256, 512)
-    ts(("vi", 0, 16), ("pu", 0, 16), FLOOR, A.add)
-    op("v", lambda e: e.transpose(T.XT[:, :], T.X[:, :]), [("X", 0, 512)], [("XT", 0, 512)])
-    tt(("v", 0, 16), ("pu", 0, 16), ("vi", 0, 16), A.subtract)
-    cp((E[0], 0, 256), (("XT", 0, 512), ("l2", 0, 16)))
-    tt(("P", 0, 256), (("v", 0, 16), ("cl", 0, 16)), (E[0], 0, 256), A.mult)
-    h = hlist("P", "N", "off", 0, 256)
-    h[0]()
+    ts(("Fq", 0, 144), ("F", 0, 144), 0.25, A.mult)
     ts(("Fh", 0, 144), ("F", 0, 144), 0.5, A.mult)
-    h[1]()
+    for name, c in (("NI", -1.0), ("N2", -2.0), ("IB", -BIG), ("I16", 65536.0), ("I11", 2048.0), ("I14", 16384.0), ("IF", 1.0), ("JF", -1.0)):
+        ts((name, 0, 128), ("ID", 0, 128), c, A.mult)
+    for name, c in (("C32", 1.0 / 8192), ("C4", 4.0 / 128), ("CK", 864.0 / 128), ("CE", 2048.0 * ROT / 128), ("QF", 0.5)):
+        fill((name, 0, 128), c)
+    for name in ("SW", "SF"):
+        cp((name, 0, 64), ("ID", 64, 128))
+        cp((name, 64, 128), ("ID", 0, 64))
+    fill(("tau", 0, 1), -0.25)
+    fill(("acc", 2, 3), -0.5 / 128)
+    fill(("kd0", 0, 8), 0.0)
+    fill(("kd1", 0, 8), 0.0)
 
-    tt(("jb", 0, 16), ("pm", 0, 16), ("i8", 0, 16), A.add)
-    ts(("NI", 0, 128), ("ID", 0, 128), -1.0, A.mult)
+    def t8(k, n=8):
+        return ("t", 8 * k, 8 * k + n)
+
+    ts(("pm", 0, 16), ("ip", 0, 16), 15, A.bitwise_and)
     cp(("pmf", 0, 1), ("pm", 0, 1))
-    ts(("t1", 0, 16), ("i5", 0, 16), 255, A.bitwise_and)
-    ts(("t1", 16, 32), ("i6", 0, 16), 255, A.bitwise_and)
-    ts(("KC", 0, 256), ("i9", 0, 256), ("pmf", 0, 1), A.add, 2048.0, A.mult)
-    cp(("pn", 0, 16), ("t1", 0, 16))
-    cp(("p2", 0, 16), ("t1", 16, 32))
-    ts(("KC", 0, 256), ("KC", 0, 256), 0.5, A.add)
-    cp(("IF", 0, 128), ("ID", 0, 128))
-    cp(("JF", 0, 128), ("NI", 0, 128))
+    ts(t8(0), ("ip", 0, 8), 7, A.bitwise_and)
+    cp(("cl", 0, 8), t8(0))
+    ts(t8(1, 16), ("ip", 0, 16), 64, A.bitwise_and)
+    ts(t8(3, 16), t8(1, 16), 2.0, A.mult, ("pmf", 0, 1), A.add)
+    tt(t8(5, 16), t8(3, 16), ("i1", 0, 16), A.add)
+    ts(t8(7, 16), t8(5, 16), 255, A.bitwise_and)
+    cp(("l1", 0, 16), t8(7, 16))
+    ts(t8(9), ("ip", 0, 8), 3, A.logical_shift_right, 1, A.bitwise_and)
+    ts(t8(10), ("ip", 0, 8), 16, A.bitwise_and)
+    ts(t8(11), ("i2", 0, 8), 255, A.bitwise_and)
+    tt(t8(12), t8(10), t8(9), A.subtract)
+    tt(t8(13), t8(11), t8(12), A.add)
+    cp(("l2", 0, 8), t8(13))
+    ts(t8(14, 16), ("i3", 0, 16), 127, A.bitwise_and)
+    cp(("l3", 0, 16), t8(14, 16))
+    ts(t8(16), ("ip", 0, 8), 31, A.bitwise_and)
+    tt(t8(17), t8(16), ("i4", 0, 8), A.add)
+    cp(("l4", 0, 8), t8(17))
+    tt(t8(18), t8(3), ("i5", 0, 8), A.add)
+    ts(("cb", 0, 8), t8(18), 8.0, A.mult)
+    ts(("TH", 0, 128), ("i6", 0, 128), 128.0, A.mult)
+    ts(("K1", 0, 120), ("i6", 0, 120), 524288.0, A.mult)
+    fill(("K1", 120, 128), -17 * 524288.0)
+    ts(("K2", 0, 128), ("i7", 0, 128), ("pmf", 0, 1), A.add, 4096.0, A.mult)
 
-    def codes():
-        tt(("Rk", 0, 256), (("N", 0, 256), ("pn", 0, 16)), ("KC", 0, 256), A.add)
+    def lists(w):
+        tt(("P", 0, 128), (("v" + w, 0, 8), ("cl", 0, 8)), ("E" + w, 0, 128), A.mult)
+        ts(("N" + w, 0, 128), ("P", 0, 128), 5, A.logical_shift_right, 2047, A.bitwise_and)
+        cp(("off" + w, 0, 128), ("N" + w, 0, 128))
 
-    def consts2():
-        ts(("TH", 0, 256), ("i10", 0, 256), 524288.0, A.mult)
-        ts(("ci", 0, 16), ("jb", 0, 16), 148.0, A.add)
-        ts(("p31", 0, 16), ("ip", 0, 16), 31, A.bitwise_and)
-        ts(("t1", 0, 16), ("ci", 0, 16), 255, A.bitwise_and)
-        ts(("t2", 0, 32), ("i3", 0, 32), 255, A.bitwise_and)
-        ts(("cb", 0, 16), ("t1", 0, 16), 8.0, A.mult)
-        tt(("t1", 16, 32), ("p31", 0, 16), ("i4", 0, 16), A.add)
-        cp(("l3", 0, 32), ("t2", 0, 32))
-        cp(("l4", 0, 16), ("t1", 16, 32))
+    def vmod(w):
+        usum("pu", 0, 8, w, ZH, NM)
+        ts(("vi", 0, 8), ("pu", 0, 8), FLOOR, A.add)
+        tt(("v" + w, 0, 8), ("pu", 0, 8), ("vi", 0, 8), A.subtract)
 
-    def z4(src):
-        act(("Z4", 0, 256), src, AF.Copy)
-        act(("Z4", 256, 512), src, AF.Copy)
-        act(("Z4", 512, 1024), ("Z4", 0, 512), AF.Copy)
+    for w in "01":
+        wf = ("wf", int(w), int(w) + 1)
+        cp(wf, ("wti" + w, 0, 1))
+        ts(("Fw" + w, 0, 144), ("F", 0, 144), wf, A.mult, 1.0 / 2048, A.mult)
+        ts(("X", 0, 256), (("EL" + w, 0, 256), ("l1", 0, 16)), float(ROT), A.add, 2048.0, A.mult)
+        turn(("XT", 0, 256), ("X", 0, 256))
+        act(("E" + w, 0, 128), (("XT", 0, 256), ("l2", 0, 8)), AF.Copy)
+        act(("ZK" + w, ZH - 128, ZH), ("ZK" + w, ZH, NM), AF.Copy)
+        act(("ZK" + w, Z4, Z4 + 256), ("ZK" + w, ZH - 128, NM), AF.Copy)
+        vmod(w)
+        lists(w)
 
-    def tcol():
-        act(("Tt", 0, 240), ("ON", 0, 240), AF.Copy, None, ("PT", 1, 2))
-        act(("Th", 0, 240), ("ON", 0, 240), AF.Copy, None, ("PT", 2, 3))
+    def main(n):
+        w = str(n % 2)
+        zk, e, dall = "ZK" + w, "E" + w, ("D" + w, 0, 2048)
+        for lo, hi in GA:
+            tt(("DF", 128 * lo, 128 * hi), (dall, ("off" + w, 8 * lo, 8 * hi)), (zk, Z4, Z4 + 128 * (hi - lo)), A.subtract)
+            act((zk, 128 * lo, 128 * hi), ("DF", 128 * lo, 128 * hi), AF.Abs)
+            act(("SG", 128 * lo, 128 * hi), ("DF", 128 * lo, 128 * hi), AF.Sign, -0.5)
+        for lo, hi, top in ((64, 128, 256), (0, 64, 64)):
+            usum("pU", lo, hi, w, 16 * lo, 16 * hi)
+            ts(("Ui", lo, hi), ("pU", lo, hi), FLOOR, A.add)
+            tt(("Ub", lo, hi), ("pU", lo, hi), ("Ui", lo, hi), A.subtract)
+            if lo:
+                tt(("PB", 128, 256), (("Ub", 120, 128), ("cl", 0, 8)), (e, 0, 128), A.mult)
+            tt(("PB", lo, hi), ((e, 120, 128), ("cl", 0, 4)), ("Ub", lo, hi), A.mult)
+            ts(("NB", lo, top), ("PB", lo, top), 5, A.logical_shift_right, 2047, A.bitwise_and)
+            cp(("offb", lo, top), ("NB", lo, top))
+        fold(("pac", 64, 128), "Fq", "SG", 1024, 2048)
+        ts(("naf", 0, 8), ("pac", 120, 128), ("tau", 0, 1), A.is_lt, 8.0, A.mult)
+        act(("nab", 0, 64), (("naf", 0, 8), ("cl", 0, 4)), AF.Copy)
+        fold(("pac", 0, 64), "Fq", "SG", 0, 1024)
+        for lo, hi in GB:
+            tt(("BB", 128 * lo, 128 * hi), (dall, ("offb", 8 * lo, 8 * hi)), (zk, 128 * lo, 128 * hi), A.is_gt)
+        for lo, hi in ((8, 15), (0, 8)):
+            k = 8 * (hi - lo)
+            fold(("pb", 8 * lo, 8 * hi), "Fh", "BB", 128 * lo, 128 * hi, ("C4", ("ON", 0, k)), ("N2", ("nab", 0, k)))
+        for i in range(4):
+            lo, hi, bank = 4 * i, min(4 * i + 4, 15), "d%d" % (i % 2)
+            act(("DG", 128 * lo, 128 * hi), (dall, ("offb", 128 + 8 * lo, 128 + 8 * hi)), AF.Copy)
+            for q in range(lo, hi):
+                mm((bank, 128 * (q - lo), 128 * (q - lo + 1)), ("NI", (zk, 1920, 2048)), ("ID", ("DG", 128 * q, 128 * q + 128)))
+            act(("CC", 128 * lo, 128 * hi), (bank, 0, 128 * (hi - lo)), AF.Sign, -0.5)
+        for lo, hi in ((0, 8), (8, 15)):
+            fold(("pac", 128 + 8 * lo, 128 + 8 * hi), "Fq", "CC", 128 * lo, 128 * hi, ("ID", ("nab", 0, 8 * (hi - lo))))
 
-    def shift(e, lo, hi):
-        a, b = 16 * lo, 16 * hi
+    def choice(n):
+        w = str(n % 2)
+        zk = "ZK" + w
+        mm(("px", 120, 128), ("ID", ("K1", 120, 128)), ("ID", ("K2", 120, 128)), ("CK", ("ON", 0, 8)), ("I16", ("naf", 0, 8)))
+        mm(("px", 0, 120), ("ID", ("K1", 0, 120)), ("ID", ("K2", 0, 120)), ("CK", ("ON", 0, 120)), last=False)
+        act(("hb", 0, 120), ("pb", 0, 120), AF.Abs, ("tau", 0, 1), -1.0)
+        act(("fb", 0, 120), ("hb", 0, 120), AF.Relu, -8.0)
+        act(("fac", 0, 248), ("pac", 0, 248), AF.Relu, ("tau", 0, 1), -1.0)
+        mm(("px", 0, 120), ("IB", ("fb", 0, 120)), ("IB", ("fac", 0, 120)), ("IB", ("fac", 128, 248)), first=False)
+        tt(("x", 0, 128), ("px", 0, 128), ("N" + w, 0, 128), A.add)
+        tt(("m", 0, 64), ("x", 0, 64), ("x", 64, 128), A.max)
+        tt(("m", 64, 96), ("m", 0, 32), ("m", 32, 64), A.max)
+        tt(("m", 96, 112), ("m", 64, 80), ("m", 80, 96), A.max)
+        tt(("Ci", 0, 8), ("m", 96, 104), ("m", 104, 112), A.max)
+        ts(("Oj", 0, 8), ("Ci", 0, 8), 12, A.logical_shift_right, 4095, A.bitwise_and)
+        cp(("ou", 0, 8), ("Oj", 0, 8))
+        ts(("LH", 0, 8), ("Ci", 0, 8), 7, A.bitwise_and)
+        ts(("LH", 8, 16), ("Ci", 0, 8), 3, A.logical_shift_right, 255, A.bitwise_and)
+        cp((zk, NM, NM + 16), ("LH", 0, 16))
+        act((zk, ZH, NM), ((zk, 0, Z4 + 128), ("ou", 0, 8)), AF.Copy)
 
-        def fn(x):
-            x.matmul(T.d2[:, a - 16:b - 16], T.IF[:, :], T[e][:, a:b], True, False)
-            x.matmul(T.d2[:, a - 16:b - 16], T.JF[:, :], T[e][:, a - 16:b - 16], False, True)
-            return x.matmul(T.d2[:, 240 + a:240 + b], T.IF[:, :], T[e][:, a - 16:b - 16], True, True)
-        op("p", fn, [("IF", 0, 128), ("JF", 0, 128), (e, a - 16, b)], [("d2", a - 16, b - 16), ("d2", 240 + a, 240 + b)])
-
-    codes()
-    shift(E[0], 1, 16)
-    z4((Z[0], 256, 512))
-    tcol()
-    late = []
-
-    for t in range(RO):
-        ec, en, zc, zn = E[t % 2], E[(t + 1) % 2], Z[t % 2], Z[(t + 1) % 2]
-
-        def g1(lo, hi=None):
-            hi = hi or lo + 1
-            tt(("DF", 256 * lo, 256 * hi), (DALL, ("off", 16 * lo, 16 * hi)), ("Z4", 0, 256 * (hi - lo)), A.subtract)
-
-        def absq(lo, hi):
-            act(("ZK", 256 * lo + 256, 256 * hi + 256), ("DF", 256 * lo, 256 * hi), AF.Abs)
-            usum("pU", 16 * lo, 16 * hi, "ZK", 256 * lo + 256, 256 * hi + 256)
-
-        def sgn(lo, hi):
-            act(("SG", 256 * lo, 256 * hi), ("DF", 256 * lo, 256 * hi), AF.Sign, -0.5)
-
-        def cnta(lo, hi):
-            fold(("pa", 16 * lo, 16 * hi), "FhB", "SG", 256 * lo, 256 * hi, (("CB", 0, 128), ("Th", 0, 16 * (hi - lo))))
-
-        def cv(q):
-            tt(("CC", 256 * q, 256 * q + 256), (DALL, ("offc", 16 * q, 16 * q + 16)), ("ZK", 0, 256), A.is_gt)
-
-        pairs = [(q, min(q + 2, NS)) for q in range(0, NS, 2)]
-
-        def sgath(n):
-            lo, hi = pairs[n]
-            act(("DG", 256 * lo, 256 * hi), (DALL, ("offc", 16 * lo, 16 * hi)), AF.Copy)
-            bank = "d%d" % (n % 2)
-
-            def fn(e):
-                for k in range(hi - lo):
-                    o = ap((bank, 256 * k, 256 * k + 256))
-                    e.matmul(o, T.NI[:, :], T.ZK[:, 0:256], True, False)
-                    r = e.matmul(o, T.ID[:, :], T.DG[:, 256 * (lo + k):256 * (lo + k) + 256], False, True)
-                return r
-            op("p", fn, [("NI", 0, 128), ("ID", 0, 128), ("ZK", 0, 256), ("DG", 256 * lo, 256 * hi)], [(bank, 0, 256 * (hi - lo))])
-
-        def ssign(n):
-            lo, hi = pairs[n]
-            act(("CC", 256 * lo, 256 * hi), ("d%d" % (n % 2), 0, 256 * (hi - lo)), AF.Sign, -0.5)
-
-        def bv(lo, hi):
-            tt(("BB", 256 * lo, 256 * hi), (DALL, ("offb", 16 * lo, 16 * hi)), ("ZK", 256 * lo + 256, 256 * hi + 256), A.is_gt)
-            fold(("pb", 16 * lo, 16 * hi), "F", "BB", 256 * lo, 256 * hi, (("C1", 0, 128), ("Tt", 0, 16 * (hi - lo))))
-
-        g1(15)
-        for f in late:
-            f()
-        sgn(15, 16)
-        act((zc, 0, 256), ("DF", 3840, 4096), AF.Abs)
-        fold(("pu", 32, 48), "Fh", "SG", 3840, 4096)
-        g1(12, 15)
-        absq(12, 15)
-        ts(("a0c", 0, 16), ("pu", 32, 48), ("PT", 0, 1), A.is_lt, 256.0, A.mult)
-        sgn(12, 15)
-        g1(11)
-        tt(("o0i", 0, 16), ("a0c", 0, 16), ("jb", 0, 16), A.add)
-        act(("SB", 0, 240), (("a0c", 0, 16), ("cl", 0, 15)), AF.Identity, -BIG, BIG / 128)
-        g1(10)
-        cp(("o0u", 0, 16), ("o0i", 0, 16))
-        g1(9)
-        cp(("ZK", 0, 256), ((zc, 0, 512), ("o0u", 0, 16)))
-        usum("pu", 64, 80, "ZK", 0, 256)
-        g1(7, 9)
-        absq(8, 12)
-        cnta(12, 15)
-        sgn(8, 12)
-        ts(("wi", 0, 16), ("pu", 64, 80), FLOOR, A.add)
-        g1(6)
-        tt(("w", 0, 16), ("pu", 64, 80), ("wi", 0, 16), A.subtract)
-        g1(4, 6)
-        absq(4, 8)
-        tt(("Pc", 0, 240), (("w", 0, 16), ("cl", 0, 15)), (ec, 0, 240), A.mult)
-        h = hlist("Pc", "Nc", "offc", 0, 240)
-        g1(3)
-        h[0]()
-        g1(2)
-        h[1]()
-        absq(2, 4)
-        g1(0, 2)
-        absq(0, 2)
-        sgath(0)
-        sgath(1)
-        ssign(0)
-        cnta(8, 12)
-        for n in range(2, len(pairs) - 1):
-            sgath(n)
-            ssign(n - 1)
-
-        chain = [lambda: ts(("Ui", 0, 240), ("pU", 0, 240), FLOOR, A.add),
-                 lambda: tt(("Ub", 0, 240), ("pU", 0, 240), ("Ui", 0, 240), A.subtract),
-                 lambda: tt(("Pb", 0, 240), ((ec, 240, 256), ("cl", 0, 15)), ("Ub", 0, 240), A.mult)]
-        vq = list(range(14, NS - 1, -1))
-        for n, q in enumerate(vq):
-            cv(q)
-            if len(vq) - n <= len(chain):
-                chain[len(chain) - (len(vq) - n)]()
-        fold(("pc", 16 * NS, 240), "FB", "CC", 256 * NS, 3840, (("CB", 0, 128), ("Tt", 0, 240 - 16 * NS)))
-        sgath(len(pairs) - 1)
-        ssign(len(pairs) - 2)
-        ssign(len(pairs) - 1)
-        h = hlist("Pb", "Nb", "offb", 0, 240)
-        h[0]()
-        h[1]()
-
-        bv(0, 4)
-        fold(("pc", 0, 16 * NS), "FhB", "CC", 0, 256 * NS, (("CB", 0, 128), ("Th", 0, 16 * NS)))
-        bv(4, 8)
-        sgn(4, 8)
-        cnta(4, 8)
-        sgn(0, 4)
-        cnta(0, 4)
-        act(("pcS", 0, 240), ("pc", 0, 240), AF.Copy)
-        bv(8, 12)
-        bv(12, 15)
-        tt(("mm", 16, 256), ("pa", 0, 240), ("pcS", 0, 240), A.min)
-        tt(("Rg", 0, 256), (("mm", 0, 256), ("p2", 0, 16)), ("Rk", 0, 256), A.min)
-
-        tt(("y", 16, 256), ("pb", 0, 240), ("SB", 0, 240), A.mult)
-        tt(("x", 0, 256), (("y", 0, 256), ("p2", 0, 16)), ("Rg", 0, 256), A.min)
-        op("v", lambda e: e.tensor_tensor_scan(T.Sc[:, :], T.RS[:, :], T.x[:, :], 0.0, A.mult, A.max),
-           [("RS", 0, 256), ("x", 0, 256)], [("Sc", 0, 256)])
-        sv = ("Sc", 15, 256, 16)
-        ts(("Oj", 0, 16), sv, -1024.0, A.add, 1.0 / 2048, A.mult)
-        ts(("Ni", 0, 16), sv, 863.5, A.add)
-        cp(("ou", 0, 16), ("Oj", 0, 16))
-        ts(("LH", 0, 16), ("Ni", 0, 16), 7, A.bitwise_and)
-        ts(("LH", 16, 32), ("Ni", 0, 16), 3, A.logical_shift_right, 255, A.bitwise_and)
-        cp((zn, 256, 512), (("ZK", 0, 4096), ("ou", 0, 16)))
-        cp((zn, 512, 544), ("LH", 0, 32))
-
+    def send(n):
+        w, t = str(n % 2), n // 2
+        zk, lc = "ZK" + w, "L%d" % n
         dst = target(cores, rank, t)
         via = route(topo, core, dst)
         to = dst if via == core else via
-        m, n = engines(topo, core, to)
+        m, k = engines(topo, core, to)
         rid, pid = topo.addr(to, core)
-        land, sem = (("L%d" % t), "arr%d" % t) if to == dst else (("R%d" % t), "rl%d" % t)
-        before("g", [(zn, 256, 544)], [])
-        g.remote_dma(T[land][:, :], T[zn][:, 256:544], T.sem[sem], T.sem["loc%d" % t], pid, rid, m)
-        after("g", [(zn, 256, 544)], [], ("loc%d" % t, n))
-        total["loc%d" % t] = n
+
+        def issue(total):
+            g.remote_dma(T[lc][:, :], T[zk][:, ZH:NM + 16], T.sem[("arr%d" if to == dst else "rl%d") % n], T.sem["loc%d" % n], pid, rid, m)
+            total["loc%d" % n] = k
+            return ("loc%d" % n, k)
+        calls.append(("g", [(zk, ZH, NM + 16)], [("sent", n, n + 1)], 500.0, HOP, issue))
         frm = cores[(rank - 1 - t % 3) % len(cores)]
-        lc = "L%d" % t
-        narr = engines(topo, route(topo, frm, core), core)[1]
-        acc[lc] = [(0, PAY, True, ("arr%d" % t, narr), "net")]
+        last = route(topo, frm, core)
+        arr = ("arr%d" % n, engines(topo, last, core)[1])
+        calls.append(("net", [("sent", n, n + 1)], [(lc, 0, PAY)], 0.0, 0.0 if last == frm else HOP, lambda total: arr))
 
-        last = t == RO - 1
-        if last:
-            dma("y", "yz", T.yz[:, :], T[zn][:, 256:512], [(zn, 256, 512)], [])
-        else:
-            usum("pu", 0, 16, zn, 256, 512)
-            z4((zn, 256, 512))
-        if t == 0:
-            consts2()
-        ts(("NB", 0, 16), sv, 524288.0, A.is_lt, 67108864.0, A.mult)
-        if not last:
-            ts(("fl", 0, 16), sv, 524288.0, A.is_ge)
-            op("p", lambda e: e.matmul(T.pu[:, 96:112], T.ON[:, 0:128], T.fl[:, :], True, True),
-               [("ON", 0, 128), ("fl", 0, 16)], [("pu", 96, 112)])
-        tt(("S3", 0, 16), sv, ("NB", 0, 16), A.add)
-        tt(("keep", 0, 240), (("S3", 0, 16), ("cl", 0, 15)), ("TH", 16, 256), A.is_lt)
-        if not last:
-            ts(("vi", 0, 16), ("pu", 0, 16), FLOOR, A.add)
-        tt(("kd", 0, 240), ("keep", 0, 240), ("d2", 0, 240), A.mult)
-        if not last:
-            tt(("v", 0, 16), ("pu", 0, 16), ("vi", 0, 16), A.subtract)
-        tt((en, 16, 256), ("kd", 0, 240), ("d2", 256, 496), A.add)
-        if not last:
-            op("s", lambda e: e.activation(T.jk[:, :], T.pu[:, 96:112], AF.Identity, accum_out=T.As[:, :]), [("pu", 96, 112)],
-               [("jk", 0, 16), ("As", 0, 1)])
-            tt(("P", 16, 256), (("v", 0, 16), ("cl", 0, 15)), (en, 16, 256), A.mult)
-            cp(("Ai", 0, 1), ("As", 0, 1))
-            h = hlist("P", "N", "off", 16, 256)
-            h[0]()
-            ts(("Aj", 0, 1), ("Ai", 0, 1), 1, A.bitwise_and)
-            h[1]()
-            cp(("PT", 0, 1), ("Aj", 0, 1))
-            act(("PT", 1, 2), ("PT", 0, 1), AF.Identity, 7.5)
-            act(("PT", 2, 3), ("PT", 0, 1), AF.Identity, -0.5)
-            tcol()
-            shift(en, 2, 16)
-            codes()
-        else:
-            cp(("X", 0, 512), ((en, 0, 256), ("l3", 0, 32)))
+    def travel(n):
+        w, t = str(n % 2), n // 2
+        zk, e = "ZK" + w, "E" + w
+        mm(("pE", 8, 128), ("IF", (e, 0, 120)))
+        mm(("pE", 136, 256), ("IF", (e, 8, 128)), ("JF", (e, 0, 120)))
+        tt(("keep", 0, 128), (("Oj", 0, 8), ("cl", 0, 8)), ("TH", 0, 128), A.is_lt)
+        tt(("kd" + w, 8, 128), ("pE", 136, 256), ("keep", 8, 128), A.mult)
+        if t == RO - 1:
+            dmas("y", "yz_" + w, [(b, a) for a, b in placed(T[zk], ZH, T.yz, w)], [(zk, ZH, NM)], [])
+            return
+        dmas("y", "rep%d" % n, [(T[zk][:, c:c + 128], T[zk][:, ZH:NM]) for c in range(Z4, ZH, 128)], [(zk, ZH, NM)], [(zk, Z4, ZH)])
+        act(("fl", 0, 8), ("keep", 120, 128), AF.Copy, accum=("acc", n % 2, n % 2 + 1))
+        if n % 2:
+            mm(("pu", 16, 17), *[("QF", ("acc", k, k + 1)) for k in range(3)])
+            cp(("ri", 0, 1), ("pu", 16, 17))
+            tt(("tau", 0, 1), ("pu", 16, 17), ("ri", 0, 1), A.subtract)
+        vmod(w)
 
-        tt(("ci", 0, 16), (lc, 256, 272), ("cb", 0, 16), A.add)
-        ts(("e15", 0, 16), (lc, 272, 288), 8.0, A.mult, 1184.0, A.add)
-        cp(("cu", 0, 16), ("ci", 0, 16))
-        tt(("e16", 0, 16), ("e15", 0, 16), (lc, 256, 272), A.add)
-        tt(("su", 0, 256), (DALL, ("cu", 0, 16)), (lc, 0, 256), A.add)
-        ts((en, 0, 16), ("e16", 0, 16), 2048.0, A.mult)
-        ts(("sh", 0, 256), ("su", 0, 256), 1, A.logical_shift_right)
-        if not last:
-            tt(("P", 0, 16), ("v", 0, 16), (en, 0, 16), A.mult)
-        cp((DALL, ("cu", 0, 16)), ("sh", 0, 256))
-        if not last:
-            h = hlist("P", "N", "off", 0, 16)
-            h[0]()
-            shift(en, 1, 2)
-            late = [h[1], lambda: tt(("Rk", 1, 256, 16), ("N", 0, 16), ("KC", 1, 256, 16), A.add)]
+    def arrival(n):
+        w, lc = str(n % 2), "L%d" % n
+        d, dall = T["D" + w], ("D" + w, 0, 2048)
+        both = n in BOTH
+        mm(("pE", 256, 264), ("ID", (lc, 128, 136)), ("ID", ("cb", 0, 8)))
+        if both:
+            mm(("pE", 264, 272), ("SW", (lc, 128, 136)), ("SW", ("cb", 0, 8)))
+        mm(("pE", 0, 8), ("I11", (lc, 128, 136)), ("I14", (lc, 136, 144)), ("CE", ("ON", 0, 8)))
+        k = 16 if both else 8
+        cp(("cu", 0, k), ("pE", 256, 256 + k))
+        tt(("E" + w, 0, 128), ("pE", 0, 128), ("kd" + w, 0, 128), A.add)
+        tt(("su", 0, 128), (dall, ("cu", 0, 8)), (lc, 0, 128), A.add)
+        ts(("sh", 0, 128), ("su", 0, 128), 0.5, A.mult, -0.25, A.add)
+        if both:
+            mm(("pE", 384, 512), ("SF", ("su", 0, 128)))
+            ts(("sh", 128, 256), ("pE", 384, 512), 0.5, A.mult, -0.25, A.add)
+        cp((dall, ("cu", 0, k)), ("sh", 0, 16 * k))
+        if n // 2 < RO - 1:
+            if not both:
+                dmas("y", "xc%d" % n, [(d[64:128, 0:1024], d[0:64, 0:1024]), (d[0:64, 1024:2048], d[64:128, 1024:2048])], [dall], [dall],
+                     XC)
+            lists(w)
+            return
+        r = slice(64 * int(w), 64 * int(w) + 64)
+        dmas("y", "yd_" + w, [(T.yd[r, 2048 - ROT:3072 - ROT], d[0:64, 0:1024]), (T.yd[r, 0:2048 - ROT], d[64:128, ROT:2048]),
+                              (T.yd[r, 3072 - ROT:2048], d[64:128, 1024:ROT])], [dall], [])
+        act(("X", 0, 256), (("E" + w, 0, 128), ("l3", 0, 16)), AF.Copy)
+        turn(("XT", 0, 256), ("X", 0, 256))
+        act(("YL" + w, 0, 128), (("XT", 0, 256), ("l4", 0, 8)), AF.Identity, -float(ROT), 1.0 / 2048)
+        dmas("s", "ye_" + w, [(b, a) for a, b in placed(T["YL" + w], 0, T.ye, w)], [("YL" + w, 0, 128)], [])
+
+    stage = [-1] * len(calls)
+    for n in range(STEPS):
+        for f, late in zip((main, choice, send, travel, arrival), LATE):
+            f(n)
+            stage += [n + late] * (len(calls) - len(stage))
+
+    known = {k: {} for k in eng}
+    snap, acc, total = {}, {}, {}
+
+    def wait(q, tok):
+        s, n = tok
+        if known[q].get(s, 0) >= n:
+            return
+        eng[q].wait_ge(T.sem[s], n)
+        for a, b in snap.get(tok, {}).items():
+            if known[q].get(a, 0) < b:
+                known[q][a] = b
+        known[q][s] = n
+
+    for q, reads, writes, busy, done, issue in in_order(calls, stage):
+        if q == "net":
+            acc[writes[0][0]] = [(0, PAY, True, issue(total), q)]
             continue
-
-        dma("y", "yda", T.yd[:, 864:2048], T.D[:, 0:1184], [("D", 0, 1184)], [])
-        dma("s", "ydb", T.yd[:, 0:864], T.D[:, 1184:2048], [("D", 1184, 2048)], [])
-        cp(("X", 15, 512, 32), (en, 0, 16))
-        cp(("X", 31, 512, 32), (en, 0, 16))
-        op("v", lambda e: e.transpose(T.XT[:, :], T.X[:, :]), [("X", 0, 512)], [("XT", 0, 512)])
-        ts(("YL", 0, 256), (("XT", 0, 512), ("l4", 0, 16)), 1.0 / 2048, A.mult, -1184.0, A.add)
-        dma("y", "ye", T.ye[:, :], T.YL[:, :], [("YL", 0, 256)], [])
+        need = {}
+        for regs, wr in ((reads, False), (writes, True)):
+            for b, lo, hi in regs:
+                for l2, h2, w2, tok, q2 in acc.get(b, []):
+                    hit = (wr or w2) and lo < h2 and l2 < hi
+                    if b in PSUM:
+                        hit = q2 != q or (q != "p" and hit)
+                    if hit and need.get(tok[0], 0) < tok[1]:
+                        need[tok[0]] = tok[1]
+        for s in sorted(need):
+            wait(q, (s, need[s]))
+        tok = issue(total)
+        snap[tok] = dict(known[q])
+        for b, lo, hi in writes:
+            acc[b] = [r for r in acc.get(b, []) if not (lo <= r[0] and r[1] <= hi and b not in PSUM)] + [(lo, hi, True, tok, q)]
+        for b, lo, hi in reads:
+            acc[b] = [r for r in acc.get(b, []) if not (r[4] == q and not r[2] and lo <= r[0] and r[1] <= hi and r[3][0] == tok[0])]
+            acc[b].append((lo, hi, False, tok, q))
+        for b, lo, hi in list(reads) + list(writes):
+            if b in PSUM:
+                acc[b] = list({(r[4], r[2], r[0], r[1]): r for r in acc[b]}.values())
 
     for s in sorted(total):
         wait("g", (s, total[s]))

@@ -1,6 +1,7 @@
 import numpy as np
 from concourse.mybir import AluOpType as A
 from concourse.mybir import ActivationFunctionType as AF
+from concourse.mybir import AxisListType
 
 RO = 5
 NENG = 8
@@ -9,14 +10,19 @@ BIG = 2.0 ** 28
 FLOOR = -1055.5 / 2048
 ROT = 1184
 JR = 256 - ROT // 8
-Z4, ZH, NM = 2048, 2432, 2560
-CYC, PEC, GATHER, SCATTER, MINC = 0.83, 0.42, 1.3, 3.8, 85
-WAKE, SAME, DMA, HOP, XC = 300.0, 200.0, 1200.0, 1500.0, 1900.0
-PASSES = 4
+QB, X0, Z4, ZH, NM = 640, 2560, 2688, 3072, 3200
+CYC, PEC, GATHER, SCATTER, MINC = 0.83, 0.42, 1.3, 3.4, 70
+WAKE, DMA, HOP, XC = 260.0, 1500.0, 1700.0, 2100.0
+PASSES, SHAKE, ORDERS = 30, 300.0, {}
+D15, SV, CV, RED = 0, 0, 0, 1
 BOTH = ()
 LATE = (0, 0, 0, 0.5, 0.5)
-GA = [(12, 16), (8, 12), (4, 8), (0, 4)]
+GA = [(12, 16, "v"), (8, 12, "v"), (4, 8, "v"), (0, 4, "v")]
 GB = [(8, 12), (12, 15), (0, 4), (4, 8)]
+GC = [(0, 4, "s"), (4, 8, "s"), (8, 12, "s"), (12, 15, "s")]
+CF = [(0, 8), (8, 15)]
+DB = ["d0", "d1", "d2"]
+UB = {120: "pU", 64: "pU", 0: "pb"}
 
 
 def _s(n, dt):
@@ -25,17 +31,17 @@ def _s(n, dt):
 
 SCRATCH = {}
 for _w in "01":
-    for _n, _c, _d in (("D", 2048, "bfloat16"), ("ZK", 2576, "bfloat16"), ("Fw", 144, "bfloat16"), ("E", 128, "float32"),
+    for _n, _c, _d in (("D", 2048, "bfloat16"), ("ZK", 3216, "bfloat16"), ("Fw", 144, "bfloat16"), ("E", 128, "float32"),
                        ("v", 8, "float32"), ("kd", 128, "float32"), ("N", 128, "int32"), ("EL", 256, "int32"), ("wti", 1, "int32"),
                        ("off", 128, "uint16"), ("YL", 128, "float32")):
         SCRATCH[_n + _w] = _s(_c, _d)
-for _n, _w in (("DF", 2048), ("SG", 2048), ("CC", 1920), ("BB", 1920), ("DG", 1920), ("fac", 248), ("hb", 120), ("fb", 120),
+for _n, _w in (("DF", 2048), ("SG", 2048), ("CC", 1920), ("BB", 1920), ("DG", 2048), ("fa", 120), ("hb", 120), ("fb", 120),
                ("naf", 16), ("nab", 64), ("fl", 8), ("cb", 8), ("K1", 128), ("K2", 128),
-               ("O8", 8), ("B8a", 8), ("B8", 8), ("F", 144), ("Fh", 144), ("Fq", 144),
-               ("ON", 128), ("ID", 128), ("NI", 128), ("N2", 128), ("IB", 128), ("I11", 128), ("I14", 128), ("I16", 128),
+               ("O8", 8), ("B8a", 8), ("B8", 8), ("F", 144), ("Fh", 144), ("Fq", 144), ("FB", 144), ("FC", 144), ("Tt", 128),
+               ("ON", 128), ("ID", 128), ("NI", 128), ("N2", 128), ("IB", 128), ("IP", 128), ("I11", 128), ("I14", 128), ("I16", 128),
                ("C32", 128), ("C4", 128), ("CK", 128), ("CE", 128), ("SW", 128)):
     SCRATCH[_n] = _s(_w, "bfloat16")
-for _n, _w in (("Ub", 128), ("x", 128), ("m", 112), ("keep", 128), ("acc", 3), ("tau", 1),
+for _n, _w in (("Ub", 128), ("x", 128), ("m", 112), ("code", 8), ("keep", 128), ("acc", 3), ("tau", 1),
                ("X", 256), ("XT", 256), ("wf", 2), ("IF", 128), ("JF", 128), ("QF", 128), ("pmf", 1), ("TH", 128), ("su", 128), ("SF", 128)):
     SCRATCH[_n] = _s(_w, "float32")
 for _n, _w in (("P", 128), ("PB", 256), ("NB", 256), ("Ui", 128), ("vi", 8), ("Ci", 8), ("Oj", 8), ("LH", 16), ("ri", 1), ("ci", 8),
@@ -44,14 +50,14 @@ for _n, _w in (("P", 128), ("PB", 256), ("NB", 256), ("Ui", 128), ("vi", 8), ("C
     SCRATCH[_n] = _s(_w, "int32")
 for _n, _w in (("offb", 256), ("ou", 8), ("cu", 16), ("cl", 8), ("l1", 16), ("l2", 8), ("l3", 16), ("l4", 8)):
     SCRATCH[_n] = _s(_w, "uint16")
-PSUM = ["pu", "pU", "pac", "pb", "px", "pE", "d0", "d1"]
+PSUM = ["pU", "pac", "pb", "px", "pE", "d0", "d1", "d2"]
 for _n in PSUM:
     SCRATCH[_n] = ("psum", [128, 512], "float32")
 STEPS = 2 * RO
 for _t in range(STEPS):
     SCRATCH["L%d" % _t] = _s(PAY, "bfloat16")
 SEMAPHORES = (["qv", "qs", "qp", "qg"] + [k + w for k in ("wt", "zv", "ef", "dv", "yd", "ye", "yz") for w in ("_0", "_1")] +
-              [k + str(t) for k in ("arr", "rl", "loc", "rep", "xc") for t in range(STEPS)])
+              [k + str(t) for k in ("arr", "rl", "loc", "rep", "rx", "xc") for t in range(STEPS)])
 
 
 def target(cores, rank, t):
@@ -88,29 +94,29 @@ def relay_program(g, core, T, topo):
 
 
 def in_order(calls, stage):
+    sign = tuple((c[0], c[3], c[4]) for c in calls)
+    if sign in ORDERS:
+        return [calls[i] for i in ORDERS[sign]]
     n = len(calls)
-    pre = [dict() for _ in range(n)]
+    busy = [c[3] for c in calls]
+    fwd = [dict() for _ in range(n)]
     seen = {}
-    for i, (q, reads, writes, busy, done, issue) in enumerate(calls):
+    for i, (q, reads, writes, _, done, issue) in enumerate(calls):
         for regs, wr in ((reads, False), (writes, True)):
             for b, lo, hi in regs:
                 for l2, h2, w2, j in seen.get(b, []):
-                    data = (wr or w2) and lo < h2 and l2 < hi
-                    if j != i and (data or b in PSUM):
-                        pre[i][j] = pre[i].get(j, False) or calls[j][0] != q or (data and q != "p")
+                    if j != i and (wr or w2) and lo < h2 and l2 < hi:
+                        chain = q == "p" and calls[j][0] == "p" and b in PSUM
+                        fwd[i][j] = max(fwd[i].get(j, 0.0), busy[j] if chain else calls[j][4] + WAKE)
         for b, lo, hi in writes:
             seen[b] = [r for r in seen.get(b, []) if not (lo <= r[0] and r[1] <= hi)] + [(lo, hi, True, i)]
         for b, lo, hi in reads:
             seen.setdefault(b, []).append((lo, hi, False, i))
-        for b, lo, hi in list(reads) + list(writes):
-            if b in PSUM:
-                seen[b] = seen[b][-12:]
-    busy = [c[3] for c in calls]
-    fwd = [{j: calls[j][4] + (SAME if calls[j][0] == calls[i][0] else WAKE) if w else busy[j] for j, w in pre[i].items()} for i in range(n)]
     bwd = [dict() for _ in range(n)]
     for i in range(n):
         for j, lag in fwd[i].items():
             bwd[j][i] = lag + busy[i] - busy[j]
+    banks = [sorted({r[0] for r in c[1] + c[2] if r[0] in PSUM}) for c in calls]
 
     def place(before, after, first, key):
         left, at, taken = [len(p) for p in before], [0.0] * n, {}
@@ -118,15 +124,26 @@ def in_order(calls, stage):
         while ready:
             i = min(ready, key=lambda i: key[i])
             ready.remove(i)
+            q = calls[i][0]
             t = max([first[i]] + [at[j] + lag for j, lag in before[i].items()])
-            l = taken.setdefault(calls[i][0], [])
-            k = len(l)
-            while k and l[k - 1][1] > t:
-                k -= 1
-            while k < len(l) and l[k][0] < t + busy[i]:
-                t = max(t, l[k][1])
-                k += 1
-            l.insert(k, (t, t + busy[i]))
+            moved = True
+            while moved:
+                moved = False
+                for r in [q] + banks[i]:
+                    l = taken.setdefault(r, [])
+                    k = len(l)
+                    while k and l[k - 1][1] + WAKE > t:
+                        k -= 1
+                    for a, b, q2 in l[k:]:
+                        pad = 0.0 if q2 == q else WAKE
+                        if a - pad < t + busy[i] and t < b + pad and (r == q or pad):
+                            t, moved = b + pad, True
+            for r in [q] + banks[i]:
+                l = taken[r]
+                k = len(l)
+                while k and l[k - 1][0] > t:
+                    k -= 1
+                l.insert(k, (t, t + busy[i], q))
             at[i] = t
             for j in after[i]:
                 left[j] -= 1
@@ -138,14 +155,21 @@ def in_order(calls, stage):
     for i in range(n - 1, -1, -1):
         way[i] = max([calls[i][4]] + [way[k] + fwd[k][i] for k in bwd[i]])
     at = place(fwd, bwd, [0.0] * n, [(stage[i], -way[i], i) for i in range(n)])
-    best = None
-    for _ in range(PASSES):
+    best, seed = None, 1
+    for p in range(PASSES):
         end = max(at[i] + calls[i][4] for i in range(n))
         if best is None or end < best[0]:
             best = (end, at)
-        back = place(bwd, fwd, [c[4] - c[3] for c in calls], [(-at[i] - busy[i], -i) for i in range(n)])
+        elif p % 3 == 0:
+            at = best[1]
+        shake = []
+        for i in range(n):
+            seed = (seed * 1103515245 + 12345) % 2147483648
+            shake.append(SHAKE * seed / 2147483648 if p % 3 == 0 and p else 0.0)
+        back = place(bwd, fwd, [c[4] - c[3] for c in calls], [(-at[i] - busy[i] + shake[i], -i) for i in range(n)])
         at = place(fwd, bwd, [0.0] * n, [(-back[i] - busy[i], i) for i in range(n)])
-    return [calls[i] for i in sorted(range(n), key=lambda i: (best[1][i], i))]
+    ORDERS[sign] = sorted(range(n), key=lambda i: (best[1][i], i))
+    return [calls[i] for i in ORDERS[sign]]
 
 
 def rank_program(g, core, T, topo):
@@ -242,12 +266,12 @@ def rank_program(g, core, T, topo):
     def pns(out, terms):
         return sum(max(64, out[2] - out[1]) * (4 if SCRATCH[l][2] == "float32" else 1) * PEC for l, r in terms)
 
-    def mm(out, *terms, first=True, last=True):
+    def mm(out, *terms, first=True, last=True, keep=None):
         def fn(e):
             for n, (l, r) in enumerate(terms):
                 x = e.matmul(ap(out), T[l][:, :], ap(r), first and n == 0, last and n == len(terms) - 1)
             return x
-        op("p", fn, [(l, 0, 128) for l, r in terms] + [rg(r) for l, r in terms], [rg(out)], pns(out, terms))
+        op("p", fn, [(l, 0, 128) for l, r in terms] + [rg(r) for l, r in terms], [keep or rg(out)], pns(out, terms))
 
     def fold(out, fm, src, lo, hi, *extra):
         def fn(e):
@@ -287,7 +311,7 @@ def rank_program(g, core, T, topo):
         dmas("y", "zv_" + w, placed(T["ZK" + w], ZH, T.zv, w), [], [("ZK" + w, ZH, NM)])
         dmas("s" if w == "0" else "y", "dv_" + w,
              [(T["D" + w][h, ROT:2048], T.dv[r, 0:2048 - ROT]) for h in hs] + [(T["D" + w][h, 0:ROT], T.dv[r, 2048 - ROT:2048]) for h in hs],
-             [], [("D" + w, 0, 2048)])
+             [], [("D" + w, 0, 2048)], XC)
 
     fill(("O8", 0, 8), 1.0)
     fill(("F", 0, 144), 0.0)
@@ -304,16 +328,20 @@ def rank_program(g, core, T, topo):
     select("B8", "B8a", [[16, 8]], A.is_ge, 0.0, 15, -1)
     select("ID", "ON", [[-1, 128]], A.is_equal, 0.0, 0, 1)
     cp(("F", 15, 128, 16), ("B8", 0, 8))
-    ts(("Fq", 0, 144), ("F", 0, 144), 0.25, A.mult)
-    ts(("Fh", 0, 144), ("F", 0, 144), 0.5, A.mult)
-    for name, c in (("NI", -1.0), ("N2", -2.0), ("IB", -BIG), ("I16", 65536.0), ("I11", 2048.0), ("I14", 16384.0), ("IF", 1.0), ("JF", -1.0)):
+    for name, c in (("Fq", 0.25), ("Fh", 0.5), ("FB", 0.25 * BIG), ("FC", 0.5 * BIG)):
+        ts((name, 0, 144), ("F", 0, 144), c, A.mult)
+    for name, c in (("NI", -1.0), ("N2", -2.0), ("IB", -BIG), ("IP", BIG), ("I16", -65536.0), ("I11", 2048.0), ("I14", 16384.0),
+                    ("IF", 1.0), ("JF", -1.0)):
         ts((name, 0, 128), ("ID", 0, 128), c, A.mult)
     for name, c in (("C32", 1.0 / 8192), ("C4", 4.0 / 128), ("CK", 864.0 / 128), ("CE", 2048.0 * ROT / 128), ("QF", 0.5)):
         fill((name, 0, 128), c)
-    for name in ("SW", "SF"):
-        cp((name, 0, 64), ("ID", 64, 128))
-        cp((name, 64, 128), ("ID", 0, 64))
+    if BOTH:
+        for name in ("SW", "SF"):
+            cp((name, 0, 64), ("ID", 64, 128))
+            cp((name, 64, 128), ("ID", 0, 64))
     fill(("tau", 0, 1), -0.25)
+    fill(("Tt", 0, 64), -0.25)
+    fill(("Tt", 64, 128), 3.75)
     fill(("acc", 2, 3), -0.5 / 128)
     fill(("kd0", 0, 8), 0.0)
     fill(("kd1", 0, 8), 0.0)
@@ -344,8 +372,8 @@ def rank_program(g, core, T, topo):
     tt(t8(18), t8(3), ("i5", 0, 8), A.add)
     ts(("cb", 0, 8), t8(18), 8.0, A.mult)
     ts(("TH", 0, 128), ("i6", 0, 128), 128.0, A.mult)
-    ts(("K1", 0, 120), ("i6", 0, 120), 524288.0, A.mult)
-    fill(("K1", 120, 128), -17 * 524288.0)
+    ts(("K1", 0, 120), ("i6", 0, 120), 5.0, A.add, 524288.0, A.mult)
+    fill(("K1", 120, 128), 524288.0)
     ts(("K2", 0, 128), ("i7", 0, 128), ("pmf", 0, 1), A.add, 4096.0, A.mult)
 
     def lists(w):
@@ -354,9 +382,9 @@ def rank_program(g, core, T, topo):
         cp(("off" + w, 0, 128), ("N" + w, 0, 128))
 
     def vmod(w):
-        usum("pu", 0, 8, w, ZH, NM)
-        ts(("vi", 0, 8), ("pu", 0, 8), FLOOR, A.add)
-        tt(("v" + w, 0, 8), ("pu", 0, 8), ("vi", 0, 8), A.subtract)
+        usum("pE", 280, 288, w, ZH, NM)
+        ts(("vi", 0, 8), ("pE", 280, 288), FLOOR, A.add)
+        tt(("v" + w, 0, 8), ("pE", 280, 288), ("vi", 0, 8), A.subtract)
 
     for w in "01":
         wf = ("wf", int(w), int(w) + 1)
@@ -365,65 +393,100 @@ def rank_program(g, core, T, topo):
         ts(("X", 0, 256), (("EL" + w, 0, 256), ("l1", 0, 16)), float(ROT), A.add, 2048.0, A.mult)
         turn(("XT", 0, 256), ("X", 0, 256))
         act(("E" + w, 0, 128), (("XT", 0, 256), ("l2", 0, 8)), AF.Copy)
-        act(("ZK" + w, ZH - 128, ZH), ("ZK" + w, ZH, NM), AF.Copy)
-        act(("ZK" + w, Z4, Z4 + 256), ("ZK" + w, ZH - 128, NM), AF.Copy)
+        for c in (0, Z4, Z4 + 128, Z4 + 256):
+            act(("ZK" + w, c, c + 128), ("ZK" + w, ZH, NM), AF.Copy)
         vmod(w)
         lists(w)
+
+    bank = [0]
+
+    def by_scalar(dall, lst, lo, hi, sub):
+        b = DB[bank[0] % len(DB)]
+        g0 = 512 * (bank[0] % 4)
+        bank[0] += 1
+        act(("DG", g0, g0 + 128 * (hi - lo)), (dall, lst), AF.Copy)
+        for k in range(hi - lo):
+            mm((b, 128 * k, 128 * k + 128), ("NI", sub), ("ID", ("DG", g0 + 128 * k, g0 + 128 * k + 128)))
+        return (b, 0, 128 * (hi - lo))
 
     def main(n):
         w = str(n % 2)
         zk, e, dall = "ZK" + w, "E" + w, ("D" + w, 0, 2048)
-        for lo, hi in GA:
-            tt(("DF", 128 * lo, 128 * hi), (dall, ("off" + w, 8 * lo, 8 * hi)), (zk, Z4, Z4 + 128 * (hi - lo)), A.subtract)
-            act((zk, 128 * lo, 128 * hi), ("DF", 128 * lo, 128 * hi), AF.Abs)
-            act(("SG", 128 * lo, 128 * hi), ("DF", 128 * lo, 128 * hi), AF.Sign, -0.5)
-        for lo, hi, top in ((64, 128, 256), (0, 64, 64)):
-            usum("pU", lo, hi, w, 16 * lo, 16 * hi)
-            ts(("Ui", lo, hi), ("pU", lo, hi), FLOOR, A.add)
-            tt(("Ub", lo, hi), ("pU", lo, hi), ("Ui", lo, hi), A.subtract)
-            if lo:
+        for lo, hi, q in GA:
+            lst = ("off" + w, 8 * lo, 8 * hi)
+            if q == "v":
+                df = ("DF", 128 * lo, 128 * hi)
+                tt(df, (dall, lst), (zk, NM - 128 * (hi - lo), NM), A.subtract)
+            else:
+                df = by_scalar(dall, lst, lo, hi, (zk, ZH, NM))
+            act((zk, QB + 128 * lo, QB + 128 * hi), df, AF.Abs)
+            if lo < SV:
+                ts(("SG", 128 * lo, 128 * hi), df, 0.0, A.is_gt, -0.5, A.add)
+            else:
+                act(("SG", 128 * lo, 128 * hi), df, AF.Sign, -0.5)
+        dmas("y", "rx%d" % n, [(T[zk][:, c:c + 128], T[zk][:, X0:X0 + 128]) for c in range(128, QB, 128)], [(zk, X0, X0 + 128)], [(zk, 128, QB)])
+        for lo, hi, top in (((120, 128, 256), (64, 120, 128), (0, 64, 64)) if D15 else ((64, 128, 256), (0, 64, 64))):
+            pu = (UB[lo], lo + 256, hi + 256)
+            usum(pu[0], pu[1], pu[2], w, QB + 16 * lo, QB + 16 * hi)
+            ts(("Ui", lo, hi), pu, FLOOR, A.add)
+            tt(("Ub", lo, hi), pu, ("Ui", lo, hi), A.subtract)
+            if top == 256:
                 tt(("PB", 128, 256), (("Ub", 120, 128), ("cl", 0, 8)), (e, 0, 128), A.mult)
-            tt(("PB", lo, hi), ((e, 120, 128), ("cl", 0, 4)), ("Ub", lo, hi), A.mult)
+            if lo == 120:
+                lo = 128
+            else:
+                tt(("PB", lo, lo + 64), ((e, 120, 128), ("cl", 0, 4)), ("Ub", lo, lo + 64), A.mult)
             ts(("NB", lo, top), ("PB", lo, top), 5, A.logical_shift_right, 2047, A.bitwise_and)
             cp(("offb", lo, top), ("NB", lo, top))
-        fold(("pac", 64, 128), "Fq", "SG", 1024, 2048)
+        fold(("pac", 64, 128), "Fh" if SV > 8 else "Fq", "SG", 1024, 2048)
         ts(("naf", 0, 8), ("pac", 120, 128), ("tau", 0, 1), A.is_lt, 8.0, A.mult)
         act(("nab", 0, 64), (("naf", 0, 8), ("cl", 0, 4)), AF.Copy)
-        fold(("pac", 0, 64), "Fq", "SG", 0, 1024)
+        fold(("pac", 0, 64), "Fh" if SV else "Fq", "SG", 0, 1024)
+        act(("fa", 0, 120), ("pac", 0, 120), AF.Relu, ("tau", 0, 1), -1.0)
         for lo, hi in GB:
-            tt(("BB", 128 * lo, 128 * hi), (dall, ("offb", 8 * lo, 8 * hi)), (zk, 128 * lo, 128 * hi), A.is_gt)
+            tt(("BB", 128 * lo, 128 * hi), (dall, ("offb", 8 * lo, 8 * hi)), (zk, QB + 128 * lo, QB + 128 * hi), A.is_gt)
         for lo, hi in ((8, 15), (0, 8)):
             k = 8 * (hi - lo)
             fold(("pb", 8 * lo, 8 * hi), "Fh", "BB", 128 * lo, 128 * hi, ("C4", ("ON", 0, k)), ("N2", ("nab", 0, k)))
-        for i in range(4):
-            lo, hi, bank = 4 * i, min(4 * i + 4, 15), "d%d" % (i % 2)
-            act(("DG", 128 * lo, 128 * hi), (dall, ("offb", 128 + 8 * lo, 128 + 8 * hi)), AF.Copy)
-            for q in range(lo, hi):
-                mm((bank, 128 * (q - lo), 128 * (q - lo + 1)), ("NI", (zk, 1920, 2048)), ("ID", ("DG", 128 * q, 128 * q + 128)))
-            act(("CC", 128 * lo, 128 * hi), (bank, 0, 128 * (hi - lo)), AF.Sign, -0.5)
-        for lo, hi in ((0, 8), (8, 15)):
-            fold(("pac", 128 + 8 * lo, 128 + 8 * hi), "Fq", "CC", 128 * lo, 128 * hi, ("ID", ("nab", 0, 8 * (hi - lo))))
+        for lo, hi, q in GC:
+            lst = ("offb", 128 + 8 * lo, 128 + 8 * hi)
+            if q == "v":
+                tt(("CC", 128 * lo, 128 * hi), (dall, lst), (zk, 128, 128 + 128 * (hi - lo)), A.is_gt)
+            else:
+                act(("CC", 128 * lo, 128 * hi), by_scalar(dall, lst, lo, hi, (zk, X0, X0 + 128)), AF.Sign, -0.5)
+        for lo, hi in CF:
+            k = 8 * (hi - lo)
+            v = [q for a, b, q in GC if lo <= a < hi][0] == "v"
+            fold(("pac", 128 + 8 * lo, 128 + 8 * hi), "FC" if v else "FB", "CC", 128 * lo, 128 * hi, ("IP", ("nab", 0, k)),
+                 ("IB", ("Tt", 64 * v, 64 * v + k)))
 
     def choice(n):
         w = str(n % 2)
         zk = "ZK" + w
-        mm(("px", 120, 128), ("ID", ("K1", 120, 128)), ("ID", ("K2", 120, 128)), ("CK", ("ON", 0, 8)), ("I16", ("naf", 0, 8)))
-        mm(("px", 0, 120), ("ID", ("K1", 0, 120)), ("ID", ("K2", 0, 120)), ("CK", ("ON", 0, 120)), last=False)
+        pall = ("px", 0, 128)
+        mm(("px", 120, 128), ("ID", ("K1", 120, 128)), ("ID", ("K2", 120, 128)), ("CK", ("ON", 0, 8)), ("I16", ("naf", 0, 8)), keep=pall)
+        mm(("px", 0, 120), ("ID", ("K1", 0, 120)), ("ID", ("K2", 0, 120)), ("CK", ("ON", 0, 120)), last=False, keep=pall)
         act(("hb", 0, 120), ("pb", 0, 120), AF.Abs, ("tau", 0, 1), -1.0)
         act(("fb", 0, 120), ("hb", 0, 120), AF.Relu, -8.0)
-        act(("fac", 0, 248), ("pac", 0, 248), AF.Relu, ("tau", 0, 1), -1.0)
-        mm(("px", 0, 120), ("IB", ("fb", 0, 120)), ("IB", ("fac", 0, 120)), ("IB", ("fac", 128, 248)), first=False)
-        tt(("x", 0, 128), ("px", 0, 128), ("N" + w, 0, 128), A.add)
-        tt(("m", 0, 64), ("x", 0, 64), ("x", 64, 128), A.max)
-        tt(("m", 64, 96), ("m", 0, 32), ("m", 32, 64), A.max)
-        tt(("m", 96, 112), ("m", 64, 80), ("m", 80, 96), A.max)
-        tt(("Ci", 0, 8), ("m", 96, 104), ("m", 104, 112), A.max)
-        ts(("Oj", 0, 8), ("Ci", 0, 8), 12, A.logical_shift_right, 4095, A.bitwise_and)
-        cp(("ou", 0, 8), ("Oj", 0, 8))
+        mm(("px", 0, 120), ("IB", ("fb", 0, 120)), ("IB", ("fa", 0, 120)), first=False, keep=pall)
+        tt(("x", 0, 128), pall, ("N" + w, 0, 128), A.add)
+        tt(("x", 0, 120), ("pac", 128, 248), ("x", 0, 120), A.min)
+        if RED:
+            for j in range(8):
+                op("v", lambda e, j=j: e.tensor_reduce(T["code"][:, j:j + 1], T.x[:, j:128:8], AxisListType.X, A.max), [("x", 0, 128)],
+                   [("code", j, j + 1)], MINC * CYC)
+        else:
+            tt(("m", 0, 64), ("x", 0, 64), ("x", 64, 128), A.max)
+            tt(("m", 64, 96), ("m", 0, 32), ("m", 32, 64), A.max)
+            tt(("m", 96, 112), ("m", 64, 80), ("m", 80, 96), A.max)
+            tt(("code", 0, 8), ("m", 96, 104), ("m", 104, 112), A.max)
+        ts(("ou", 0, 8), ("code", 0, 8), 1.0 / 4096, A.mult, -864.0 / 4096, A.add)
+        ts(("Ci", 0, 8), ("code", 0, 8), -5.0 * 524288, A.add)
         ts(("LH", 0, 8), ("Ci", 0, 8), 7, A.bitwise_and)
         ts(("LH", 8, 16), ("Ci", 0, 8), 3, A.logical_shift_right, 255, A.bitwise_and)
         cp((zk, NM, NM + 16), ("LH", 0, 16))
-        act((zk, ZH, NM), ((zk, 0, Z4 + 128), ("ou", 0, 8)), AF.Copy)
+        act((zk, ZH, NM), ((zk, 0, X0), ("ou", 0, 8)), AF.Copy)
+        ts(("Oj", 0, 8), ("Ci", 0, 8), 12, A.logical_shift_right, 4095, A.bitwise_and)
 
     def send(n):
         w, t = str(n % 2), n // 2
@@ -454,24 +517,36 @@ def rank_program(g, core, T, topo):
         if t == RO - 1:
             dmas("y", "yz_" + w, [(b, a) for a, b in placed(T[zk], ZH, T.yz, w)], [(zk, ZH, NM)], [])
             return
-        dmas("y", "rep%d" % n, [(T[zk][:, c:c + 128], T[zk][:, ZH:NM]) for c in range(Z4, ZH, 128)], [(zk, ZH, NM)], [(zk, Z4, ZH)])
+        dmas("y", "rep%d" % n, [(T[zk][:, c:c + 128], T[zk][:, ZH:NM]) for c in (0, Z4, Z4 + 128, Z4 + 256)], [(zk, ZH, NM)],
+             [(zk, 0, 128), (zk, Z4, ZH)])
         act(("fl", 0, 8), ("keep", 120, 128), AF.Copy, accum=("acc", n % 2, n % 2 + 1))
         if n % 2:
-            mm(("pu", 16, 17), *[("QF", ("acc", k, k + 1)) for k in range(3)])
-            cp(("ri", 0, 1), ("pu", 16, 17))
-            tt(("tau", 0, 1), ("pu", 16, 17), ("ri", 0, 1), A.subtract)
+            mm(("pE", 296, 297), *[("QF", ("acc", k, k + 1)) for k in range(3)])
+            cp(("ri", 0, 1), ("pE", 296, 297))
+            tt(("tau", 0, 1), ("pE", 296, 297), ("ri", 0, 1), A.subtract)
+            if "s" in [q for a, b, q in GC]:
+                act(("Tt", 0, 64), ("ON", 0, 64), AF.Copy, None, ("tau", 0, 1))
+            if "v" in [q for a, b, q in GC]:
+                act(("Tt", 64, 128), ("ON", 0, 64), AF.Identity, 4.0, ("tau", 0, 1))
         vmod(w)
 
     def arrival(n):
         w, lc = str(n % 2), "L%d" % n
         d, dall = T["D" + w], ("D" + w, 0, 2048)
         both = n in BOTH
-        mm(("pE", 256, 264), ("ID", (lc, 128, 136)), ("ID", ("cb", 0, 8)))
+        if CV:
+            tt(("ci", 0, 8), (lc, 128, 136), ("cb", 0, 8), A.add)
+            cp(("cu", 0, 8), ("ci", 0, 8))
+        else:
+            mm(("pE", 256, 264), ("ID", (lc, 128, 136)), ("ID", ("cb", 0, 8)))
         if both:
             mm(("pE", 264, 272), ("SW", (lc, 128, 136)), ("SW", ("cb", 0, 8)))
         mm(("pE", 0, 8), ("I11", (lc, 128, 136)), ("I14", (lc, 136, 144)), ("CE", ("ON", 0, 8)))
         k = 16 if both else 8
-        cp(("cu", 0, k), ("pE", 256, 256 + k))
+        if not CV:
+            cp(("cu", 0, k), ("pE", 256, 256 + k))
+        elif both:
+            cp(("cu", 8, 16), ("pE", 264, 272))
         tt(("E" + w, 0, 128), ("pE", 0, 128), ("kd" + w, 0, 128), A.add)
         tt(("su", 0, 128), (dall, ("cu", 0, 8)), (lc, 0, 128), A.add)
         ts(("sh", 0, 128), ("su", 0, 128), 0.5, A.mult, -0.25, A.add)
@@ -487,7 +562,7 @@ def rank_program(g, core, T, topo):
             return
         r = slice(64 * int(w), 64 * int(w) + 64)
         dmas("y", "yd_" + w, [(T.yd[r, 2048 - ROT:3072 - ROT], d[0:64, 0:1024]), (T.yd[r, 0:2048 - ROT], d[64:128, ROT:2048]),
-                              (T.yd[r, 3072 - ROT:2048], d[64:128, 1024:ROT])], [dall], [])
+                              (T.yd[r, 3072 - ROT:2048], d[64:128, 1024:ROT])], [dall], [], XC)
         act(("X", 0, 256), (("E" + w, 0, 128), ("l3", 0, 16)), AF.Copy)
         turn(("XT", 0, 256), ("X", 0, 256))
         act(("YL" + w, 0, 128), (("XT", 0, 256), ("l4", 0, 8)), AF.Identity, -float(ROT), 1.0 / 2048)

@@ -4,25 +4,23 @@ from concourse.mybir import ActivationFunctionType as AF
 from concourse.mybir import AxisListType
 
 RO = 5
-NENG = 8
 PAY = 144
 BIG = 2.0 ** 28
 FLOOR = -1055.5 / 2048
 ROT = 1184
 JR = 256 - ROT // 8
-QB, X0, Z4, ZH, NM = 640, 2560, 2688, 3072, 3200
-CYC, PEC, GATHER, SCATTER, MINC = 0.83, 0.42, 1.3, 3.4, 70
-WAKE, DMA, HOP, XC = 260.0, 1500.0, 1700.0, 2100.0
-PASSES, SHAKE, ORDERS = 30, 300.0, {}
-D15, SV, CV, RED = 0, 0, 0, 1
-BOTH = ()
+ZH, W0, QB, X0 = 16, 400, 656, 2576
+CYC, PEC, GATHER, SCATTER, MINC, FIX = 0.83, 0.47, 1.15, 3.4, 64, 35
+WAKE, DMA, HOP, XC = 250.0, 1500.0, 1600.0, 2200.0
+PASSES, ORDERS = 1300, {}
 LATE = (0, 0, 0, 0.5, 0.5)
-GA = [(12, 16, "v"), (8, 12, "v"), (4, 8, "v"), (0, 4, "v")]
-GB = [(8, 12), (12, 15), (0, 4), (4, 8)]
-GC = [(0, 4, "s"), (4, 8, "s"), (8, 12, "s"), (12, 15, "s")]
-CF = [(0, 8), (8, 15)]
+GA = [(12, 16, "v"), (8, 12, "v"), (4, 8, "v"), (2, 4, "v"), (0, 2, "s")]
+AB = [(12, 16), (8, 12), (4, 8), (2, 4)]
+SGP = [(8, 16), (2, 8)]
+GB = [(8, 15), (0, 4), (4, 8)]
+GC = [(0, 4), (4, 8), (8, 12), (12, 15)]
+VC = (8, 9)
 DB = ["d0", "d1", "d2"]
-UB = {120: "pU", 64: "pU", 0: "pb"}
 
 
 def _s(n, dt):
@@ -31,24 +29,24 @@ def _s(n, dt):
 
 SCRATCH = {}
 for _w in "01":
-    for _n, _c, _d in (("D", 2048, "bfloat16"), ("ZK", 3216, "bfloat16"), ("Fw", 144, "bfloat16"), ("E", 128, "float32"),
-                       ("v", 8, "float32"), ("kd", 128, "float32"), ("N", 128, "int32"), ("EL", 256, "int32"), ("wti", 1, "int32"),
-                       ("off", 128, "uint16"), ("YL", 128, "float32")):
+    for _n, _c, _d in (("D", 2048, "bfloat16"), ("ZK", 2704, "bfloat16"), ("Fw", 144, "bfloat16"), ("E", 128, "float32"),
+                       ("v", 8, "float32"), ("kd", 128, "float32"), ("N", 128, "int32"), ("EL", 128, "int32"), ("wti", 1, "int32"),
+                       ("off", 128, "uint16"), ("YL", 128, "float32"), ("ZN", 128, "bfloat16")):
         SCRATCH[_n + _w] = _s(_c, _d)
 for _n, _w in (("DF", 2048), ("SG", 2048), ("CC", 1920), ("BB", 1920), ("DG", 2048), ("fa", 120), ("hb", 120), ("fb", 120),
-               ("naf", 16), ("nab", 64), ("fl", 8), ("cb", 8), ("K1", 128), ("K2", 128),
-               ("O8", 8), ("B8a", 8), ("B8", 8), ("F", 144), ("Fh", 144), ("Fq", 144), ("FB", 144), ("FC", 144), ("Tt", 128),
-               ("ON", 128), ("ID", 128), ("NI", 128), ("N2", 128), ("IB", 128), ("IP", 128), ("I11", 128), ("I14", 128), ("I16", 128),
-               ("C32", 128), ("C4", 128), ("CK", 128), ("CE", 128), ("SW", 128)):
+               ("naf", 16), ("nab", 64), ("fl", 8), ("CE", 8), ("K1", 128), ("K2", 128),
+               ("O8", 8), ("B8a", 8), ("B8", 8), ("F", 144), ("Fh", 144), ("Fq", 144), ("FB", 144), ("FC", 144), ("CB", 128), ("Tt", 128),
+               ("ON", 128), ("ID", 128), ("NI", 128), ("N8", 128), ("IB", 128), ("IP", 128), ("I11", 128), ("I14", 128), ("I18", 128),
+               ("C32", 128), ("CK", 128)):
     SCRATCH[_n] = _s(_w, "bfloat16")
-for _n, _w in (("Ub", 128), ("x", 128), ("m", 112), ("code", 8), ("keep", 128), ("acc", 3), ("tau", 1),
-               ("X", 256), ("XT", 256), ("wf", 2), ("IF", 128), ("JF", 128), ("QF", 128), ("pmf", 1), ("TH", 128), ("su", 128), ("SF", 128)):
+for _n, _w in (("Ub", 128), ("x", 128), ("keep", 128), ("acc", 3), ("tau", 1), ("X", 256), ("XT", 256), ("wf", 2),
+               ("cb", 1), ("J8", 16), ("IF", 128), ("JF", 128), ("QF", 128), ("pmf", 1), ("TH", 128), ("su", 128)):
     SCRATCH[_n] = _s(_w, "float32")
-for _n, _w in (("P", 128), ("PB", 256), ("NB", 256), ("Ui", 128), ("vi", 8), ("Ci", 8), ("Oj", 8), ("LH", 16), ("ri", 1), ("ci", 8),
-               ("sh", 256), ("ip", 16), ("pm", 16), ("t", 160),
-               ("i1", 16), ("i2", 8), ("i3", 16), ("i4", 8), ("i5", 8), ("i6", 128), ("i7", 128)):
+for _n, _w in (("P", 128), ("PB", 256), ("NB", 256), ("Ui", 128), ("vi", 8), ("Ci", 8), ("Oj", 8), ("LH", 16), ("ri", 1),
+               ("sh", 128), ("ip", 16), ("pm", 16), ("t", 160),
+               ("i1", 16), ("i2", 8), ("i3", 16), ("i4", 8), ("i5", 8), ("i6", 128), ("i7", 128), ("i8", 8)):
     SCRATCH[_n] = _s(_w, "int32")
-for _n, _w in (("offb", 256), ("ou", 8), ("cu", 16), ("cl", 8), ("l1", 16), ("l2", 8), ("l3", 16), ("l4", 8)):
+for _n, _w in (("offb", 256), ("ou", 8), ("cu", 8), ("cl", 8), ("l1", 16), ("l2", 8), ("l3", 16), ("l4", 8), ("l5", 8), ("l6", 8)):
     SCRATCH[_n] = _s(_w, "uint16")
 PSUM = ["pU", "pac", "pb", "px", "pE", "d0", "d1", "d2"]
 for _n in PSUM:
@@ -57,7 +55,7 @@ STEPS = 2 * RO
 for _t in range(STEPS):
     SCRATCH["L%d" % _t] = _s(PAY, "bfloat16")
 SEMAPHORES = (["qv", "qs", "qp", "qg"] + [k + w for k in ("wt", "zv", "ef", "dv", "yd", "ye", "yz") for w in ("_0", "_1")] +
-              [k + str(t) for k in ("arr", "rl", "loc", "rep", "rx", "xc") for t in range(STEPS)])
+              [k + str(t) for k in ("arr", "rl", "loc", "xc", "rep") for t in range(STEPS)])
 
 
 def target(cores, rank, t):
@@ -73,8 +71,7 @@ def route(topo, src, dst):
 
 
 def engines(topo, src, dst):
-    e = topo.engines(src, dst)[:NENG]
-    return sum(1 << k for k in e), len(e)
+    return topo.mask(src, dst), len(topo.engines(src, dst))
 
 
 def relay_program(g, core, T, topo):
@@ -101,7 +98,8 @@ def in_order(calls, stage):
     busy = [c[3] for c in calls]
     fwd = [dict() for _ in range(n)]
     seen = {}
-    for i, (q, reads, writes, _, done, issue) in enumerate(calls):
+    begin = [c[6] if len(c) > 6 else 0.0 for c in calls]
+    for i, (q, reads, writes) in enumerate(c[:3] for c in calls):
         for regs, wr in ((reads, False), (writes, True)):
             for b, lo, hi in regs:
                 for l2, h2, w2, j in seen.get(b, []):
@@ -151,23 +149,32 @@ def in_order(calls, stage):
                     ready.append(j)
         return at
 
+    def span(at):
+        return max(at[i] + calls[i][4] for i in range(n))
+
+    seed = [1]
+
+    def rnd():
+        seed[0] = (seed[0] * 1103515245 + 12345) % 2147483648
+        return seed[0] / 2147483648
+
     way = [0.0] * n
     for i in range(n - 1, -1, -1):
         way[i] = max([calls[i][4]] + [way[k] + fwd[k][i] for k in bwd[i]])
-    at = place(fwd, bwd, [0.0] * n, [(stage[i], -way[i], i) for i in range(n)])
-    best, seed = None, 1
+    at = place(fwd, bwd, begin, [(stage[i], -way[i], i) for i in range(n)])
+    kind = [(c[0], c[2][0][0].rstrip("0123456789"), c[2][0][1]) if c[2] else (c[0], "", 0) for c in calls]
+    best = (span(at), at)
     for p in range(PASSES):
-        end = max(at[i] + calls[i][4] for i in range(n))
-        if best is None or end < best[0]:
-            best = (end, at)
-        elif p % 3 == 0:
-            at = best[1]
-        shake = []
-        for i in range(n):
-            seed = (seed * 1103515245 + 12345) % 2147483648
-            shake.append(SHAKE * seed / 2147483648 if p % 3 == 0 and p else 0.0)
-        back = place(bwd, fwd, [c[4] - c[3] for c in calls], [(-at[i] - busy[i] + shake[i], -i) for i in range(n)])
-        at = place(fwd, bwd, [0.0] * n, [(-back[i] - busy[i], i) for i in range(n)])
+        if p % 2 == 0:
+            c, sh = rnd() * best[0], 1500 * rnd() if p > 2 else 0.0
+            d = [sh * rnd() if abs(best[1][i] - c) < 3000 else sh / 2 for i in range(n)]
+        else:
+            m = {k: (rnd() - 0.5) * 2000 if rnd() < 0.1 and p > 2 else 0.0 for k in sorted(set(kind))}
+            d = [m[k] for k in kind]
+        back = place(bwd, fwd, [c[4] - c[3] for c in calls], [(-best[1][i] - busy[i] + d[i], -i) for i in range(n)])
+        at = place(fwd, bwd, begin, [(-back[i] - busy[i], i) for i in range(n)])
+        if span(at) <= best[0]:
+            best = (span(at), at)
     ORDERS[sign] = sorted(range(n), key=lambda i: (best[1][i], i))
     return [calls[i] for i in ORDERS[sign]]
 
@@ -189,13 +196,13 @@ def rank_program(g, core, T, topo):
             return (s, total[s])
         calls.append((q, reads, writes, ns, ns, issue))
 
-    def dmas(q, s, pairs, reads, writes, ns=None):
+    def dmas(q, s, pairs, reads, writes, ns=None, first=0.0):
         def issue(total):
             for out, in_ in pairs:
                 eng[q].dma_start(out, in_).then_inc(T.sem[s], 16)
             total[s] = 16 * len(pairs)
             return (s, total[s])
-        calls.append((q, reads, writes, 60.0 * len(pairs), ns or DMA, issue))
+        calls.append((q, reads, writes, 60.0 * len(pairs), ns or DMA, issue, first))
 
     def ap(v):
         return T[v[0]][:, v[1]:v[2]] if len(v) == 3 else T[v[0]][:, v[1]:v[2]:v[3]]
@@ -212,7 +219,7 @@ def rank_program(g, core, T, topo):
         if isinstance(out[0], tuple):
             return 50 + (a[2] - a[1]) * SCATTER * CYC
         n = len(range(*out[1:]))
-        return 50 + n * GATHER * CYC if isinstance(a[0], tuple) else max(MINC, n * per) * CYC
+        return 50 + n * GATHER * CYC if isinstance(a[0], tuple) else max(MINC, n * per) * CYC + FIX
 
     def narrow(*vs):
         return 0.5 if all(SCRATCH[v[0]][2] in ("bfloat16", "uint16") for v in vs if not isinstance(v[0], tuple)) else 1
@@ -283,8 +290,8 @@ def rank_program(g, core, T, topo):
         op("p", fn, [(fm, 0, 144), (src, lo, hi)] + [(l, 0, 128) for l, r in extra] + [rg(r) for l, r in extra], [rg(out)],
            pns(out, [(fm, 0)] * 16 + list(extra)))
 
-    def usum(bank, lo, hi, w, slo, shi):
-        fold((bank, lo, hi), "Fw" + w, "ZK" + w, slo, shi, ("C32", ("ON", 0, hi - lo)))
+    def usum(out, w, lo, hi):
+        fold(out, "Fw" + w, "ZK" + w, lo, hi, ("C32", ("ON", 0, out[2] - out[1])))
 
     def turn(out, a):
         op("v", lambda e: e.transpose(ap(out), ap(a)), [rg(a)], [rg(out)], ns(out, a, 1))
@@ -297,50 +304,47 @@ def rank_program(g, core, T, topo):
         n = SCRATCH[out][1][1]
         op("g", lambda e: e.affine_select(T[out][:, :], T[a][:, :], *args), [(a, 0, n)], [(out, 0, n)], 170 + 2 * n * CYC)
 
-    def placed(sb, c0, hbm, w):
+    def placed(sb, hbm, w):
         r = slice(64 * int(w), 64 * int(w) + 64)
         b = 128 - JR
-        return [(sb[0:64, c0:c0 + 128], hbm[r, JR:JR + 128]), (sb[64:128, c0:c0 + b], hbm[r, JR + 128:256]),
-                (sb[64:128, c0 + b:c0 + 128], hbm[r, 0:JR])]
+        return [(sb[0:64, 0:128], hbm[r, JR:JR + 128]), (sb[64:128, 0:b], hbm[r, JR + 128:256]), (sb[64:128, b:128], hbm[r, 0:JR])]
 
     for w in "01":
         r = slice(64 * int(w), 64 * int(w) + 64)
         hs = (slice(0, 64), slice(64, 128))
-        dmas("s", "ef_" + w, [(T["EL" + w][h, :], T.ef[r, :]) for h in hs], [], [("EL" + w, 0, 256)])
-        dmas("y", "wt_" + w, [(T["wti" + w][h, :], T.wt[r, :]) for h in hs], [], [("wti" + w, 0, 1)])
-        dmas("y", "zv_" + w, placed(T["ZK" + w], ZH, T.zv, w), [], [("ZK" + w, ZH, NM)])
-        dmas("s" if w == "0" else "y", "dv_" + w,
+        after = [("D0", 0, 1)] if w == "1" else []
+        dmas("s" if w == "0" else "y", "ef_" + w, placed(T["EL" + w], T.ef, w), after, [("EL" + w, 0, 128)])
+        dmas("y", "wt_" + w, [(T["wti" + w][h, :], T.wt[r, :]) for h in hs], after, [("wti" + w, 0, 1)])
+        dmas("y", "zv_" + w, placed(T["ZN" + w], T.zv, w), after, [("ZN" + w, 0, 128)])
+        dmas("y", "dv_" + w,
              [(T["D" + w][h, ROT:2048], T.dv[r, 0:2048 - ROT]) for h in hs] + [(T["D" + w][h, 0:ROT], T.dv[r, 2048 - ROT:2048]) for h in hs],
-             [], [("D" + w, 0, 2048)], XC)
+             after, [("D" + w, 0, 2048)], XC + 900, 400.0)
 
     fill(("O8", 0, 8), 1.0)
     fill(("F", 0, 144), 0.0)
     fill(("ON", 0, 128), 1.0)
     iota("ip", [[0, 16]], 0, 1)
-    iota("i1", [[16, 8], [0, 2]], JR, 0)
+    iota("i1", [[1, 8], [0, 2]], 0, 8)
     iota("i2", [[-2, 8]], 15, 32)
     iota("i3", [[1, 8], [0, 2]], 1144, -8)
-    iota("i4", [[32, 8]], 0, 0)
-    iota("i5", [[16, 8]], 0, 0)
+    iota("i4", [[2, 8]], 0, 32)
+    iota("i5", [[8, 8]], 0, 0)
     iota("i6", [[1, 16], [0, 8]], 0, 0)
     iota("i7", [[0, 16], [16, 8]], 0, 0)
+    iota("i8", [[1, 8]], 0, 8)
     select("B8a", "O8", [[-16, 8]], A.is_ge, 0.0, 0, 1)
     select("B8", "B8a", [[16, 8]], A.is_ge, 0.0, 15, -1)
     select("ID", "ON", [[-1, 128]], A.is_equal, 0.0, 0, 1)
     cp(("F", 15, 128, 16), ("B8", 0, 8))
     for name, c in (("Fq", 0.25), ("Fh", 0.5), ("FB", 0.25 * BIG), ("FC", 0.5 * BIG)):
         ts((name, 0, 144), ("F", 0, 144), c, A.mult)
-    for name, c in (("NI", -1.0), ("N2", -2.0), ("IB", -BIG), ("IP", BIG), ("I16", -65536.0), ("I11", 2048.0), ("I14", 16384.0),
+    for name, c in (("NI", -1.0), ("N8", -8.0), ("IB", -BIG), ("IP", 4 * BIG), ("I18", -262144.0), ("I11", 2048.0), ("I14", 16384.0),
                     ("IF", 1.0), ("JF", -1.0)):
         ts((name, 0, 128), ("ID", 0, 128), c, A.mult)
-    for name, c in (("C32", 1.0 / 8192), ("C4", 4.0 / 128), ("CK", 864.0 / 128), ("CE", 2048.0 * ROT / 128), ("QF", 0.5)):
+    for name, c in (("C32", 1.0 / 8192), ("CK", 864.0 / 128), ("QF", 0.5), ("CB", -4 * BIG / 128)):
         fill((name, 0, 128), c)
-    if BOTH:
-        for name in ("SW", "SF"):
-            cp((name, 0, 64), ("ID", 64, 128))
-            cp((name, 64, 128), ("ID", 0, 64))
     fill(("tau", 0, 1), -0.25)
-    fill(("Tt", 0, 64), -0.25)
+    fill(("Tt", 0, 64), -4.25)
     fill(("Tt", 64, 128), 3.75)
     fill(("acc", 2, 3), -0.5 / 128)
     fill(("kd0", 0, 8), 0.0)
@@ -353,10 +357,13 @@ def rank_program(g, core, T, topo):
     cp(("pmf", 0, 1), ("pm", 0, 1))
     ts(t8(0), ("ip", 0, 8), 7, A.bitwise_and)
     cp(("cl", 0, 8), t8(0))
-    ts(t8(1, 16), ("ip", 0, 16), 64, A.bitwise_and)
-    ts(t8(3, 16), t8(1, 16), 2.0, A.mult, ("pmf", 0, 1), A.add)
-    tt(t8(5, 16), t8(3, 16), ("i1", 0, 16), A.add)
-    ts(t8(7, 16), t8(5, 16), 255, A.bitwise_and)
+    ts(t8(1), ("ip", 0, 8), 64, A.bitwise_and)
+    ts(t8(2), ("pm", 0, 8), 4.0, A.mult)
+    tt(t8(3), t8(1), t8(2), A.add)
+    ts(("cb", 0, 1), t8(3, 1), 16.0, A.mult)
+    ts(t8(4), ("i8", 0, 8), 127, A.bitwise_and)
+    cp(("l5", 0, 8), t8(4))
+    ts(t8(7, 16), ("i1", 0, 16), 127, A.bitwise_and)
     cp(("l1", 0, 16), t8(7, 16))
     ts(t8(9), ("ip", 0, 8), 3, A.logical_shift_right, 1, A.bitwise_and)
     ts(t8(10), ("ip", 0, 8), 16, A.bitwise_and)
@@ -366,14 +373,19 @@ def rank_program(g, core, T, topo):
     cp(("l2", 0, 8), t8(13))
     ts(t8(14, 16), ("i3", 0, 16), 127, A.bitwise_and)
     cp(("l3", 0, 16), t8(14, 16))
-    ts(t8(16), ("ip", 0, 8), 31, A.bitwise_and)
-    tt(t8(17), t8(16), ("i4", 0, 8), A.add)
-    cp(("l4", 0, 8), t8(17))
-    tt(t8(18), t8(3), ("i5", 0, 8), A.add)
-    ts(("cb", 0, 8), t8(18), 8.0, A.mult)
+    ts(t8(16), ("i4", 0, 8), 255, A.bitwise_and)
+    tt(t8(17), t8(16), t8(9), A.add)
+    tt(t8(18), t8(17), t8(10), A.add)
+    cp(("l4", 0, 8), t8(18))
+    ts(t8(5), t8(0), -16.0, A.mult)
+    tt(t8(6), t8(17), t8(5), A.add)
+    cp(("l6", 0, 8), t8(6))
+    cp(("J8", 0, 8), ("i5", 0, 8))
+    fill(("J8", 8, 16), 0.0)
+    ts(("CE", 0, 8), ("i5", 0, 8), -float(ROT), A.add, -2048.0, A.mult)
     ts(("TH", 0, 128), ("i6", 0, 128), 128.0, A.mult)
-    ts(("K1", 0, 120), ("i6", 0, 120), 5.0, A.add, 524288.0, A.mult)
-    fill(("K1", 120, 128), 524288.0)
+    ts(("K1", 0, 120), ("i6", 0, 120), 524288.0, A.mult)
+    fill(("K1", 120, 128), -3 * 262144.0)
     ts(("K2", 0, 128), ("i7", 0, 128), ("pmf", 0, 1), A.add, 4096.0, A.mult)
 
     def lists(w):
@@ -381,21 +393,33 @@ def rank_program(g, core, T, topo):
         ts(("N" + w, 0, 128), ("P", 0, 128), 5, A.logical_shift_right, 2047, A.bitwise_and)
         cp(("off" + w, 0, 128), ("N" + w, 0, 128))
 
-    def vmod(w):
-        usum("pE", 280, 288, w, ZH, NM)
+    def vmod(w, first=False):
+        if first:
+            def fn(e):
+                e.matmul(T.pE[:, 280:288], T.C32[:, :], T.ON[:, 0:8], True, False)
+                for jl in range(16):
+                    r = e.matmul(T.pE[:, 280:288], T["Fw" + w][:, 15 - jl:143 - jl], T["ZN" + w][:, 8 * jl:8 * jl + 8], False, jl == 15)
+                return r
+            op("p", fn, [("C32", 0, 128), ("ON", 0, 8), ("Fw" + w, 0, 144), ("ZN" + w, 0, 128)], [("pE", 280, 288)], 17 * 64 * PEC)
+        else:
+            usum(("pE", 280, 288), w, ZH, ZH + 128)
         ts(("vi", 0, 8), ("pE", 280, 288), FLOOR, A.add)
         tt(("v" + w, 0, 8), ("pE", 280, 288), ("vi", 0, 8), A.subtract)
+
+    def four(w):
+        act(("ZK" + w, ZH + 128, ZH + 256), ("ZK" + w, ZH, ZH + 128), AF.Copy)
+        act(("ZK" + w, ZH + 256, ZH + 512), ("ZK" + w, ZH, ZH + 256), AF.Copy)
 
     for w in "01":
         wf = ("wf", int(w), int(w) + 1)
         cp(wf, ("wti" + w, 0, 1))
         ts(("Fw" + w, 0, 144), ("F", 0, 144), wf, A.mult, 1.0 / 2048, A.mult)
-        ts(("X", 0, 256), (("EL" + w, 0, 256), ("l1", 0, 16)), float(ROT), A.add, 2048.0, A.mult)
+        ts(("X", 0, 256), (("EL" + w, 0, 128), ("l1", 0, 16)), float(ROT), A.add, 2048.0, A.mult)
         turn(("XT", 0, 256), ("X", 0, 256))
         act(("E" + w, 0, 128), (("XT", 0, 256), ("l2", 0, 8)), AF.Copy)
-        for c in (0, Z4, Z4 + 128, Z4 + 256):
-            act(("ZK" + w, c, c + 128), ("ZK" + w, ZH, NM), AF.Copy)
-        vmod(w)
+        act(("ZK" + w, ZH, ZH + 128), (("ZN" + w, 0, 128), ("l5", 0, 8)), AF.Copy)
+        four(w)
+        vmod(w, True)
         lists(w)
 
     bank = [0]
@@ -416,76 +440,66 @@ def rank_program(g, core, T, topo):
             lst = ("off" + w, 8 * lo, 8 * hi)
             if q == "v":
                 df = ("DF", 128 * lo, 128 * hi)
-                tt(df, (dall, lst), (zk, NM - 128 * (hi - lo), NM), A.subtract)
+                tt(df, (dall, lst), (zk, ZH, ZH + 128 * (hi - lo)), A.subtract)
             else:
-                df = by_scalar(dall, lst, lo, hi, (zk, ZH, NM))
-            act((zk, QB + 128 * lo, QB + 128 * hi), df, AF.Abs)
-            if lo < SV:
-                ts(("SG", 128 * lo, 128 * hi), df, 0.0, A.is_gt, -0.5, A.add)
-            else:
+                df = by_scalar(dall, lst, lo, hi, (zk, ZH, ZH + 128))
+            if q == "s":
+                act((zk, QB + 128 * lo, QB + 128 * hi), df, AF.Abs)
                 act(("SG", 128 * lo, 128 * hi), df, AF.Sign, -0.5)
-        dmas("y", "rx%d" % n, [(T[zk][:, c:c + 128], T[zk][:, X0:X0 + 128]) for c in range(128, QB, 128)], [(zk, X0, X0 + 128)], [(zk, 128, QB)])
-        for lo, hi, top in (((120, 128, 256), (64, 120, 128), (0, 64, 64)) if D15 else ((64, 128, 256), (0, 64, 64))):
-            pu = (UB[lo], lo + 256, hi + 256)
-            usum(pu[0], pu[1], pu[2], w, QB + 16 * lo, QB + 16 * hi)
-            ts(("Ui", lo, hi), pu, FLOOR, A.add)
-            tt(("Ub", lo, hi), pu, ("Ui", lo, hi), A.subtract)
-            if top == 256:
+        for lo, hi in AB:
+            act((zk, QB + 128 * lo, QB + 128 * hi), ("DF", 128 * lo, 128 * hi), AF.Abs)
+        for lo, hi in SGP:
+            act(("SG", 128 * lo, 128 * hi), ("DF", 128 * lo, 128 * hi), AF.Sign, -0.5)
+        act((zk, QB - 128, QB), ("DF", 1920, 2048), AF.Abs)
+        for lo, top, pu in ((64, 256, ("pU", 0, 64)), (0, 64, ("pb", 256, 320))):
+            usum(pu, w, QB + 16 * lo, QB + 16 * lo + 1024)
+            ts(("Ui", lo, lo + 64), pu, FLOOR, A.add)
+            tt(("Ub", lo, lo + 64), pu, ("Ui", lo, lo + 64), A.subtract)
+            if lo:
                 tt(("PB", 128, 256), (("Ub", 120, 128), ("cl", 0, 8)), (e, 0, 128), A.mult)
-            if lo == 120:
-                lo = 128
-            else:
-                tt(("PB", lo, lo + 64), ((e, 120, 128), ("cl", 0, 4)), ("Ub", lo, lo + 64), A.mult)
+            tt(("PB", lo, lo + 64), ((e, 120, 128), ("cl", 0, 4)), ("Ub", lo, lo + 64), A.mult)
             ts(("NB", lo, top), ("PB", lo, top), 5, A.logical_shift_right, 2047, A.bitwise_and)
             cp(("offb", lo, top), ("NB", lo, top))
-        fold(("pac", 64, 128), "Fh" if SV > 8 else "Fq", "SG", 1024, 2048)
-        ts(("naf", 0, 8), ("pac", 120, 128), ("tau", 0, 1), A.is_lt, 8.0, A.mult)
+        fold(("pac", 64, 128), "Fq", "SG", 1024, 2048)
+        act(("naf", 0, 8), ("pac", 120, 128), AF.Sign, ("tau", 0, 1), -1.0)
         act(("nab", 0, 64), (("naf", 0, 8), ("cl", 0, 4)), AF.Copy)
-        fold(("pac", 0, 64), "Fh" if SV else "Fq", "SG", 0, 1024)
+        fold(("pac", 0, 64), "Fq", "SG", 0, 1024)
         act(("fa", 0, 120), ("pac", 0, 120), AF.Relu, ("tau", 0, 1), -1.0)
         for lo, hi in GB:
             tt(("BB", 128 * lo, 128 * hi), (dall, ("offb", 8 * lo, 8 * hi)), (zk, QB + 128 * lo, QB + 128 * hi), A.is_gt)
         for lo, hi in ((8, 15), (0, 8)):
             k = 8 * (hi - lo)
-            fold(("pb", 8 * lo, 8 * hi), "Fh", "BB", 128 * lo, 128 * hi, ("C4", ("ON", 0, k)), ("N2", ("nab", 0, k)))
-        for lo, hi, q in GC:
-            lst = ("offb", 128 + 8 * lo, 128 + 8 * hi)
-            if q == "v":
-                tt(("CC", 128 * lo, 128 * hi), (dall, lst), (zk, 128, 128 + 128 * (hi - lo)), A.is_gt)
-            else:
-                act(("CC", 128 * lo, 128 * hi), by_scalar(dall, lst, lo, hi, (zk, X0, X0 + 128)), AF.Sign, -0.5)
-        for lo, hi in CF:
+            fold(("pb", 8 * lo, 8 * hi), "Fh", "BB", 128 * lo, 128 * hi, ("NI", ("Tt", 64, 64 + k)), ("N8", ("nab", 0, k)))
+        vc = 8 if n in VC else 15
+        for lo, hi in GC:
+            if lo < vc:
+                act(("CC", 128 * lo, 128 * hi), by_scalar(dall, ("offb", 128 + 8 * lo, 128 + 8 * hi), lo, hi, (zk, X0, X0 + 128)), AF.Sign, -0.5)
+        for q in range(vc, 15):
+            tt(("CC", 128 * q, 128 * q + 128), (dall, ("offb", 128 + 8 * q, 136 + 8 * q)), (zk, X0, X0 + 128), A.is_gt)
+        for lo, hi in ((0, 8), (8, 15)):
             k = 8 * (hi - lo)
-            v = [q for a, b, q in GC if lo <= a < hi][0] == "v"
-            fold(("pac", 128 + 8 * lo, 128 + 8 * hi), "FC" if v else "FB", "CC", 128 * lo, 128 * hi, ("IP", ("nab", 0, k)),
-                 ("IB", ("Tt", 64 * v, 64 * v + k)))
+            more = [("FC", ("CC", 0, 0)), ("CB", ("ON", 0, k))] if lo == vc else [("FB", ("CC", 0, 0))]
+            fold(("pac", 128 + 8 * lo, 128 + 8 * hi), more[0][0], "CC", 128 * lo, 128 * hi, ("IP", ("nab", 0, k)), ("IB", ("Tt", 0, k)), *more[1:])
 
     def choice(n):
         w = str(n % 2)
         zk = "ZK" + w
         pall = ("px", 0, 128)
-        mm(("px", 120, 128), ("ID", ("K1", 120, 128)), ("ID", ("K2", 120, 128)), ("CK", ("ON", 0, 8)), ("I16", ("naf", 0, 8)), keep=pall)
+        mm(("px", 120, 128), ("ID", ("K1", 120, 128)), ("ID", ("K2", 120, 128)), ("CK", ("ON", 0, 8)), ("I18", ("naf", 0, 8)), keep=pall)
         mm(("px", 0, 120), ("ID", ("K1", 0, 120)), ("ID", ("K2", 0, 120)), ("CK", ("ON", 0, 120)), last=False, keep=pall)
-        act(("hb", 0, 120), ("pb", 0, 120), AF.Abs, ("tau", 0, 1), -1.0)
-        act(("fb", 0, 120), ("hb", 0, 120), AF.Relu, -8.0)
-        mm(("px", 0, 120), ("IB", ("fb", 0, 120)), ("IB", ("fa", 0, 120)), first=False, keep=pall)
+        act(("hb", 0, 120), ("pb", 0, 120), AF.Relu, -8.0, -1.0)
+        act(("fb", 0, 120), ("pb", 0, 120), AF.Relu, -8.0)
+        mm(("px", 0, 120), ("IB", ("fa", 0, 120)), ("IB", ("hb", 0, 120)), ("IB", ("fb", 0, 120)), first=False, keep=pall)
         tt(("x", 0, 128), pall, ("N" + w, 0, 128), A.add)
         tt(("x", 0, 120), ("pac", 128, 248), ("x", 0, 120), A.min)
-        if RED:
-            for j in range(8):
-                op("v", lambda e, j=j: e.tensor_reduce(T["code"][:, j:j + 1], T.x[:, j:128:8], AxisListType.X, A.max), [("x", 0, 128)],
-                   [("code", j, j + 1)], MINC * CYC)
-        else:
-            tt(("m", 0, 64), ("x", 0, 64), ("x", 64, 128), A.max)
-            tt(("m", 64, 96), ("m", 0, 32), ("m", 32, 64), A.max)
-            tt(("m", 96, 112), ("m", 64, 80), ("m", 80, 96), A.max)
-            tt(("code", 0, 8), ("m", 96, 104), ("m", 104, 112), A.max)
-        ts(("ou", 0, 8), ("code", 0, 8), 1.0 / 4096, A.mult, -864.0 / 4096, A.add)
-        ts(("Ci", 0, 8), ("code", 0, 8), -5.0 * 524288, A.add)
+        for j in range(8):
+            op("v", lambda e, j=j: e.tensor_reduce(T.Ci[:, j:j + 1], T.x[:, j:128:8], AxisListType.X, A.max), [("x", 0, 128)],
+               [("Ci", j, j + 1)], MINC * CYC + FIX)
+        ts(("ou", 0, 8), ("Ci", 0, 8), 1.0 / 4096, A.mult, 256 - 864.0 / 4096, A.add)
         ts(("LH", 0, 8), ("Ci", 0, 8), 7, A.bitwise_and)
         ts(("LH", 8, 16), ("Ci", 0, 8), 3, A.logical_shift_right, 255, A.bitwise_and)
-        cp((zk, NM, NM + 16), ("LH", 0, 16))
-        act((zk, ZH, NM), ((zk, 0, X0), ("ou", 0, 8)), AF.Copy)
+        tt((zk, 0, ZH), ("LH", 0, 16), ("J8", 0, 16), A.add)
+        act((zk, ZH, ZH + 128), ((zk, W0, X0), ("ou", 0, 8)), AF.Copy)
         ts(("Oj", 0, 8), ("Ci", 0, 8), 12, A.logical_shift_right, 4095, A.bitwise_and)
 
     def send(n):
@@ -498,14 +512,14 @@ def rank_program(g, core, T, topo):
         rid, pid = topo.addr(to, core)
 
         def issue(total):
-            g.remote_dma(T[lc][:, :], T[zk][:, ZH:NM + 16], T.sem[("arr%d" if to == dst else "rl%d") % n], T.sem["loc%d" % n], pid, rid, m)
+            g.remote_dma(T[lc][:, :], T[zk][:, 0:PAY], T.sem[("arr%d" if to == dst else "rl%d") % n], T.sem["loc%d" % n], pid, rid, m)
             total["loc%d" % n] = k
             return ("loc%d" % n, k)
-        calls.append(("g", [(zk, ZH, NM + 16)], [("sent", n, n + 1)], 500.0, HOP, issue))
+        calls.append(("g", [(zk, 0, PAY)], [("sent", n, n + 1)], 500.0, HOP, issue))
         frm = cores[(rank - 1 - t % 3) % len(cores)]
         last = route(topo, frm, core)
         arr = ("arr%d" % n, engines(topo, last, core)[1])
-        calls.append(("net", [("sent", n, n + 1)], [(lc, 0, PAY)], 0.0, 0.0 if last == frm else HOP, lambda total: arr))
+        calls.append(("net", [("sent", n, n + 1)], [(lc, 0, PAY)], 0.0, 0.0 if last == frm else HOP - 300, lambda total: arr))
 
     def travel(n):
         w, t = str(n % 2), n // 2
@@ -515,49 +529,31 @@ def rank_program(g, core, T, topo):
         tt(("keep", 0, 128), (("Oj", 0, 8), ("cl", 0, 8)), ("TH", 0, 128), A.is_lt)
         tt(("kd" + w, 8, 128), ("pE", 136, 256), ("keep", 8, 128), A.mult)
         if t == RO - 1:
-            dmas("y", "yz_" + w, [(b, a) for a, b in placed(T[zk], ZH, T.yz, w)], [(zk, ZH, NM)], [])
+            act(("ZN" + w, 0, 128), ((zk, ZH, ZH + 128), ("l6", 0, 8)), AF.Copy)
+            dmas("y", "yz_" + w, [(b, a) for a, b in placed(T["ZN" + w], T.yz, w)], [("ZN" + w, 0, 128)], [])
             return
-        dmas("y", "rep%d" % n, [(T[zk][:, c:c + 128], T[zk][:, ZH:NM]) for c in (0, Z4, Z4 + 128, Z4 + 256)], [(zk, ZH, NM)],
-             [(zk, 0, 128), (zk, Z4, ZH)])
+        dmas("y", "rep%d" % n, [(T[zk][:, c:c + 128], T[zk][:, ZH:ZH + 128]) for c in range(ZH + 128, W0 + 128, 128)],
+             [(zk, ZH, ZH + 128), ("sent", n, n + 1)], [(zk, ZH + 128, W0 + 128)])
         act(("fl", 0, 8), ("keep", 120, 128), AF.Copy, accum=("acc", n % 2, n % 2 + 1))
         if n % 2:
             mm(("pE", 296, 297), *[("QF", ("acc", k, k + 1)) for k in range(3)])
             cp(("ri", 0, 1), ("pE", 296, 297))
             tt(("tau", 0, 1), ("pE", 296, 297), ("ri", 0, 1), A.subtract)
-            if "s" in [q for a, b, q in GC]:
-                act(("Tt", 0, 64), ("ON", 0, 64), AF.Copy, None, ("tau", 0, 1))
-            if "v" in [q for a, b, q in GC]:
-                act(("Tt", 64, 128), ("ON", 0, 64), AF.Identity, 4.0, ("tau", 0, 1))
+            act(("Tt", 0, 64), ("ON", 0, 64), AF.Identity, -4.0, ("tau", 0, 1))
+            act(("Tt", 64, 128), ("ON", 0, 64), AF.Identity, 4.0, ("tau", 0, 1))
         vmod(w)
 
     def arrival(n):
         w, lc = str(n % 2), "L%d" % n
         d, dall = T["D" + w], ("D" + w, 0, 2048)
-        both = n in BOTH
-        if CV:
-            tt(("ci", 0, 8), (lc, 128, 136), ("cb", 0, 8), A.add)
-            cp(("cu", 0, 8), ("ci", 0, 8))
-        else:
-            mm(("pE", 256, 264), ("ID", (lc, 128, 136)), ("ID", ("cb", 0, 8)))
-        if both:
-            mm(("pE", 264, 272), ("SW", (lc, 128, 136)), ("SW", ("cb", 0, 8)))
-        mm(("pE", 0, 8), ("I11", (lc, 128, 136)), ("I14", (lc, 136, 144)), ("CE", ("ON", 0, 8)))
-        k = 16 if both else 8
-        if not CV:
-            cp(("cu", 0, k), ("pE", 256, 256 + k))
-        elif both:
-            cp(("cu", 8, 16), ("pE", 264, 272))
+        ts(("cu", 0, 8), (lc, 0, 8), ("cb", 0, 1), A.add)
+        mm(("pE", 0, 8), ("I11", (lc, 0, 8)), ("I14", (lc, 8, 16)), ("ID", ("CE", 0, 8)))
         tt(("E" + w, 0, 128), ("pE", 0, 128), ("kd" + w, 0, 128), A.add)
-        tt(("su", 0, 128), (dall, ("cu", 0, 8)), (lc, 0, 128), A.add)
+        tt(("su", 0, 128), (dall, ("cu", 0, 8)), (lc, ZH, PAY), A.add)
         ts(("sh", 0, 128), ("su", 0, 128), 0.5, A.mult, -0.25, A.add)
-        if both:
-            mm(("pE", 384, 512), ("SF", ("su", 0, 128)))
-            ts(("sh", 128, 256), ("pE", 384, 512), 0.5, A.mult, -0.25, A.add)
-        cp((dall, ("cu", 0, k)), ("sh", 0, 16 * k))
+        cp((dall, ("cu", 0, 8)), ("sh", 0, 128))
         if n // 2 < RO - 1:
-            if not both:
-                dmas("y", "xc%d" % n, [(d[64:128, 0:1024], d[0:64, 0:1024]), (d[0:64, 1024:2048], d[64:128, 1024:2048])], [dall], [dall],
-                     XC)
+            dmas("y", "xc%d" % n, [(d[64:128, 0:1024], d[0:64, 0:1024]), (d[0:64, 1024:2048], d[64:128, 1024:2048])], [dall], [dall], XC)
             lists(w)
             return
         r = slice(64 * int(w), 64 * int(w) + 64)
@@ -566,7 +562,7 @@ def rank_program(g, core, T, topo):
         act(("X", 0, 256), (("E" + w, 0, 128), ("l3", 0, 16)), AF.Copy)
         turn(("XT", 0, 256), ("X", 0, 256))
         act(("YL" + w, 0, 128), (("XT", 0, 256), ("l4", 0, 8)), AF.Identity, -float(ROT), 1.0 / 2048)
-        dmas("s", "ye_" + w, [(b, a) for a, b in placed(T["YL" + w], 0, T.ye, w)], [("YL" + w, 0, 128)], [])
+        dmas("s", "ye_" + w, [(b, a) for a, b in placed(T["YL" + w], T.ye, w)], [("YL" + w, 0, 128)], [])
 
     stage = [-1] * len(calls)
     for n in range(STEPS):
@@ -587,7 +583,7 @@ def rank_program(g, core, T, topo):
                 known[q][a] = b
         known[q][s] = n
 
-    for q, reads, writes, busy, done, issue in in_order(calls, stage):
+    for q, reads, writes, busy, done, issue in (c[:6] for c in in_order(calls, stage)):
         if q == "net":
             acc[writes[0][0]] = [(0, PAY, True, issue(total), q)]
             continue

import numpy as np
from concourse.mybir import AluOpType as A
from concourse.mybir import ActivationFunctionType as AF
from concourse.mybir import AxisListType

RO = 5
PAY = 144
BIG = 2.0 ** 28
FLOOR = -1055.5 / 2048
ROT = 1184
JR = 256 - ROT // 8
ZH, W0, QB, X0 = 16, 400, 656, 2576
CYC, PEC, GATHER, SCATTER, MINC, FIX = 0.83, 0.47, 1.15, 3.4, 64, 35
WAKE, DMA, HOP, XC = 250.0, 1500.0, 1600.0, 2200.0
PASSES, ORDERS = 1300, {}
LATE = (0, 0, 0, 0.5, 0.5)
GA = [(12, 16, "v"), (8, 12, "v"), (4, 8, "v"), (2, 4, "v"), (0, 2, "s")]
AB = [(12, 16), (8, 12), (4, 8), (2, 4)]
SGP = [(8, 16), (2, 8)]
GB = [(8, 15), (0, 4), (4, 8)]
GC = [(0, 4), (4, 8), (8, 12), (12, 15)]
VC = (8, 9)
DB = ["d0", "d1", "d2"]


def _s(n, dt):
    return ("sbuf", [128, n], dt)


SCRATCH = {}
for _w in "01":
    for _n, _c, _d in (("D", 2048, "bfloat16"), ("ZK", 2704, "bfloat16"), ("Fw", 144, "bfloat16"), ("E", 128, "float32"),
                       ("v", 8, "float32"), ("kd", 128, "float32"), ("N", 128, "int32"), ("EL", 128, "int32"), ("wti", 1, "int32"),
                       ("off", 128, "uint16"), ("YL", 128, "float32"), ("ZN", 128, "bfloat16")):
        SCRATCH[_n + _w] = _s(_c, _d)
for _n, _w in (("DF", 2048), ("SG", 2048), ("CC", 1920), ("BB", 1920), ("DG", 2048), ("fa", 120), ("hb", 120), ("fb", 120),
               ("naf", 16), ("nab", 64), ("fl", 8), ("CE", 8), ("K1", 128), ("K2", 128),
               ("O8", 8), ("B8a", 8), ("B8", 8), ("F", 144), ("Fh", 144), ("Fq", 144), ("FB", 144), ("FC", 144), ("CB", 128), ("Tt", 128),
               ("ON", 128), ("ID", 128), ("NI", 128), ("N8", 128), ("IB", 128), ("IP", 128), ("I11", 128), ("I14", 128), ("I18", 128),
               ("C32", 128), ("CK", 128)):
    SCRATCH[_n] = _s(_w, "bfloat16")
for _n, _w in (("Ub", 128), ("x", 128), ("keep", 128), ("acc", 3), ("tau", 1), ("X", 256), ("XT", 256), ("wf", 2),
               ("cb", 1), ("J8", 16), ("IF", 128), ("JF", 128), ("QF", 128), ("pmf", 1), ("TH", 128), ("su", 128)):
    SCRATCH[_n] = _s(_w, "float32")
for _n, _w in (("P", 128), ("PB", 256), ("NB", 256), ("Ui", 128), ("vi", 8), ("Ci", 8), ("Oj", 8), ("LH", 16), ("ri", 1),
               ("sh", 128), ("ip", 16), ("pm", 16), ("t", 160),
               ("i1", 16), ("i2", 8), ("i3", 16), ("i4", 8), ("i5", 8), ("i6", 128), ("i7", 128), ("i8", 8)):
    SCRATCH[_n] = _s(_w, "int32")
for _n, _w in (("offb", 256), ("ou", 8), ("cu", 8), ("cl", 8), ("l1", 16), ("l2", 8), ("l3", 16), ("l4", 8), ("l5", 8), ("l6", 8)):
    SCRATCH[_n] = _s(_w, "uint16")
PSUM = ["pU", "pac", "pb", "px", "pE", "d0", "d1", "d2"]
for _n in PSUM:
    SCRATCH[_n] = ("psum", [128, 512], "float32")
STEPS = 2 * RO
for _t in range(STEPS):
    SCRATCH["L%d" % _t] = _s(PAY, "bfloat16")
SEMAPHORES = (["qv", "qs", "qp", "qg"] + [k + w for k in ("wt", "zv", "ef", "dv", "yd", "ye", "yz") for w in ("_0", "_1")] +
              [k + str(t) for k in ("arr", "rl", "loc", "xc", "rep") for t in range(STEPS)])


def target(cores, rank, t):
    return cores[(rank + 1 + t % 3) % len(cores)]


def route(topo, src, dst):
    if topo.may_write(src, dst):
        return src
    cand = [c for c in topo.cores_of(src) if c != src and topo.may_write(c, dst)]
    same = [c for c in cand if topo.die(c) == topo.die(src)]
    return (same or cand)[0]


def engines(topo, src, dst):
    return topo.mask(src, dst), len(topo.engines(src, dst))


def relay_program(g, core, T, topo):
    used = []
    for n in range(STEPS):
        for r in range(len(T.cores)):
            src, dst = T.cores[r], target(T.cores, r, n // 2)
            if src != core and route(topo, src, dst) == core:
                m, k = engines(topo, core, dst)
                _, nin = engines(topo, src, core)
                rid, pid = topo.addr(dst, core)
                g.wait_ge(T.sem["rl%d" % n], nin)
                g.remote_dma(T["L%d" % n][:, :], T["L%d" % n][:, :], T.sem["arr%d" % n], T.sem["loc%d" % n], pid, rid, m)
                used.append((n, k))
    for n, k in used:
        g.wait_ge(T.sem["loc%d" % n], k)


def in_order(calls, stage):
    sign = tuple((c[0], c[3], c[4]) for c in calls)
    if sign in ORDERS:
        return [calls[i] for i in ORDERS[sign]]
    n = len(calls)
    busy = [c[3] for c in calls]
    fwd = [dict() for _ in range(n)]
    seen = {}
    begin = [c[6] if len(c) > 6 else 0.0 for c in calls]
    for i, (q, reads, writes) in enumerate(c[:3] for c in calls):
        for regs, wr in ((reads, False), (writes, True)):
            for b, lo, hi in regs:
                for l2, h2, w2, j in seen.get(b, []):
                    if j != i and (wr or w2) and lo < h2 and l2 < hi:
                        chain = q == "p" and calls[j][0] == "p" and b in PSUM
                        fwd[i][j] = max(fwd[i].get(j, 0.0), busy[j] if chain else calls[j][4] + WAKE)
        for b, lo, hi in writes:
            seen[b] = [r for r in seen.get(b, []) if not (lo <= r[0] and r[1] <= hi)] + [(lo, hi, True, i)]
        for b, lo, hi in reads:
            seen.setdefault(b, []).append((lo, hi, False, i))
    bwd = [dict() for _ in range(n)]
    for i in range(n):
        for j, lag in fwd[i].items():
            bwd[j][i] = lag + busy[i] - busy[j]
    banks = [sorted({r[0] for r in c[1] + c[2] if r[0] in PSUM}) for c in calls]

    def place(before, after, first, key):
        left, at, taken = [len(p) for p in before], [0.0] * n, {}
        ready = [i for i in range(n) if not left[i]]
        while ready:
            i = min(ready, key=lambda i: key[i])
            ready.remove(i)
            q = calls[i][0]
            t = max([first[i]] + [at[j] + lag for j, lag in before[i].items()])
            moved = True
            while moved:
                moved = False
                for r in [q] + banks[i]:
                    l = taken.setdefault(r, [])
                    k = len(l)
                    while k and l[k - 1][1] + WAKE > t:
                        k -= 1
                    for a, b, q2 in l[k:]:
                        pad = 0.0 if q2 == q else WAKE
                        if a - pad < t + busy[i] and t < b + pad and (r == q or pad):
                            t, moved = b + pad, True
            for r in [q] + banks[i]:
                l = taken[r]
                k = len(l)
                while k and l[k - 1][0] > t:
                    k -= 1
                l.insert(k, (t, t + busy[i], q))
            at[i] = t
            for j in after[i]:
                left[j] -= 1
                if not left[j]:
                    ready.append(j)
        return at

    def span(at):
        return max(at[i] + calls[i][4] for i in range(n))

    seed = [1]

    def rnd():
        seed[0] = (seed[0] * 1103515245 + 12345) % 2147483648
        return seed[0] / 2147483648

    way = [0.0] * n
    for i in range(n - 1, -1, -1):
        way[i] = max([calls[i][4]] + [way[k] + fwd[k][i] for k in bwd[i]])
    at = place(fwd, bwd, begin, [(stage[i], -way[i], i) for i in range(n)])
    kind = [(c[0], c[2][0][0].rstrip("0123456789"), c[2][0][1]) if c[2] else (c[0], "", 0) for c in calls]
    best = (span(at), at)
    for p in range(PASSES):
        if p % 2 == 0:
            c, sh = rnd() * best[0], 1500 * rnd() if p > 2 else 0.0
            d = [sh * rnd() if abs(best[1][i] - c) < 3000 else sh / 2 for i in range(n)]
        else:
            m = {k: (rnd() - 0.5) * 2000 if rnd() < 0.1 and p > 2 else 0.0 for k in sorted(set(kind))}
            d = [m[k] for k in kind]
        back = place(bwd, fwd, [c[4] - c[3] for c in calls], [(-best[1][i] - busy[i] + d[i], -i) for i in range(n)])
        at = place(fwd, bwd, begin, [(-back[i] - busy[i], i) for i in range(n)])
        if span(at) <= best[0]:
            best = (span(at), at)
    ORDERS[sign] = sorted(range(n), key=lambda i: (best[1][i], i))
    return [calls[i] for i in ORDERS[sign]]


def rank_program(g, core, T, topo):
    rank = T.rank_of(core)
    if rank is None:
        relay_program(g, core, T, topo)
        return
    cores = T.cores
    eng = {"v": g.vector, "s": g.scalar, "p": g.tensor, "g": g, "y": g.sync}
    calls = []

    def op(q, fn, reads, writes, ns):
        def issue(total):
            s = "q" + q
            total[s] = total.get(s, 0) + 1
            fn(eng[q]).then_inc(T.sem[s], 1)
            return (s, total[s])
        calls.append((q, reads, writes, ns, ns, issue))

    def dmas(q, s, pairs, reads, writes, ns=None, first=0.0):
        def issue(total):
            for out, in_ in pairs:
                eng[q].dma_start(out, in_).then_inc(T.sem[s], 16)
            total[s] = 16 * len(pairs)
            return (s, total[s])
        calls.append((q, reads, writes, 60.0 * len(pairs), ns or DMA, issue, first))

    def ap(v):
        return T[v[0]][:, v[1]:v[2]] if len(v) == 3 else T[v[0]][:, v[1]:v[2]:v[3]]

    def rg(v):
        return (v[0], v[1], v[2])

    def opnd(v):
        if isinstance(v[0], tuple):
            return ap(v[0]).indirect(ap(v[1])), [rg(v[0]), rg(v[1])]
        return ap(v), [rg(v)]

    def ns(out, a, per):
        if isinstance(out[0], tuple):
            return 50 + (a[2] - a[1]) * SCATTER * CYC
        n = len(range(*out[1:]))
        return 50 + n * GATHER * CYC if isinstance(a[0], tuple) else max(MINC, n * per) * CYC + FIX

    def narrow(*vs):
        return 0.5 if all(SCRATCH[v[0]][2] in ("bfloat16", "uint16") for v in vs if not isinstance(v[0], tuple)) else 1

    def tt(out, a, b, o):
        oa, orr = opnd(out)
        aa, ar = opnd(a)
        ba, br = opnd(b)
        op("v", lambda e: e.tensor_tensor(oa, aa, ba, o), ar + br + orr[1:], orr[:1], ns(out, a, 1 if a[0] in PSUM else 2))

    def ts(out, a, s1, o1, s2=None, o2=None):
        oa, orr = opnd(out)
        aa, ar = opnd(a)
        rd = list(ar)
        sc = []
        for s in (s1, s2):
            if isinstance(s, tuple):
                rd.append(rg(s))
                sc.append(ap(s))
            else:
                sc.append(s)
        if o2 is None:
            op("v", lambda e: e.tensor_scalar(oa, aa, sc[0], None, o1), rd, orr[:1], ns(out, a, narrow(out, a)))
        else:
            op("v", lambda e: e.tensor_scalar(oa, aa, sc[0], sc[1], o1, o2), rd, orr[:1], ns(out, a, narrow(out, a)))

    def cp(out, a):
        oa, orr = opnd(out)
        aa, ar = opnd(a)
        op("v", lambda e: e.tensor_copy(oa, aa), ar + orr[1:], orr[:1], ns(out, a, narrow(out, a)))

    def fill(out, c):
        op("v", lambda e: e.memset(ap(out), c), [], [rg(out)], ns(out, out, narrow(out)))

    def act(out, a, f, bias=None, scale=None, accum=None):
        aa, ar = opnd(a)
        kw = {}
        rd = list(ar)
        wr = [rg(out)]
        for k, c in (("bias", bias), ("scale", scale)):
            if isinstance(c, tuple):
                kw[k] = ap(c)
                rd.append(rg(c))
            elif c is not None:
                kw[k] = c
        if accum is not None:
            kw["accum_out"] = ap(accum)
            wr.append(rg(accum))
        op("s", lambda e: e.activation(ap(out), aa, f, **kw), rd, wr, ns(out, a, 1))

    def pns(out, terms):
        return sum(max(64, out[2] - out[1]) * (4 if SCRATCH[l][2] == "float32" else 1) * PEC for l, r in terms)

    def mm(out, *terms, first=True, last=True, keep=None):
        def fn(e):
            for n, (l, r) in enumerate(terms):
                x = e.matmul(ap(out), T[l][:, :], ap(r), first and n == 0, last and n == len(terms) - 1)
            return x
        op("p", fn, [(l, 0, 128) for l, r in terms] + [rg(r) for l, r in terms], [keep or rg(out)], pns(out, terms))

    def fold(out, fm, src, lo, hi, *extra):
        def fn(e):
            for n, (l, r) in enumerate(extra):
                e.matmul(ap(out), T[l][:, :], ap(r), n == 0, False)
            for jl in range(16):
                r = e.matmul(ap(out), T[fm][:, 15 - jl:143 - jl], T[src][:, lo + jl:hi:16], jl == 0 and not extra, jl == 15)
            return r
        op("p", fn, [(fm, 0, 144), (src, lo, hi)] + [(l, 0, 128) for l, r in extra] + [rg(r) for l, r in extra], [rg(out)],
           pns(out, [(fm, 0)] * 16 + list(extra)))

    def usum(out, w, lo, hi):
        fold(out, "Fw" + w, "ZK" + w, lo, hi, ("C32", ("ON", 0, out[2] - out[1])))

    def turn(out, a):
        op("v", lambda e: e.transpose(ap(out), ap(a)), [rg(a)], [rg(out)], ns(out, a, 1))

    def iota(name, pattern, base, cm):
        n = SCRATCH[name][1][1]
        op("g", lambda e: e.iota(T[name][:, :], pattern, base, cm), [], [(name, 0, n)], 130 + 2 * n * CYC)

    def select(out, a, *args):
        n = SCRATCH[out][1][1]
        op("g", lambda e: e.affine_select(T[out][:, :], T[a][:, :], *args), [(a, 0, n)], [(out, 0, n)], 170 + 2 * n * CYC)

    def placed(sb, hbm, w):
        r = slice(64 * int(w), 64 * int(w) + 64)
        b = 128 - JR
        return [(sb[0:64, 0:128], hbm[r, JR:JR + 128]), (sb[64:128, 0:b], hbm[r, JR + 128:256]), (sb[64:128, b:128], hbm[r, 0:JR])]

    for w in "01":
        r = slice(64 * int(w), 64 * int(w) + 64)
        hs = (slice(0, 64), slice(64, 128))
        after = [("D0", 0, 1)] if w == "1" else []
        dmas("s" if w == "0" else "y", "ef_" + w, placed(T["EL" + w], T.ef, w), after, [("EL" + w, 0, 128)])
        dmas("y", "wt_" + w, [(T["wti" + w][h, :], T.wt[r, :]) for h in hs], after, [("wti" + w, 0, 1)])
        dmas("y", "zv_" + w, placed(T["ZN" + w], T.zv, w), after, [("ZN" + w, 0, 128)])
        dmas("y", "dv_" + w,
             [(T["D" + w][h, ROT:2048], T.dv[r, 0:2048 - ROT]) for h in hs] + [(T["D" + w][h, 0:ROT], T.dv[r, 2048 - ROT:2048]) for h in hs],
             after, [("D" + w, 0, 2048)], XC + 900, 400.0)

    fill(("O8", 0, 8), 1.0)
    fill(("F", 0, 144), 0.0)
    fill(("ON", 0, 128), 1.0)
    iota("ip", [[0, 16]], 0, 1)
    iota("i1", [[1, 8], [0, 2]], 0, 8)
    iota("i2", [[-2, 8]], 15, 32)
    iota("i3", [[1, 8], [0, 2]], 1144, -8)
    iota("i4", [[2, 8]], 0, 32)
    iota("i5", [[8, 8]], 0, 0)
    iota("i6", [[1, 16], [0, 8]], 0, 0)
    iota("i7", [[0, 16], [16, 8]], 0, 0)
    iota("i8", [[1, 8]], 0, 8)
    select("B8a", "O8", [[-16, 8]], A.is_ge, 0.0, 0, 1)
    select("B8", "B8a", [[16, 8]], A.is_ge, 0.0, 15, -1)
    select("ID", "ON", [[-1, 128]], A.is_equal, 0.0, 0, 1)
    cp(("F", 15, 128, 16), ("B8", 0, 8))
    for name, c in (("Fq", 0.25), ("Fh", 0.5), ("FB", 0.25 * BIG), ("FC", 0.5 * BIG)):
        ts((name, 0, 144), ("F", 0, 144), c, A.mult)
    for name, c in (("NI", -1.0), ("N8", -8.0), ("IB", -BIG), ("IP", 4 * BIG), ("I18", -262144.0), ("I11", 2048.0), ("I14", 16384.0),
                    ("IF", 1.0), ("JF", -1.0)):
        ts((name, 0, 128), ("ID", 0, 128), c, A.mult)
    for name, c in (("C32", 1.0 / 8192), ("CK", 864.0 / 128), ("QF", 0.5), ("CB", -4 * BIG / 128)):
        fill((name, 0, 128), c)
    fill(("tau", 0, 1), -0.25)
    fill(("Tt", 0, 64), -4.25)
    fill(("Tt", 64, 128), 3.75)
    fill(("acc", 2, 3), -0.5 / 128)
    fill(("kd0", 0, 8), 0.0)
    fill(("kd1", 0, 8), 0.0)

    def t8(k, n=8):
        return ("t", 8 * k, 8 * k + n)

    ts(("pm", 0, 16), ("ip", 0, 16), 15, A.bitwise_and)
    cp(("pmf", 0, 1), ("pm", 0, 1))
    ts(t8(0), ("ip", 0, 8), 7, A.bitwise_and)
    cp(("cl", 0, 8), t8(0))
    ts(t8(1), ("ip", 0, 8), 64, A.bitwise_and)
    ts(t8(2), ("pm", 0, 8), 4.0, A.mult)
    tt(t8(3), t8(1), t8(2), A.add)
    ts(("cb", 0, 1), t8(3, 1), 16.0, A.mult)
    ts(t8(4), ("i8", 0, 8), 127, A.bitwise_and)
    cp(("l5", 0, 8), t8(4))
    ts(t8(7, 16), ("i1", 0, 16), 127, A.bitwise_and)
    cp(("l1", 0, 16), t8(7, 16))
    ts(t8(9), ("ip", 0, 8), 3, A.logical_shift_right, 1, A.bitwise_and)
    ts(t8(10), ("ip", 0, 8), 16, A.bitwise_and)
    ts(t8(11), ("i2", 0, 8), 255, A.bitwise_and)
    tt(t8(12), t8(10), t8(9), A.subtract)
    tt(t8(13), t8(11), t8(12), A.add)
    cp(("l2", 0, 8), t8(13))
    ts(t8(14, 16), ("i3", 0, 16), 127, A.bitwise_and)
    cp(("l3", 0, 16), t8(14, 16))
    ts(t8(16), ("i4", 0, 8), 255, A.bitwise_and)
    tt(t8(17), t8(16), t8(9), A.add)
    tt(t8(18), t8(17), t8(10), A.add)
    cp(("l4", 0, 8), t8(18))
    ts(t8(5), t8(0), -16.0, A.mult)
    tt(t8(6), t8(17), t8(5), A.add)
    cp(("l6", 0, 8), t8(6))
    cp(("J8", 0, 8), ("i5", 0, 8))
    fill(("J8", 8, 16), 0.0)
    ts(("CE", 0, 8), ("i5", 0, 8), -float(ROT), A.add, -2048.0, A.mult)
    ts(("TH", 0, 128), ("i6", 0, 128), 128.0, A.mult)
    ts(("K1", 0, 120), ("i6", 0, 120), 524288.0, A.mult)
    fill(("K1", 120, 128), -3 * 262144.0)
    ts(("K2", 0, 128), ("i7", 0, 128), ("pmf", 0, 1), A.add, 4096.0, A.mult)

    def lists(w):
        tt(("P", 0, 128), (("v" + w, 0, 8), ("cl", 0, 8)), ("E" + w, 0, 128), A.mult)
        ts(("N" + w, 0, 128), ("P", 0, 128), 5, A.logical_shift_right, 2047, A.bitwise_and)
        cp(("off" + w, 0, 128), ("N" + w, 0, 128))

    def vmod(w, first=False):
        if first:
            def fn(e):
                e.matmul(T.pE[:, 280:288], T.C32[:, :], T.ON[:, 0:8], True, False)
                for jl in range(16):
                    r = e.matmul(T.pE[:, 280:288], T["Fw" + w][:, 15 - jl:143 - jl], T["ZN" + w][:, 8 * jl:8 * jl + 8], False, jl == 15)
                return r
            op("p", fn, [("C32", 0, 128), ("ON", 0, 8), ("Fw" + w, 0, 144), ("ZN" + w, 0, 128)], [("pE", 280, 288)], 17 * 64 * PEC)
        else:
            usum(("pE", 280, 288), w, ZH, ZH + 128)
        ts(("vi", 0, 8), ("pE", 280, 288), FLOOR, A.add)
        tt(("v" + w, 0, 8), ("pE", 280, 288), ("vi", 0, 8), A.subtract)

    def four(w):
        act(("ZK" + w, ZH + 128, ZH + 256), ("ZK" + w, ZH, ZH + 128), AF.Copy)
        act(("ZK" + w, ZH + 256, ZH + 512), ("ZK" + w, ZH, ZH + 256), AF.Copy)

    for w in "01":
        wf = ("wf", int(w), int(w) + 1)
        cp(wf, ("wti" + w, 0, 1))
        ts(("Fw" + w, 0, 144), ("F", 0, 144), wf, A.mult, 1.0 / 2048, A.mult)
        ts(("X", 0, 256), (("EL" + w, 0, 128), ("l1", 0, 16)), float(ROT), A.add, 2048.0, A.mult)
        turn(("XT", 0, 256), ("X", 0, 256))
        act(("E" + w, 0, 128), (("XT", 0, 256), ("l2", 0, 8)), AF.Copy)
        act(("ZK" + w, ZH, ZH + 128), (("ZN" + w, 0, 128), ("l5", 0, 8)), AF.Copy)
        four(w)
        vmod(w, True)
        lists(w)

    bank = [0]

    def by_scalar(dall, lst, lo, hi, sub):
        b = DB[bank[0] % len(DB)]
        g0 = 512 * (bank[0] % 4)
        bank[0] += 1
        act(("DG", g0, g0 + 128 * (hi - lo)), (dall, lst), AF.Copy)
        for k in range(hi - lo):
            mm((b, 128 * k, 128 * k + 128), ("NI", sub), ("ID", ("DG", g0 + 128 * k, g0 + 128 * k + 128)))
        return (b, 0, 128 * (hi - lo))

    def main(n):
        w = str(n % 2)
        zk, e, dall = "ZK" + w, "E" + w, ("D" + w, 0, 2048)
        for lo, hi, q in GA:
            lst = ("off" + w, 8 * lo, 8 * hi)
            if q == "v":
                df = ("DF", 128 * lo, 128 * hi)
                tt(df, (dall, lst), (zk, ZH, ZH + 128 * (hi - lo)), A.subtract)
            else:
                df = by_scalar(dall, lst, lo, hi, (zk, ZH, ZH + 128))
            if q == "s":
                act((zk, QB + 128 * lo, QB + 128 * hi), df, AF.Abs)
                act(("SG", 128 * lo, 128 * hi), df, AF.Sign, -0.5)
        for lo, hi in AB:
            act((zk, QB + 128 * lo, QB + 128 * hi), ("DF", 128 * lo, 128 * hi), AF.Abs)
        for lo, hi in SGP:
            act(("SG", 128 * lo, 128 * hi), ("DF", 128 * lo, 128 * hi), AF.Sign, -0.5)
        act((zk, QB - 128, QB), ("DF", 1920, 2048), AF.Abs)
        for lo, top, pu in ((64, 256, ("pU", 0, 64)), (0, 64, ("pb", 256, 320))):
            usum(pu, w, QB + 16 * lo, QB + 16 * lo + 1024)
            ts(("Ui", lo, lo + 64), pu, FLOOR, A.add)
            tt(("Ub", lo, lo + 64), pu, ("Ui", lo, lo + 64), A.subtract)
            if lo:
                tt(("PB", 128, 256), (("Ub", 120, 128), ("cl", 0, 8)), (e, 0, 128), A.mult)
            tt(("PB", lo, lo + 64), ((e, 120, 128), ("cl", 0, 4)), ("Ub", lo, lo + 64), A.mult)
            ts(("NB", lo, top), ("PB", lo, top), 5, A.logical_shift_right, 2047, A.bitwise_and)
            cp(("offb", lo, top), ("NB", lo, top))
        fold(("pac", 64, 128), "Fq", "SG", 1024, 2048)
        act(("naf", 0, 8), ("pac", 120, 128), AF.Sign, ("tau", 0, 1), -1.0)
        act(("nab", 0, 64), (("naf", 0, 8), ("cl", 0, 4)), AF.Copy)
        fold(("pac", 0, 64), "Fq", "SG", 0, 1024)
        act(("fa", 0, 120), ("pac", 0, 120), AF.Relu, ("tau", 0, 1), -1.0)
        for lo, hi in GB:
            tt(("BB", 128 * lo, 128 * hi), (dall, ("offb", 8 * lo, 8 * hi)), (zk, QB + 128 * lo, QB + 128 * hi), A.is_gt)
        for lo, hi in ((8, 15), (0, 8)):
            k = 8 * (hi - lo)
            fold(("pb", 8 * lo, 8 * hi), "Fh", "BB", 128 * lo, 128 * hi, ("NI", ("Tt", 64, 64 + k)), ("N8", ("nab", 0, k)))
        vc = 8 if n in VC else 15
        for lo, hi in GC:
            if lo < vc:
                act(("CC", 128 * lo, 128 * hi), by_scalar(dall, ("offb", 128 + 8 * lo, 128 + 8 * hi), lo, hi, (zk, X0, X0 + 128)), AF.Sign, -0.5)
        for q in range(vc, 15):
            tt(("CC", 128 * q, 128 * q + 128), (dall, ("offb", 128 + 8 * q, 136 + 8 * q)), (zk, X0, X0 + 128), A.is_gt)
        for lo, hi in ((0, 8), (8, 15)):
            k = 8 * (hi - lo)
            more = [("FC", ("CC", 0, 0)), ("CB", ("ON", 0, k))] if lo == vc else [("FB", ("CC", 0, 0))]
            fold(("pac", 128 + 8 * lo, 128 + 8 * hi), more[0][0], "CC", 128 * lo, 128 * hi, ("IP", ("nab", 0, k)), ("IB", ("Tt", 0, k)), *more[1:])

    def choice(n):
        w = str(n % 2)
        zk = "ZK" + w
        pall = ("px", 0, 128)
        mm(("px", 120, 128), ("ID", ("K1", 120, 128)), ("ID", ("K2", 120, 128)), ("CK", ("ON", 0, 8)), ("I18", ("naf", 0, 8)), keep=pall)
        mm(("px", 0, 120), ("ID", ("K1", 0, 120)), ("ID", ("K2", 0, 120)), ("CK", ("ON", 0, 120)), last=False, keep=pall)
        act(("hb", 0, 120), ("pb", 0, 120), AF.Relu, -8.0, -1.0)
        act(("fb", 0, 120), ("pb", 0, 120), AF.Relu, -8.0)
        mm(("px", 0, 120), ("IB", ("fa", 0, 120)), ("IB", ("hb", 0, 120)), ("IB", ("fb", 0, 120)), first=False, keep=pall)
        tt(("x", 0, 128), pall, ("N" + w, 0, 128), A.add)
        tt(("x", 0, 120), ("pac", 128, 248), ("x", 0, 120), A.min)
        for j in range(8):
            op("v", lambda e, j=j: e.tensor_reduce(T.Ci[:, j:j + 1], T.x[:, j:128:8], AxisListType.X, A.max), [("x", 0, 128)],
               [("Ci", j, j + 1)], MINC * CYC + FIX)
        ts(("ou", 0, 8), ("Ci", 0, 8), 1.0 / 4096, A.mult, 256 - 864.0 / 4096, A.add)
        ts(("LH", 0, 8), ("Ci", 0, 8), 7, A.bitwise_and)
        ts(("LH", 8, 16), ("Ci", 0, 8), 3, A.logical_shift_right, 255, A.bitwise_and)
        tt((zk, 0, ZH), ("LH", 0, 16), ("J8", 0, 16), A.add)
        act((zk, ZH, ZH + 128), ((zk, W0, X0), ("ou", 0, 8)), AF.Copy)
        ts(("Oj", 0, 8), ("Ci", 0, 8), 12, A.logical_shift_right, 4095, A.bitwise_and)

    def send(n):
        w, t = str(n % 2), n // 2
        zk, lc = "ZK" + w, "L%d" % n
        dst = target(cores, rank, t)
        via = route(topo, core, dst)
        to = dst if via == core else via
        m, k = engines(topo, core, to)
        rid, pid = topo.addr(to, core)

        def issue(total):
            g.remote_dma(T[lc][:, :], T[zk][:, 0:PAY], T.sem[("arr%d" if to == dst else "rl%d") % n], T.sem["loc%d" % n], pid, rid, m)
            total["loc%d" % n] = k
            return ("loc%d" % n, k)
        calls.append(("g", [(zk, 0, PAY)], [("sent", n, n + 1)], 500.0, HOP, issue))
        frm = cores[(rank - 1 - t % 3) % len(cores)]
        last = route(topo, frm, core)
        arr = ("arr%d" % n, engines(topo, last, core)[1])
        calls.append(("net", [("sent", n, n + 1)], [(lc, 0, PAY)], 0.0, 0.0 if last == frm else HOP - 300, lambda total: arr))

    def travel(n):
        w, t = str(n % 2), n // 2
        zk, e = "ZK" + w, "E" + w
        mm(("pE", 8, 128), ("IF", (e, 0, 120)))
        mm(("pE", 136, 256), ("IF", (e, 8, 128)), ("JF", (e, 0, 120)))
        tt(("keep", 0, 128), (("Oj", 0, 8), ("cl", 0, 8)), ("TH", 0, 128), A.is_lt)
        tt(("kd" + w, 8, 128), ("pE", 136, 256), ("keep", 8, 128), A.mult)
        if t == RO - 1:
            act(("ZN" + w, 0, 128), ((zk, ZH, ZH + 128), ("l6", 0, 8)), AF.Copy)
            dmas("y", "yz_" + w, [(b, a) for a, b in placed(T["ZN" + w], T.yz, w)], [("ZN" + w, 0, 128)], [])
            return
        dmas("y", "rep%d" % n, [(T[zk][:, c:c + 128], T[zk][:, ZH:ZH + 128]) for c in range(ZH + 128, W0 + 128, 128)],
             [(zk, ZH, ZH + 128), ("sent", n, n + 1)], [(zk, ZH + 128, W0 + 128)])
        act(("fl", 0, 8), ("keep", 120, 128), AF.Copy, accum=("acc", n % 2, n % 2 + 1))
        if n % 2:
            mm(("pE", 296, 297), *[("QF", ("acc", k, k + 1)) for k in range(3)])
            cp(("ri", 0, 1), ("pE", 296, 297))
            tt(("tau", 0, 1), ("pE", 296, 297), ("ri", 0, 1), A.subtract)
            act(("Tt", 0, 64), ("ON", 0, 64), AF.Identity, -4.0, ("tau", 0, 1))
            act(("Tt", 64, 128), ("ON", 0, 64), AF.Identity, 4.0, ("tau", 0, 1))
        vmod(w)

    def arrival(n):
        w, lc = str(n % 2), "L%d" % n
        d, dall = T["D" + w], ("D" + w, 0, 2048)
        ts(("cu", 0, 8), (lc, 0, 8), ("cb", 0, 1), A.add)
        mm(("pE", 0, 8), ("I11", (lc, 0, 8)), ("I14", (lc, 8, 16)), ("ID", ("CE", 0, 8)))
        tt(("E" + w, 0, 128), ("pE", 0, 128), ("kd" + w, 0, 128), A.add)
        tt(("su", 0, 128), (dall, ("cu", 0, 8)), (lc, ZH, PAY), A.add)
        ts(("sh", 0, 128), ("su", 0, 128), 0.5, A.mult, -0.25, A.add)
        cp((dall, ("cu", 0, 8)), ("sh", 0, 128))
        if n // 2 < RO - 1:
            dmas("y", "xc%d" % n, [(d[64:128, 0:1024], d[0:64, 0:1024]), (d[0:64, 1024:2048], d[64:128, 1024:2048])], [dall], [dall], XC)
            lists(w)
            return
        r = slice(64 * int(w), 64 * int(w) + 64)
        dmas("y", "yd_" + w, [(T.yd[r, 2048 - ROT:3072 - ROT], d[0:64, 0:1024]), (T.yd[r, 0:2048 - ROT], d[64:128, ROT:2048]),
                              (T.yd[r, 3072 - ROT:2048], d[64:128, 1024:ROT])], [dall], [], XC)
        act(("X", 0, 256), (("E" + w, 0, 128), ("l3", 0, 16)), AF.Copy)
        turn(("XT", 0, 256), ("X", 0, 256))
        act(("YL" + w, 0, 128), (("XT", 0, 256), ("l4", 0, 8)), AF.Identity, -float(ROT), 1.0 / 2048)
        dmas("s", "ye_" + w, [(b, a) for a, b in placed(T["YL" + w], T.ye, w)], [("YL" + w, 0, 128)], [])

    stage = [-1] * len(calls)
    for n in range(STEPS):
        for f, late in zip((main, choice, send, travel, arrival), LATE):
            f(n)
            stage += [n + late] * (len(calls) - len(stage))

    known = {k: {} for k in eng}
    snap, acc, total = {}, {}, {}

    def wait(q, tok):
        s, n = tok
        if known[q].get(s, 0) >= n:
            return
        eng[q].wait_ge(T.sem[s], n)
        for a, b in snap.get(tok, {}).items():
            if known[q].get(a, 0) < b:
                known[q][a] = b
        known[q][s] = n

    for q, reads, writes, busy, done, issue in (c[:6] for c in in_order(calls, stage)):
        if q == "net":
            acc[writes[0][0]] = [(0, PAY, True, issue(total), q)]
            continue
        need = {}
        for regs, wr in ((reads, False), (writes, True)):
            for b, lo, hi in regs:
                for l2, h2, w2, tok, q2 in acc.get(b, []):
                    hit = (wr or w2) and lo < h2 and l2 < hi
                    if b in PSUM:
                        hit = q2 != q or (q != "p" and hit)
                    if hit and need.get(tok[0], 0) < tok[1]:
                        need[tok[0]] = tok[1]
        for s in sorted(need):
            wait(q, (s, need[s]))
        tok = issue(total)
        snap[tok] = dict(known[q])
        for b, lo, hi in writes:
            acc[b] = [r for r in acc.get(b, []) if not (lo <= r[0] and r[1] <= hi and b not in PSUM)] + [(lo, hi, True, tok, q)]
        for b, lo, hi in reads:
            acc[b] = [r for r in acc.get(b, []) if not (r[4] == q and not r[2] and lo <= r[0] and r[1] <= hi and r[3][0] == tok[0])]
            acc[b].append((lo, hi, False, tok, q))
        for b, lo, hi in list(reads) + list(writes):
            if b in PSUM:
                acc[b] = list({(r[4], r[2], r[0], r[1]): r for r in acc[b]}.values())

    for s in sorted(total):
        wait("g", (s, total[s]))
